import numpy as np, ml_dtypes
CORES = [40,64,80,88,96,104,120,144]
N = 8
BF = ml_dtypes.bfloat16
def gentries(a):
    return np.ascontiguousarray(a.reshape(8, 16, -1).transpose(0, 2, 1)).reshape(8, -1)
def gtable(e):
    e = np.asarray(e); return np.ascontiguousarray(e.reshape(8, -1, 16).transpose(0, 2, 1)).reshape(128, -1).astype(np.int32)
V, L, TV, LV, H = 1024, 256, 2, 2, 3
W = V + TV * LV * L
def parts(rng):
    x = rng.integers(0, 64, (N, 8, 16, V)); ch = rng.integers(0, V, (N, 8, 16, V)); b, a, c = rng.integers(0, V, (3, N, 8, L))
    y = rng.integers(0, 64, (N, 8, 16, L)); th = rng.integers(285, 361, (N, 8, 1)) + rng.integers(-40, 41, (N, 8, 16))
    return x, ch, b, a, c, y, th
def pack(x, ch, b, a, c, y, th):
    return {"x": x.reshape(N, 128, V).astype(np.float32).astype(BF), "ch": np.ascontiguousarray(ch.reshape(N, 128, V)).astype(np.int32), "sb": np.stack([gtable(e) for e in b]),
            "ia": np.stack([gtable(e) for e in a]), "ic": np.stack([gtable(e) for e in c]), "y": y.reshape(N, 128, L).astype(np.float32).astype(BF), "th": np.ascontiguousarray(th.reshape(N, 128, 1)).astype(np.int32)}
def setup_inputs(rng):
    x, ch, b, a, c, y, th = parts(rng); m = rng.random((N, 8, L))
    c = np.where(m < 0.06, a, np.where(m < 0.12, b, c))
    return pack(x, ch, b, a, c, y, th)
def setup_inputs_spread(rng):
    x, ch, b, a, c, y, th = parts(rng)
    x = np.floor(np.exp2(6 * rng.random((N, 8, 1, V))) * rng.random((N, 8, 16, V))).astype(np.int64)
    y = np.floor(np.exp2(6 * rng.random((N, 8, 1, L))) * rng.random((N, 8, 16, L))).astype(np.int64)
    e = rng.integers(1, 4, (N, 8, 1, 1))
    ch = np.minimum(np.floor(V * rng.random((N, 8, 16, V)) ** e).astype(np.int64), V - 1)
    b, a, c = [np.minimum(np.floor(V * rng.random((N, 8, L)) ** e[:, :, 0]).astype(np.int64), V - 1) for i in range(3)]
    th = np.minimum(np.exp2(9 * rng.random((N, 8, 16))).astype(np.int64) - 1, 511)
    return pack(x, ch, b, a, c, y, th)
def setup_inputs_ends(rng):
    x, ch, b, a, c, y, th = parts(rng)
    x = np.where(rng.random((N, 8, 1, V)) < 0.5, 63 * rng.integers(0, 2, (N, 8, 1, V)), 63 * rng.integers(0, 2, x.shape))
    s = rng.integers(0, 2, (N, 8, 1)); s[:, 6:] = 1
    x[..., 0] = 63 * (1 - s); x[..., V - 1] = 63 * s; x[..., V - 2] = 63 * (np.arange(16) % 2)
    y = 63 * rng.integers(0, 2, y.shape); th = 511 * rng.integers(0, 2, th.shape)
    u = rng.random(ch.shape); ch = np.where(u < 0.75, (V - 1) * rng.integers(0, 2, ch.shape), np.where(u < 0.85, V - 2, ch))
    o = []
    for e in (b, a, c):
        u = rng.random(e.shape); o.append(np.where(u < 0.7, (V - 1) * rng.integers(0, 2, e.shape), np.where(u < 0.8, V - 2, e)))
    b, a, c = o
    for k in (3, 14, 15):
        ch[:, 7, k, V - 1] = V - 1; ch[:, 7, k, 0] = 0; ch[:, 7, k, V - 2] = V - 2; th[:, 7, k] = 0
    x[:, 7, :, V - 3] = 0; x[:, 7, 15, V - 3] = 1
    ch[:, 7, 0, V - 1] = V - 1; ch[:, 7, 0, 0] = V - 3; ch[:, 7, 0, V - 2] = V - 2; th[:, 7, 0] = 0
    ch[:, 6, :15, V - 2] = ch[:, 6, :15, 0]
    ch[:, 6, 15, V - 1] = V - 1; ch[:, 6, 15, 0] = 0; ch[:, 6, 15, V - 2] = V - 2; th[:, 6, 15] = 0
    for i in (0, 2, L - 1):
        a[:, 6:, i] = V - 1; b[:, 6:, i] = 0; c[:, 6:, i] = V - 2
    return pack(x, ch, b, a, c, y, th)
def setup_inputs_crowd(rng):
    x, ch, b, a, c, y, th = parts(rng)
    for q in range(N):
        for g in range(8):
            o = rng.permutation(V); mode = (q + g) % 4
            if mode == 3:
                b[q, g], a[q, g], c[q, g] = o[rng.integers(0, 3, (3, L))]; ch[q, g][:, o[:3]] = o[rng.integers(3, 7, (16, 3))]
                continue
            a[q, g] = o[0]; b[q, g] = o[1]; c[q, g] = o[2]
            ch[q, g, :, o[0]] = o[3]; ch[q, g, :, o[1]] = o[4]; ch[q, g, :, o[2]] = o[5]
            x[q, g, :, o[3]] = 63; x[q, g, :, o[4]] = 0; x[q, g, :, o[5]] = 63 * (np.arange(16) % 2)
            j = int(rng.choice(np.array([0, L - 1, L // 2])))
            if mode < 2: th[q, g] = rng.integers(100, 251, 16)
            if mode == 1: c[q, g, j] = o[1]
            if mode == 2:
                th[q, g] = rng.integers(420, 501, 16); ch[q, g, :7, o[2]] = o[4]
                ch[q, g, :, o[6]] = o[5]; ch[q, g, :8, o[6]] = o[4]
                n = int(rng.choice(np.array([1, L // 2, L - 1]))); c[q, g, rng.permutation(L)[:n]] = o[6]
                ch[q, g, :, o[7]] = o[8]; x[q, g, :, o[8]] = 0; b[q, g, j] = o[7]
    return pack(x, ch, b, a, c, y, th)
def setup_inputs_brink(rng):
    x, ch, b, a, c, y, th = parts(rng); h = V // 3; k = h // 2
    for q in range(N):
        for g in range(8):
            o = rng.permutation(V); ca, cb, cc = o[:h], o[h:2 * h], o[2 * h:]
            m = int(rng.integers(5, 15)); th[q, g] = 16 * m
            x[q, g][:, cc] = 31
            sg = np.where(np.argsort(rng.random((16, h)), axis=0) < rng.choice(np.array([7, 8, 9, 10]), h), 1, -1)
            for cls, sign in ((ca, sg), (cb, np.ones((16, h), np.int64))):
                big = np.full((16, h), m); ex = np.where(np.arange(h) < k, 1, rng.integers(-1, 1, h)); big[rng.integers(0, 16, h), np.arange(h)] += ex
                x[q, g][:, cls] = 31 + sign * big
            for cls, cnt in ((ca, (0, 1, 8, 9, 15, 16)), (cb, (16, 16, 16, 8, 9, 15))):
                on = np.argsort(rng.random((16, h)), axis=0) < rng.choice(np.array(cnt), h)
                ch[q, g][:, cls] = np.where(on, cls[rng.integers(0, k, (16, h))], cls[rng.integers(k, h, (16, h))])
            ch[q, g][:, cc] = cc[rng.integers(0, len(cc), (16, len(cc)))]
            a[q, g] = ca[rng.integers(0, h, L)]; b[q, g] = cb[rng.integers(0, h, L)]; c[q, g] = cc[rng.integers(0, len(cc), L)]
            y[q, g] = np.where(rng.random((16, L)) < 0.8, 31 + m, y[q, g])
    return pack(x, ch, b, a, c, y, th)
def setup_inputs_corners(rng):
    x, ch, b, a, c, y, th = parts(rng)
    kind = rng.integers(0, 4, (N, 8, 1, V)); v = np.arange(V)
    ch = np.where(kind == 0, v, np.where(kind == 1, (V - 1) * rng.integers(0, 2, ch.shape), np.where((kind == 3) & (rng.random(ch.shape) < 0.5), v, ch)))
    b = np.where(rng.random(b.shape) < 0.2, (V - 1) * rng.integers(0, 2, b.shape), b)
    a = np.where(rng.random(a.shape) < 0.2, (V - 1) * rng.integers(0, 2, a.shape), a)
    m = rng.integers(0, 7, (N, 8, L)); a = np.where(m < 2, b, a); c = np.where((m == 0) | (m == 2), b, np.where(m == 3, a, c))
    th[:, 0] = 0; th[:, 1] = 511; th[:, 2] = 511 * rng.integers(0, 2, (N, 16))
    x[:, 3] = rng.integers(0, 64, (N, 1, 1)); x[:, 4] = 63 * rng.integers(0, 2, (N, 16, V))
    y = np.where(rng.random((N, 8, 1, L)) < 0.3, 63 * rng.integers(0, 2, (N, 8, 1, L)), y)
    return pack(x, ch, b, a, c, y, th)
def check_inputs(d):
    bad = []
    for k, lo, hi in (("x", 0, 63), ("ch", 0, V - 1), ("sb", 0, V - 1), ("ia", 0, V - 1), ("ic", 0, V - 1), ("y", 0, 63), ("th", 0, 511)):
        v = np.asarray(d[k]).astype(np.float64)
        if not (np.min(v) >= lo and np.max(v) <= hi): bad.append("range of " + k)
        elif np.any(v != np.floor(v)): bad.append("whole numbers of " + k)
    return bad
def pick(s, ix):
    return np.array([[np.take(s[q, g], ix[q, g], axis=1) for g in range(8)] for q in range(N)])
def kids(s, ch):
    return pick(s, ch.reshape(N, 8, 16 * L)).reshape(N, 8, 16, 16, L)
def reference(x, ch, sb, ia, ic, y, th):
    X = np.zeros((N, 8, 16, W), np.int32); C = np.zeros((N, 8, 16, W), np.int32)
    X[..., :V] = x.astype(np.float32).astype(np.int32).reshape(N, 8, 16, V); C[..., :V] = ch.reshape(N, 8, 16, V)
    b, a, c = [np.stack([gentries(e) for e in z]).astype(np.int32) for z in (sb, ia, ic)]
    Y = y.astype(np.float32).astype(np.int32).reshape(N, 8, 16, L); t0 = th.astype(np.int32).reshape(N, 8, 16, 1)
    lane = np.arange(L, dtype=np.int32); slot = np.arange(16)[:, None]; A = np.zeros((N, 8, 1, 1), np.int32)
    for t in range(TV):
        pa, pb, pc = a, b, c; off = np.zeros((N, 8, L), bool)
        for lev in range(LV):
            n = V + (t * LV + lev) * L
            ka, kb, kc = pick(C, pa), pick(C, pb), pick(C, pc)
            xa, xb, xc = kids(X, ka), kids(X, kb), kids(X, kc)
            al = np.add.reduce(np.abs(xa - xc), axis=2) > t0 + A; be = np.add.reduce(np.abs(xb - xc), axis=2) > t0 + A
            dist = np.add.reduce(np.abs(xa - xb), axis=2); vote = np.add.reduce((xa >= xb).astype(np.int32), axis=2) >= 9
            col = al & be
            M = np.where(al & (~be | vote), ka, kb)
            ks = np.argmax(np.where(col | ~np.any(col, axis=2, keepdims=True), dist, -1), axis=2)[:, :, None]
            off = off | (np.add.reduce(col.astype(np.int32), axis=2) >= 9)
            if lev < LV - 1: M = np.where(slot == ks, n + L + lane, M)
            na, nb, nc = [np.take_along_axis(z, ks, 2)[:, :, 0] for z in (ka, kb, kc)]
            new = np.clip(pick(X, pa) + pick(X, pb) - pick(X, pc), 0, 63)
            half = (pick(X, nb) + Y) >> 1
            first = np.argmax(nb[:, :, :, None] == nb[:, :, None, :], axis=3) == lane
            for q in range(N):
                for g in range(8):
                    w = first[q, g]; X[q, g][:, nb[q, g][w]] = half[q, g][:, w]
            X[..., n:n + L] = new; C[..., n:n + L] = M
            pa, pb, pc = na, nb, nc
        n0 = V + t * LV * L; x0 = X[..., n0:n0 + L]
        Y = np.where(off[:, :, None], np.abs(Y - x0), x0)
        c = b; a = np.where(off, a, n0 + lane); b = np.where(off, b, n0 + lane)
        A = np.add.reduce(off.astype(np.int32), axis=2).reshape(N, 8, 1, 1)
        if t < TV - 1: a, c, Y = np.roll(a, H, axis=0), np.roll(c, H, axis=0), np.roll(Y, H, axis=0)
    return {"xo": X.reshape(N, 128, W).astype(np.float32).astype(BF), "co": np.ascontiguousarray(C[..., V:]).reshape(N, 128, W - V).astype(np.float32),
            "so": np.stack([gtable(e) for e in b]).astype(np.float32), "yo": Y.reshape(N, 128, L).astype(np.float32).astype(BF)}

@@ -1,0 +1,590 @@
+import numpy as np
+from concourse.mybir import dt, AluOpType, AxisListType, ActivationFunctionType
+
+ALU = AluOpType
+ACT = ActivationFunctionType
+V, L, TV, LV, H = 1024, 256, 2, 2, 3
+W_, WC = 128, 8
+TR = 16
+CHUNKS = [32, 32, 32, 32]
+EMODE = [[0, 1, 0, 1], [0, 1, 0, 1]]
+RED = [(0, 64), (64, 128)]
+ADDON = False
+LEAD = 12000.0
+TRIES, SEED = 1200, 0
+BIG = 16384.0
+THETA = 8.5 * BIG
+
+B, F, I32, U, K = "bfloat16", "float32", "int32", "uint16", "float16"
+PER_STREAM = {
+    "X": (TR + 2048, B), "C": (1536, I32), "CO": (1024, F), "y": (128, B), "sa": (16, U), "ra": (8, U),
+    "ry": (128, B), "yn": (128, B), "ym": (128, B), "lst": (48, U), "k16": (384, U), "kf": (384, K),
+    "xb": (2048, B), "xc": (2048, B), "dab": (2048, B), "dcb": (2048, B), "rab": (2048, B), "acb": (2048, B), "aac": (2048, B),
+    "pqr": (384, B), "albe": (256, K), "prod": (640, K), "keyt": (128, F), "scn": (128, F), "oht": (128, K), "oh": (128, K),
+    "zc": (8, F), "zx": (128, F), "ne": (128, B), "nd": (128, B), "zt": (8, K), "idx": (32, U), "xz": (128, B), "hh": (256, B),
+    "rnd": (128, I32), "nvc": (128, K), "w12": (256, K), "sm": (128, F), "off0": (128, B), "yw": (672, B), "thr": (4, F),
+}
+SHARED = {
+    "l32": (56, I32), "la": (48, U), "ab": (32, F), "rc": (16, U),
+    "ones": (128, B), "idb": (128, B), "nidb": (128, B), "bo0": (128, B), "bob": (128, B), "idk": (128, K), "idp": (128, K), "idn": (128, K),
+    "id4k": (128, B), "bok": (128, K), "db": (256, B), "ndb": (256, B), "dk": (256, K), "dk128": (256, K), "dk4k": (256, K),
+    "wb": (144, B), "wn": (144, B), "wk": (144, K), "pi": (4, I32), "pc": (8, F), "tb": (128, B), "seg": (128, F), "rst": (128, B),
+    "tri": (128, B), "tri0": (128, F), "ci": (32, I32), "cu": (32, U), "jc": (48, B), "jf": (128, F), "nid": (512, F), "nl": (64, F), "m192": (16, B),
+}
+SCRATCH = {n: ("sbuf", [128, c], d) for n, (c, d) in SHARED.items()}
+for s_ in range(2):
+    SCRATCH.update({"%s_%d" % (n, s_): ("sbuf", [128, c], d) for n, (c, d) in PER_STREAM.items()})
+    SCRATCH.update({"%s_%d" % (n, s_): ("psum", [128, 512], F) for n in ("pa", "pk", "pr0", "pr1")})
+NDMA = 60
+MSG = (("rc", "arc"), ("ra_0", "ara0"), ("ry_0", "ary0"), ("ra_1", "ara1"), ("ry_1", "ary1"))
+SEMAPHORES = ["dve", "act", "pe", "pool", "sent"] + [m_[1] for m_ in MSG] + ["d%d" % i for i in range(NDMA)]
+G_, SC_, PE_, TT_ = 1.56, 3.8, 0.5, 2.0
+HOP, SAME = 100.0, 70.0
+
+
+def way(T, topo, r):
+    src, dst = T.cores[r], T.cores[(r + H) % len(T.cores)]
+    if topo.may_write(src, dst):
+        return [src, dst]
+    can = [c for c in topo.cores_of(src) if c not in T.cores and topo.may_write(src, c) and topo.may_write(c, dst)]
+    near = [c for c in can if topo.die(c) == topo.die(src)]
+    return [src, (near or can)[0], dst]
+
+
+def emask(topo, a, b):
+    e = topo.engines(a, b)[:8]
+    return sum(1 << k for k in e), len(e)
+
+
+def wide(a):
+    return SCRATCH[a["name"]][2] in (F, I32)
+
+
+def build(g, T, topo, rank):
+    ops = []
+    last = {}
+    bank = {}
+    ndma = [0]
+    now = [None]
+
+    def A(name, a=None, b=None, s=None, h=None):
+        if name not in SCRATCH:
+            name = "%s_%d" % (name, now[0])
+        n = SCRATCH[name][1][1]
+        a0, b0, s0 = a or 0, n if b is None else b, s or 1
+        cols = range(a0, b0, s0)
+        bits = ((1 << (b0 - a0)) - 1) << a0 if s0 == 1 else sum(1 << c for c in cols)
+        bits = bits | bits << n if h is None else bits << (n * h)
+        p0, p1 = (0, 128) if h is None else (64 * h, 64 * h + 64)
+        ap = T[name][p0:p1, a0:b0] if s0 == 1 else T[name][p0:p1, a0:b0:s0]
+        return {"name": name, "ap": ap, "n": len(cols), "acc": [(name, bits)], "ind": False}
+
+    def IND(win, off):
+        return {"name": win["name"], "ap": win["ap"].indirect(off["ap"]), "n": 16 * off["n"], "acc": win["acc"], "off": off["acc"], "ind": True}
+
+    def op(eng, fn, reads, writes, busy, lat=0.0, sem=None):
+        i = len(ops)
+        deps = {}
+
+        def dep(j):
+            same = eng == "pe" and ops[j]["eng"] == "pe"
+            if deps.get(j) != "w":
+                deps[j] = "o" if same else "w"
+        acc = []
+        for a in reads:
+            if isinstance(a, dict):
+                acc += [(x, False) for x in a["acc"] + a.get("off", [])]
+        for a in writes:
+            acc += [(x, True) for x in a["acc"]] + [(x, False) for x in a.get("off", [])]
+        for (name, bits), w in acc:
+            keep = []
+            for (j, bj, wj) in last.get(name, []):
+                if j != i and bj & bits and (w or wj):
+                    dep(j)
+                if w and not (bj & ~bits) and j != i:
+                    continue
+                keep.append((j, bj, wj))
+            keep.append((i, bits, w))
+            last[name] = keep
+            if SCRATCH[name][0] == "psum":
+                st = bank.setdefault(name, [eng, [], [], None])
+                if st[0] != eng:
+                    st[0], st[1], st[2] = eng, [], st[1]
+                for j in st[2]:
+                    dep(j)
+                if i not in st[1]:
+                    st[1].append(i)
+                if eng == "pe":
+                    if st[3] is not None and st[3] != i:
+                        dep(st[3])
+                    st[3] = i
+        ops.append({"eng": eng, "fn": fn, "deps": deps, "busy": busy, "lat": lat, "sem": sem, "s": now[0]})
+        return i
+
+    def vcost(out, ins, two=False):
+        n = out["n"]
+        if out["ind"]:
+            return 50 + n * SC_
+        if ins[0]["ind"]:
+            return 50 + n * G_
+        if two:
+            ps = any(SCRATCH[a["name"]][0] == "psum" for a in ins)
+            return 30 + max(64, n * (1 if ps else TT_))
+        return 30 + max(64, n * (1 if any(wide(a) for a in [out] + ins) else 0.5))
+
+    def sc(x):
+        return x["ap"] if isinstance(x, dict) else x
+
+    def cp(out, in_):
+        return op("dve", lambda: g.vector.tensor_copy(out["ap"], in_["ap"]), [in_], [out], vcost(out, [in_]))
+
+    def tt(out, a, b, o):
+        return op("dve", lambda: g.vector.tensor_tensor(out["ap"], a["ap"], b["ap"], o), [a, b], [out], vcost(out, [a, b], True))
+
+    def ts(out, a, s1, o0, s2=None, o1=None):
+        if o1 is None:
+            fn = lambda: g.vector.tensor_scalar(out["ap"], a["ap"], sc(s1), None, o0)
+        else:
+            fn = lambda: g.vector.tensor_scalar(out["ap"], a["ap"], sc(s1), sc(s2), o0, o1)
+        return op("dve", fn, [a, s1, s2], [out], vcost(out, [a]))
+
+    def tr(out, a):
+        return op("dve", lambda: g.vector.transpose(out["ap"], a["ap"]), [a], [out], vcost(out, [a]))
+
+    def scan(out, d0, d1, o0, o1):
+        return op("dve", lambda: g.vector.tensor_tensor_scan(out["ap"], d0["ap"], d1["ap"], 0.0, o0, o1), [d0, d1], [out], vcost(out, [d0, d1]))
+
+    def ms(out, v):
+        return op("dve", lambda: g.vector.memset(out["ap"], v), [], [out], 30 + max(64, out["n"] * 0.5))
+
+    def act(out, a, f, acc=None, bias=0.0, scale=1.0):
+        if acc is None:
+            fn = lambda: g.scalar.activation(out["ap"], a["ap"], f, sc(bias), scale)
+        else:
+            fn = lambda: g.scalar.activation(out["ap"], a["ap"], f, accum_out=acc["ap"])
+        return op("act", fn, [a, bias], [out] + ([acc] if acc else []), 65 + max(64, out["n"] * (G_ if a["ind"] else 1)))
+
+    def mm(*groups, start=True, stop=True):
+        out = groups[0][0]
+
+        def fn():
+            r = out
+            for o, terms in groups:
+                for q, (w, x) in enumerate(terms):
+                    r = g.tensor.matmul(o["ap"], w["ap"], x["ap"], start and q == 0, stop and q == len(terms) - 1)
+            return r
+        return op("pe", fn, [a for o, terms in groups for t_ in terms for a in t_], [o for o, terms in groups],
+                  sum(12 + PE_ * max(64, x["n"]) for o, terms in groups for w, x in terms))
+
+    def both(name, a, n, terms):
+        return mm(*[(A(name, a + h * n, a + (h + 1) * n), [(A(w, 128 * h, 128 * h + 128), A(*x)) for w, x in terms]) for h in range(2)])
+
+    def iota(out, pat, base, cm):
+        if SCRATCH[out["name"]][2] == I32:
+            fn = lambda: g.iota(out["ap"], pat, base, cm)
+        else:
+            fn = lambda: g.iota(out["ap"], pat, base, cm, allow_small_or_imprecise_dtypes=True)
+        return op("pool", fn, [], [out], 130 + 2 * out["n"])
+
+    def asel(out, a, pat, cmp_, fill, base, cm):
+        return op("pool", lambda: g.affine_select(out["ap"], a["ap"], pat, cmp_, fill, base, cm), [a], [out], 170 + 2 * out["n"])
+
+    def dma(q, out, in_, nbytes):
+        s = "d%d" % ndma[0]
+        ndma[0] += 1
+        h = g.sync if q == "sp" else g.scalar
+        rd = [in_] if isinstance(in_, dict) else []
+        wr = [out] if isinstance(out, dict) else []
+        return op(q, lambda: h.dma_start(sc(out), sc(in_)), rd, wr, 70, 1800 + nbytes / 150.0, (s, 16))
+
+    path = way(T, topo, rank)
+    rid, pid = topo.addr(path[1], path[0])
+    mk, ne_ = emask(topo, path[0], path[1])
+    back = way(T, topo, (rank - H) % len(T.cores))
+    na_ = emask(topo, back[-2], back[-1])[1]
+    sends = []
+
+    def send(src):
+        land, sem = MSG[len(sends)]
+        fn = lambda: g.remote_dma(T[land][:], src["ap"], T.sem[sem], T.sem.sent, pid, rid, mk)
+        i = op("pool", fn, [src], [], 500, 0.0, ("sent", None))
+        if sends:
+            ops[i]["deps"].setdefault(sends[-1], "o")
+        sends.append(i)
+        j = op("net", None, [], [A(land)], 0, 5000.0, (sem, na_))
+        ops[j]["deps"][i] = "t"
+
+    for s in range(2):
+        now[0] = s
+        rows = slice(64 * s, 64 * s + 64)
+        for h in range(2):
+            q = ("sp", "act")[h]
+            for j, x in ((1, T.sb), (2, T.ic), (0, T.ia)):
+                dma(q, A("l32", 16 * j + WC * s, 16 * j + WC * s + WC, h=h), x[rows, WC * h:WC * h + WC], 2048)
+            dma(q, A("C", 0, V, h=h), T.ch[rows, :], 524288 + 786432 * s)
+            dma(q, A("X", TR, TR + V, h=h), T.x[rows, :], 786432 * (s + 1))
+    for s in range(2):
+        now[0] = s
+        rows = slice(64 * s, 64 * s + 64)
+        for h in range(2):
+            dma("sp", A("l32", 48 + 4 * s, 49 + 4 * s, h=h), T.th[rows, :], 786432 * 2)
+            dma("sp", A("y", h=h), T.y[rows, W_ * h:W_ * h + W_], 786432 * 2)
+        ms(A("X", 0, TR), 0.0)
+    for q in ("sp", "act"):
+        mine = [i for i, o in enumerate(ops) if o["eng"] == q]
+        for i, j in zip(mine, mine[1:]):
+            ops[j]["deps"][i] = "o"
+    now[0] = None
+    ms(A("ones"), 1.0)
+    ms(A("m192"), -192.0)
+    asel(A("idb"), A("ones"), [[-1, 128]], ALU.is_equal, 0.0, 0, 1)
+    asel(A("bo0"), A("ones"), [[-16, 8], [0, 16]], ALU.is_ge, 0.0, 0, 1)
+    asel(A("bob"), A("bo0"), [[16, 8], [0, 16]], ALU.is_ge, 0.0, 15, -1)
+    for h in range(2):
+        ms(A("db", 128 * h, 128 * h + 128, h=1 - h), 0.0)
+        for q in range(2):
+            cp(A("db", 128 * h + 64 * q, 128 * h + 64 * q + 64, h=h), A("idb", 64 * h, 64 * h + 64, h=h))
+    iota(A("pi", 0, 1), [[0, 1]], 0, 1)
+    ts(A("pi", 1, 2), A("pi", 0, 1), 15, ALU.bitwise_and)
+    ts(A("pi", 2, 3), A("pi", 0, 1), 64, ALU.bitwise_and)
+    cp(A("pc", 0, 2), A("pi", 1, 3))
+    ts(A("pc", 2, 3), A("pc", 0, 1), -1.0, ALU.mult, 15.0, ALU.add)
+    ts(A("pc", 3, 4), A("pc", 0, 1), -1.0, ALU.mult, 16.0, ALU.add)
+    ts(A("pc", 4, 5), A("pc", 1, 2), 2.0, ALU.mult, A("pc", 0, 1), ALU.add)
+    ts(A("pc", 5, 6), A("pc", 0, 1), 16.0, ALU.mult)
+    R_, R15, R16, HR, RX16 = A("pc", 0, 1), A("pc", 2, 3), A("pc", 3, 4), A("pc", 4, 5), A("pc", 5, 6)
+    for name, w in (("nidb", -1.0), ("idk", 1.0), ("idp", 1.0 / 128), ("idn", -1.0 / 128), ("id4k", 4096.0)):
+        ts(A(name), A("idb"), w, ALU.mult)
+    for name, w in (("ndb", -1.0), ("dk", 1.0), ("dk128", -128.0), ("dk4k", 4096.0)):
+        ts(A(name), A("db"), w, ALU.mult)
+    cp(A("bok"), A("bob"))
+    for name, w in (("wb", 1.0), ("wn", -16.0), ("wk", 1.0)):
+        ms(A(name), 0.0)
+        ts(A(name, 15, 143, 16), A("bob", 0, 128, 16), w, ALU.mult)
+
+    def W(name, k):
+        return A(name, 15 - k, 143 - k)
+    ts(A("tb"), A("ones"), R15, ALU.mult)
+    ms(A("seg"), 1.0)
+    ms(A("seg", 0, 128, 16), 0.0)
+    ts(A("rst"), A("seg"), -1.0, ALU.mult, 1.0, ALU.add)
+    iota(A("tri0"), [[0, 8], [1, 16]], 0, 0)
+    ts(A("jf"), A("tri0"), R_, ALU.is_ge, 4096.0, ALU.mult)
+    ts(A("tri"), A("jf"), R16, ALU.max)
+    iota(A("ci", 0, 16), [[1, 16]], 0, 0)
+    iota(A("ci", 16, 32), [[16, 16]], 15, 0)
+    cp(A("cu"), A("ci"))
+    ms(A("jc", WC, 48), 0.0)
+    ts(A("jc", 0, WC), A("ci", 0, WC), 256.0, ALU.mult, RX16, ALU.add)
+    iota(A("nid"), [[512, 2], [1, 256]], V + L, 0)
+    iota(A("nl", 32, 64), [[512, 2], [0, 2], [16, WC]], V, 0)
+    ts(A("nl", 0, 32), A("nl", 32, 64), HR, ALU.add)
+    for s in range(2):
+        now[0] = s
+        for j in (1, 2, 0):
+            o = 16 * j + WC * s
+            cp(A("la", o, o + WC), A("l32", o, o + WC))
+            if j < 2:
+                cp(A("ab", 16 * s + WC * j, 16 * s + WC * j + WC), A("l32", o, o + WC))
+        cp(A("yw", 640, 656), A("jc", 0, 16))
+        cp(A("thr", 0, 1), A("l32", 48 + 4 * s, 49 + 4 * s))
+    now[0] = None
+    send(A("la", 16, 32))
+
+    SL = {"a": 0, "c": 1, "b": 2}
+    w = W_
+    for s in range(2):
+        now[0] = s
+        ring = [0]
+        PP, EE, X0, WY, OFF = [A("yw", w * q, w * q + w) for q in range(5)]
+        for t in range(TV):
+            xw = A("X", TR, TR + V + 512 * t)
+            sw = A("X", 0, TR + V + 512 * t)
+            yv = "y" if t == 0 else "ry"
+            n0 = TR + V + 512 * t
+            old = A("ab", 16 * s, 16 * s + 16) if t == 0 else A("sm", 40, 48)
+            for lev in range(LV):
+                fin = lev == LV - 1
+                n = n0 + lev * L
+                m = t * LV + lev
+                cw = A("C", 0, V + (0 if t == 0 else 256 * (lev + 1)))
+
+                def cur(x):
+                    if t == 0:
+                        o = {"a": 0, "b": 16, "c": 32}[x] + WC * s
+                        return A("la", o, o + WC)
+                    return {"a": A("ra"), "b": A("sa", WC, 2 * WC), "c": A("rc", WC * s, WC * s + WC)}[x]
+
+                def kk(name, x, a=0, b=w):
+                    return A(name, SL[x] * w + a, SL[x] * w + b)
+                if lev > 0:
+                    cp(A("k16"), IND(cw, A("lst", WC, 4 * WC)))
+                    act(A("pqr"), IND(xw, A("lst", WC, 4 * WC)), ACT.Copy)
+                else:
+                    for x in "bca":
+                        cp(kk("k16", x), IND(cw, cur(x)))
+                    for x in "bca":
+                        act(kk("pqr", x), IND(xw, cur(x)), ACT.Copy)
+                cp(A("kf"), A("k16"))
+                q0 = 2 * w if fin else 0
+                mm((A("pk", q0, 3 * w), [(A("idk"), A("kf", q0, 3 * w))]),
+                   (A("pk", 3 * w, 4 * w), [(A("idp"), kk("kf", "a")), (A("idn"), kk("kf", "b"))]))
+                both("pr0", 0, w, [("db", ("pqr", 0, w)), ("db", ("pqr", 2 * w, 3 * w)), ("ndb", ("pqr", w, 2 * w))])
+                ts(A("X", n, n + L), A("pr0", 0, L), 0.0, ALU.max, 63.0, ALU.min)
+                if t == TV - 1 and fin:
+                    dma("sp", T.xo[64 * s:64 * s + 64, 1536:2048], A("X", TR + 1536, TR + 2048, h=0), 65536)
+                s0 = 0
+                for cwid, em in zip(CHUNKS, EMODE[s]):
+                    a, b = 16 * s0, 16 * (s0 + cwid)
+                    ga, gb, gc_ = [IND(xw, kk("k16", x, s0, s0 + cwid)) for x in "abc"]
+                    act(A("xb", a, b), gb, ACT.Copy)
+                    if em:
+                        act(A("xc", a, b), gc_, ACT.Copy)
+                    else:
+                        tt(A("dcb", a, b), gc_, A("xb", a, b), ALU.subtract)
+                        act(A("acb", a, b), A("dcb", a, b), ACT.Abs)
+                    tt(A("dab", a, b), ga, A("xb", a, b), ALU.subtract)
+                    ts(A("rab", a, b), A("dab", a, b), -2.0 ** -11, ALU.max, 32.0, ALU.mult)
+                    us = list(range(a, b, 512))
+                    rbs = []
+                    for u in us:
+                        rbs.append(A("pr%d" % (ring[0] % 2)))
+                        ring[0] += 1
+                    if em:
+                        for u, rb in zip(us, rbs):
+                            mm((rb, [(A("idb"), A("xc", u, u + 512)), (A("nidb"), A("xb", u, u + 512))]), stop=not ADDON)
+                            act(A("acb", u, u + 512), rb, ACT.Abs)
+                    for u, rb in zip(us, rbs):
+                        if em and ADDON:
+                            mm((rb, [(A("nidb"), A("dab", u, u + 512))]), start=False)
+                        elif em:
+                            mm((rb, [(A("idb"), A("xb", u, u + 512)), (A("nidb"), A("xc", u, u + 512)), (A("idb"), A("dab", u, u + 512))]))
+                        else:
+                            mm((rb, [(A("nidb"), A("dcb", u, u + 512)), (A("idb"), A("dab", u, u + 512))]))
+                        act(A("aac", u, u + 512), rb, ACT.Abs)
+                    s0 += cwid
+
+                def red(name, wn, a, b):
+                    return [(W(wn, k), A(name, 16 * a + k, 16 * b, 16)) for k in range(16)]
+                key = A("pa", 2 * w, 3 * w)
+                for a, b in RED:
+                    mm((A("pa", w + a, w + b), red("acb", "wb", a, b)))
+                    mm((A("pa", 2 * w + a, 2 * w + b), [(A("idb"), A("tb", a, b))] + red("dab", "wn", a, b)), stop=False)
+                    mm((A("pa", 2 * w + a, 2 * w + b), red("rab", "wb", a, b)), start=False)
+                    mm((A("pa", a, b), red("aac", "wb", a, b)))
+                slots = "jbx" if fin else "jacbx"
+                ns = len(slots)
+
+                def PR(x):
+                    return A("prod", slots.index(x) * w, (slots.index(x) + 1) * w)
+                ts(A("albe"), A("pa", 0, 2 * w), A("thr", t, t + 1), ALU.is_gt, 128.0, ALU.mult)
+                tt(PR("x"), A("albe", 0, w), A("albe", w, 2 * w), ALU.mult)
+                tt(key, PR("x"), key, ALU.add)
+                tr(A("keyt"), key)
+                scan(A("scn"), A("seg"), A("keyt"), ALU.mult, ALU.max)
+                tt(A("oht"), IND(A("scn"), A("cu", 16, 16 + WC)), A("keyt"), ALU.is_equal)
+                tr(A("oh"), A("oht"))
+                for x in ("b" if fin else "bca"):
+                    tt(PR(x), A("oh"), kk("pk", x), ALU.mult)
+                ts(PR("j"), A("oh"), R_, ALU.mult)
+                mm((A("pr0", 0, ns * WC), [(A("idb"), A("yw", 640, 664) if fin else A("jc", 0, ns * WC))] + [(W("wk", r), A("prod", r, ns * w, 16)) for r in range(16)]),
+                   (A("pr0", w, 2 * w), [(A("idb"), A("tri")), (A("bok"), PR("b"))]))
+                lo, nu = (40, 1) if fin else (0, 4)
+                cp(A("lst", lo, lo + nu * WC), A("pr0", 0, nu * WC))
+                act(A("zc"), A("pr0", (ns - 2) * WC, (ns - 1) * WC), ACT.Identity, bias=R16)
+                act(A("zx"), IND(A("zc"), A("cu", 0, WC)), ACT.Copy)
+                cl = A("pr0", (ns - 1) * WC, ns * WC)
+                if fin:
+                    for q in range(2 if t < TV - 1 else 1):
+                        act(A("sm", WC * q, WC * q + WC), cl, ACT.Relu, bias=THETA / 2, scale=-0.5)
+                else:
+                    act(A("yw", 656, 664), cl, ACT.Relu, bias=-128.0 * BIG, scale=16.0)
+                tt(A("ne"), A("zx"), A("pr0", w, 2 * w), ALU.not_equal)
+                scan(A("nd"), A("rst"), A("ne"), ALU.max, ALU.min)
+                tt(A("zt"), A("nd", 15, w, 16), A("zc"), ALU.mult)
+                act(A("xz"), IND(A("xb"), A("lst", lo, lo + WC)), ACT.Copy)
+                both("pr1", 0, w, [("db", ("xz",)), ("db", (yv,))])
+                act(A("hh"), A("pr1", 0, L), ACT.Identity, bias=191.75, scale=0.5)
+                both("pr0", 2 * w, WC, [("dk", ("zt",))])
+                ts(A("idx", 0, 32, 2), A("pr0", 2 * w, 2 * w + 2 * WC), R_, ALU.add)
+                if fin:
+                    k = old["n"]
+                    tt(A("sm", 16, 16 + k), old, A("sm", 0, k), ALU.add)
+                    tt(A("sm", 32 + 24 * t, 32 + 24 * t + k), A("sm", 16, 16 + k), A("nl", 16 * t, 16 * t + k), ALU.min)
+                    if t < TV - 1:
+                        cp(A("sa"), A("sm", 32, 48))
+                        send(A("sa", 0, WC))
+                for c in range(2 * WC - 1, -1, -1):
+                    tt(IND(sw, A("idx", 2 * c, 2 * c + 1)), A("hh", 16 * c, 16 * c + 16), A("m192"), ALU.add)
+                dk = A("pk", 3 * w, 4 * w)
+                ts(A("rnd"), key, -49.0 / 128, ALU.add, 16200.0, ALU.max)
+                tt(A("nvc"), A("rnd"), key, ALU.is_lt)
+                tt(A("w12", 0, w), A("albe", 0, w), dk, ALU.mult)
+                tt(A("w12", w, 2 * w), A("nvc"), dk, ALU.mult)
+                terms = [("dk", ("kf", 2 * w, 3 * w)), ("dk", ("w12", 0, w)), ("dk128", ("w12", w, 2 * w))]
+                co, m0 = A("CO", m * L, (m + 1) * L), A("pk", 0, L)
+                both("pk", 0, w, terms + ([] if fin else [("dk4k", ("oh",))]))
+                if not fin:
+                    tt(co, A("nid", t * L, t * L + L), m0, ALU.min)
+                    if t < TV - 1:
+                        cp(A("C", V + m * L, V + (m + 1) * L), co)
+                else:
+                    if t < TV - 1:
+                        cp(A("C", V + m * L, V + (m + 1) * L), m0)
+                    act(co, m0, ACT.Copy)
+                for h in range(2):
+                    dma("sp", T.co[64 * s:64 * s + 64, m * L + w * h:m * L + w * h + w], A("CO", m * L + w * h, m * L + w * h + w, h=h), 65536)
+                cnt = A("pa", 3 * w, 4 * w)
+                mm((cnt, [(A("bok"), PR("x"))] + ([(A("id4k"), A("off0"))] if fin else [])))
+                if not fin:
+                    act(A("off0"), cnt, ACT.Relu, bias=-512.0, scale=1.0 / 256)
+                    for h in range(2):
+                        act(A("yw", 2 * w, 3 * w, h=h), A("X", n0 + w * h, n0 + w * h + w, h=h), ACT.Copy)
+                    mm((cnt, [(A("idb"), A(yv)), (A("nidb"), X0)]))
+                    act(PP, cnt, ACT.Abs)
+                    mm((cnt, [(A("idb"), PP), (A("nidb"), X0)]))
+                    act(EE, cnt, ACT.Copy)
+                else:
+                    yn = "yn" if t == 0 else "ym"
+                    ts(OFF, cnt, THETA, ALU.is_ge)
+                    tt(WY, OFF, EE, ALU.mult)
+                    mm((cnt, [(A("idb"), WY), (A("idb"), X0)]))
+                    act(A(yn), cnt, ACT.Copy)
+                    if t < TV - 1:
+                        send(A(yn))
+                        mm((cnt, [(A("db", 0, 128), OFF), (A("db", 128, 256), OFF)]))
+                        act(PP, cnt, ACT.Identity, A("thr", 2, 3))
+                        tt(A("thr", 1, 2), A("thr", 0, 1), A("thr", 2, 3), ALU.add)
+        rows = slice(64 * s, 64 * s + 64)
+        for h in range(2):
+            q = ("sp", "act")[h]
+            dma(q, T.xo[rows, 768 * h:768 * h + 768], A("X", TR + 768 * h, TR + 768 * h + 768, h=h), 196608)
+            dma("sp", T.so[rows, WC * h:WC * h + WC], A("sm", 56, 64, h=h), 2048)
+            dma("sp", T.yo[rows, w * h:w * h + w], A("ym", h=h), 16384)
+    return ops, ne_ * len(sends)
+
+
+def sweep(ops, before, after, prio, look, back):
+    n = len(ops)
+    left = [len(b) for b in before]
+    ready = [ops[i]["lat"] if back else 0.0 for i in range(n)]
+    pool = {o["eng"]: [] for o in ops}
+    for i, o in enumerate(ops):
+        if not left[i]:
+            pool[o["eng"]].append(i)
+    free = {e: 0.0 for e in pool}
+    order, end, start = [], [0.0] * n, [0.0] * n
+    for _ in range(n):
+        best = None
+        for e, lst in pool.items():
+            if lst:
+                t0 = max(free[e], min([ready[i] for i in lst]))
+                if best is None or t0 < best[0]:
+                    best = (t0, e)
+        t0, e = best
+        i = -max([(prio[i], -i) for i in pool[e] if ready[i] <= t0 + look])[1]
+        pool[e].remove(i)
+        start[i] = max(free[e], ready[i])
+        free[e] = start[i] + ops[i]["busy"]
+        end[i] = free[e] + (0.0 if back else ops[i]["lat"])
+        order.append(i)
+        for u, d in after[i]:
+            if ready[u] < free[e] + d:
+                ready[u] = free[e] + d
+            left[u] -= 1
+            if not left[u]:
+                pool[ops[u]["eng"]].append(u)
+    return order, start, end
+
+
+def plan(ops):
+    n = len(ops)
+    fw, bw = [[] for _ in ops], [[] for _ in ops]
+    for i, o in enumerate(ops):
+        for j, k in o["deps"].items():
+            d = 0.0 if k == "o" else ops[j]["lat"] + (0.0 if k == "t" else SAME if o["eng"] == ops[j]["eng"] else HOP)
+            fw[j].append((i, d))
+            bw[i].append((j, d))
+    base = [0.0] * n
+    for i in range(n - 1, -1, -1):
+        base[i] = ops[i]["busy"] + max([base[u] + d for u, d in fw[i]] + [ops[i]["lat"]])
+    rng = np.random.default_rng(SEED)
+    best = r = None
+    for k in range(TRIES):
+        look = float(rng.choice([40.0, 150.0, 300.0]))
+        if k % 8 == 0 and k < TRIES // 2:
+            lead = LEAD * float(rng.uniform(0.5, 2.0))
+            prio = [p + (lead if ops[i]["s"] != 1 else 0.0) for i, p in enumerate(base)]
+        else:
+            src = r if k < TRIES // 2 else best
+            z = rng.uniform(0, float(rng.choice([0.0, 100.0, 400.0])), n)
+            prio = sweep(ops, fw, bw, [src[2][i] + float(z[i]) for i in range(n)], look, True)[2]
+        r = sweep(ops, bw, fw, prio, look, False)
+        if best is None or max(r[2]) <= max(best[2]):
+            best = r
+    return best
+
+
+def emit(g, T, ops, order, nsent):
+    Q = {"dve": g.vector, "act": g.scalar, "pe": g.tensor, "pool": g, "sp": g.sync}
+    need = set(j for o in ops for j, k in o["deps"].items() if k == "w")
+    count = {e: 0 for e in Q}
+    known = {e: {} for e in Q}
+    mark, clock = {}, {}
+    for i in order:
+        o = ops[i]
+        e = o["eng"]
+        if e == "net":
+            mark[i], clock[i] = o["sem"], {o["sem"][0]: o["sem"][1]}
+            continue
+        kn = known[e]
+        want = sorted((j for j, k in o["deps"].items() if k == "w"), key=lambda j: -mark[j][1])
+        for j in want:
+            s, v = mark[j]
+            if kn.get(s, 0) < v:
+                Q[e].wait_ge(T.sem[s], v)
+                for s2, v2 in clock[j].items():
+                    if kn.get(s2, 0) < v2:
+                        kn[s2] = v2
+        ins = o["fn"]()
+        if o["sem"] is None:
+            if i in need:
+                count[e] += 1
+                ins.then_inc(T.sem[e], 1)
+                mark[i] = (e, count[e])
+        elif o["sem"][1] is not None:
+            ins.then_inc(T.sem[o["sem"][0]], 16)
+            mark[i] = o["sem"]
+        if i in mark:
+            clock[i] = dict(kn)
+            clock[i][mark[i][0]] = mark[i][1]
+    for e in ("dve", "act", "pe", "pool"):
+        if count[e]:
+            g.wait_ge(T.sem[e], count[e])
+    g.wait_ge(T.sem.sent, nsent)
+    for i, o in enumerate(ops):
+        if o["sem"] is not None and o["sem"][1] is not None:
+            g.wait_ge(T.sem[o["sem"][0]], o["sem"][1])
+
+
+ORDER = []
+
+
+def rank_program(g, core, T, topo):
+    rank = T.rank_of(core)
+    if rank is None:
+        for r in range(len(T.cores)):
+            path = way(T, topo, r)
+            if len(path) == 3 and path[1] == core:
+                rid, pid = topo.addr(path[2], core)
+                nin = emask(topo, path[0], core)[1]
+                mk, nout = emask(topo, core, path[2])
+                for land, sem in MSG:
+                    g.wait_ge(T.sem[sem], nin)
+                    g.remote_dma(T[land][:], T[land][:], T.sem[sem], T.sem.sent, pid, rid, mk)
+                g.wait_ge(T.sem.sent, nout * len(MSG))
+        return
+    ops, nsent = build(g, T, topo, rank)
+    if not ORDER:
+        ORDER.append(plan(ops))
+    emit(g, T, ops, ORDER[0][0], nsent)

@@ -5,13 +5,14 @@ ALU = AluOpType
 ACT = ActivationFunctionType
 V, L, TV, LV, H = 1024, 256, 2, 2, 3
 W_, WC = 128, 8
-TR = 16
+TR = 32
 CHUNKS = [32, 32, 32, 32]
-EMODE = [[0, 1, 0, 1], [0, 1, 0, 1]]
+EMODE = [[[0, 0, 0, 1], [0, 1, 0, 1], [0, 1, 0, 1], [0, 1, 0, 1]], [[0, 1, 0, 1], [0, 0, 0, 1], [0, 1, 0, 1], [0, 0, 0, 0]]]
+SUBA, SUBV = 32, 32
 RED = [(0, 64), (64, 128)]
 ADDON = False
-LEAD = 12000.0
-TRIES, SEED = 1200, 0
+LEAD = 9000.0
+TRIES, SEED = 128, 3050
 BIG = 16384.0
 THETA = 8.5 * BIG
 
@@ -21,25 +22,25 @@ PER_STREAM = {
     "ry": (128, B), "yn": (128, B), "ym": (128, B), "lst": (48, U), "k16": (384, U), "kf": (384, K),
     "xb": (2048, B), "xc": (2048, B), "dab": (2048, B), "dcb": (2048, B), "rab": (2048, B), "acb": (2048, B), "aac": (2048, B),
     "pqr": (384, B), "albe": (256, K), "prod": (640, K), "keyt": (128, F), "scn": (128, F), "oht": (128, K), "oh": (128, K),
-    "zc": (8, F), "zx": (128, F), "ne": (128, B), "nd": (128, B), "zt": (8, K), "idx": (32, U), "xz": (128, B), "hh": (256, B),
+    "zc": (8, F), "zx": (256, F), "ne": (256, B), "nd": (256, B), "zt": (8, K), "idx": (16, U), "xz": (128, B), "hh": (256, B),
     "rnd": (128, I32), "nvc": (128, K), "w12": (256, K), "sm": (128, F), "off0": (128, B), "yw": (672, B), "thr": (4, F),
 }
 SHARED = {
     "l32": (56, I32), "la": (48, U), "ab": (32, F), "rc": (16, U),
     "ones": (128, B), "idb": (128, B), "nidb": (128, B), "bo0": (128, B), "bob": (128, B), "idk": (128, K), "idp": (128, K), "idn": (128, K),
     "id4k": (128, B), "bok": (128, K), "db": (256, B), "ndb": (256, B), "dk": (256, K), "dk128": (256, K), "dk4k": (256, K),
-    "wb": (144, B), "wn": (144, B), "wk": (144, K), "pi": (4, I32), "pc": (8, F), "tb": (128, B), "seg": (128, F), "rst": (128, B),
-    "tri": (128, B), "tri0": (128, F), "ci": (32, I32), "cu": (32, U), "jc": (48, B), "jf": (128, F), "nid": (512, F), "nl": (64, F), "m192": (16, B),
+    "wb": (144, B), "wn": (144, B), "wk": (144, K), "pi": (4, I32), "pc": (8, F), "tb": (128, B), "seg": (128, F), "rst": (256, B),
+    "tri": (256, B), "tri0": (256, F), "ci": (48, I32), "cu": (48, U), "jc": (48, B), "jf": (256, F), "nid": (512, F), "nl": (64, F), "m192": (32, B),
 }
 SCRATCH = {n: ("sbuf", [128, c], d) for n, (c, d) in SHARED.items()}
 for s_ in range(2):
     SCRATCH.update({"%s_%d" % (n, s_): ("sbuf", [128, c], d) for n, (c, d) in PER_STREAM.items()})
     SCRATCH.update({"%s_%d" % (n, s_): ("psum", [128, 512], F) for n in ("pa", "pk", "pr0", "pr1")})
-NDMA = 60
+NDMA = 68
 MSG = (("rc", "arc"), ("ra_0", "ara0"), ("ry_0", "ary0"), ("ra_1", "ara1"), ("ry_1", "ary1"))
 SEMAPHORES = ["dve", "act", "pe", "pool", "sent"] + [m_[1] for m_ in MSG] + ["d%d" % i for i in range(NDMA)]
-G_, SC_, PE_, TT_ = 1.56, 3.8, 0.5, 2.0
-HOP, SAME = 100.0, 70.0
+G_, SC_, PE_, TT_ = 1.6, 4.0, 0.52, 2.0
+HOP, SAME = 110.0, 75.0
 
 
 def way(T, topo, r):
@@ -221,8 +222,8 @@ def build(g, T, topo, rank):
             q = ("sp", "act")[h]
             for j, x in ((1, T.sb), (2, T.ic), (0, T.ia)):
                 dma(q, A("l32", 16 * j + WC * s, 16 * j + WC * s + WC, h=h), x[rows, WC * h:WC * h + WC], 2048)
-            dma(q, A("C", 0, V, h=h), T.ch[rows, :], 524288 + 786432 * s)
-            dma(q, A("X", TR, TR + V, h=h), T.x[rows, :], 786432 * (s + 1))
+            dma(q, A("X", TR, TR + V, h=h), T.x[rows, :], 262144 + 786432 * s)
+            dma(q, A("C", 0, V, h=h), T.ch[rows, :], 786432 * (s + 1))
     for s in range(2):
         now[0] = s
         rows = slice(64 * s, 64 * s + 64)
@@ -249,7 +250,7 @@ def build(g, T, topo, rank):
     ts(A("pi", 2, 3), A("pi", 0, 1), 64, ALU.bitwise_and)
     cp(A("pc", 0, 2), A("pi", 1, 3))
     ts(A("pc", 2, 3), A("pc", 0, 1), -1.0, ALU.mult, 15.0, ALU.add)
-    ts(A("pc", 3, 4), A("pc", 0, 1), -1.0, ALU.mult, 16.0, ALU.add)
+    ts(A("pc", 3, 4), A("pc", 0, 1), 16.0, ALU.add)
     ts(A("pc", 4, 5), A("pc", 1, 2), 2.0, ALU.mult, A("pc", 0, 1), ALU.add)
     ts(A("pc", 5, 6), A("pc", 0, 1), 16.0, ALU.mult)
     R_, R15, R16, HR, RX16 = A("pc", 0, 1), A("pc", 2, 3), A("pc", 3, 4), A("pc", 4, 5), A("pc", 5, 6)
@@ -267,10 +268,12 @@ def build(g, T, topo, rank):
     ts(A("tb"), A("ones"), R15, ALU.mult)
     ms(A("seg"), 1.0)
     ms(A("seg", 0, 128, 16), 0.0)
-    ts(A("rst"), A("seg"), -1.0, ALU.mult, 1.0, ALU.add)
-    iota(A("tri0"), [[0, 8], [1, 16]], 0, 0)
+    ms(A("rst"), 0.0)
+    ms(A("rst", 0, 256, 32), 1.0)
+    iota(A("tri0"), [[-16, 2], [0, 4], [1, 32]], 0, 0)
     ts(A("jf"), A("tri0"), R_, ALU.is_ge, 4096.0, ALU.mult)
-    ts(A("tri"), A("jf"), R16, ALU.max)
+    ts(A("tri"), A("jf"), float(TR), ALU.max)
+    iota(A("ci", 32, 48), [[1, 2], [2, 4], [0, 2]], 0, 0)
     iota(A("ci", 0, 16), [[1, 16]], 0, 0)
     iota(A("ci", 16, 32), [[16, 16]], 15, 0)
     cp(A("cu"), A("ci"))
@@ -329,21 +332,29 @@ def build(g, T, topo, rank):
                 q0 = 2 * w if fin else 0
                 mm((A("pk", q0, 3 * w), [(A("idk"), A("kf", q0, 3 * w))]),
                    (A("pk", 3 * w, 4 * w), [(A("idp"), kk("kf", "a")), (A("idn"), kk("kf", "b"))]))
-                both("pr0", 0, w, [("db", ("pqr", 0, w)), ("db", ("pqr", 2 * w, 3 * w)), ("ndb", ("pqr", w, 2 * w))])
-                ts(A("X", n, n + L), A("pr0", 0, L), 0.0, ALU.max, 63.0, ALU.min)
-                if t == TV - 1 and fin:
-                    dma("sp", T.xo[64 * s:64 * s + 64, 1536:2048], A("X", TR + 1536, TR + 2048, h=0), 65536)
+                mm((A("pr0", L, L + w), [(A("idb"), kk("pqr", "a")), (A("idb"), kk("pqr", "b")), (A("nidb"), kk("pqr", "c"))]))
+                own = ("pqr", 0, w) if fin else ("yw", 2 * w, 3 * w)
+                ts(A(*own), A("pr0", L, L + w), 0.0, ALU.max, 63.0, ALU.min)
+                if t < TV - 1:
+                    both("pr0", 0, w, [("db", own)])
+                    act(A("X", n, n + L), A("pr0", 0, L), ACT.Copy)
+                else:
+                    for h in range(2):
+                        dma("sp", T.xo[64 * s:64 * s + 64, n - TR + w * h:n - TR + w * h + w], A(*own, h=h), 16384)
                 s0 = 0
-                for cwid, em in zip(CHUNKS, EMODE[s]):
+                for cwid, em in zip(CHUNKS, EMODE[s][m]):
                     a, b = 16 * s0, 16 * (s0 + cwid)
-                    ga, gb, gc_ = [IND(xw, kk("k16", x, s0, s0 + cwid)) for x in "abc"]
-                    act(A("xb", a, b), gb, ACT.Copy)
+                    for e0 in range(s0, s0 + cwid, SUBA):
+                        act(A("xb", 16 * e0, 16 * (e0 + SUBA)), IND(xw, kk("k16", "b", e0, e0 + SUBA)), ACT.Copy)
                     if em:
-                        act(A("xc", a, b), gc_, ACT.Copy)
-                    else:
-                        tt(A("dcb", a, b), gc_, A("xb", a, b), ALU.subtract)
-                        act(A("acb", a, b), A("dcb", a, b), ACT.Abs)
-                    tt(A("dab", a, b), ga, A("xb", a, b), ALU.subtract)
+                        for e0 in range(s0, s0 + cwid, SUBA):
+                            act(A("xc", 16 * e0, 16 * (e0 + SUBA)), IND(xw, kk("k16", "c", e0, e0 + SUBA)), ACT.Copy)
+                    for x in ("a" if em else "ca"):
+                        for e0 in range(s0, s0 + cwid, SUBV):
+                            cols = (16 * e0, 16 * (e0 + SUBV))
+                            tt(A("d%sb" % x, *cols), IND(xw, kk("k16", x, e0, e0 + SUBV)), A("xb", *cols), ALU.subtract)
+                        if x == "c":
+                            act(A("acb", a, b), A("dcb", a, b), ACT.Abs)
                     ts(A("rab", a, b), A("dab", a, b), -2.0 ** -11, ALU.max, 32.0, ALU.mult)
                     us = list(range(a, b, 512))
                     rbs = []
@@ -377,8 +388,9 @@ def build(g, T, topo, rank):
 
                 def PR(x):
                     return A("prod", slots.index(x) * w, (slots.index(x) + 1) * w)
-                ts(A("albe"), A("pa", 0, 2 * w), A("thr", t, t + 1), ALU.is_gt, 128.0, ALU.mult)
-                tt(PR("x"), A("albe", 0, w), A("albe", w, 2 * w), ALU.mult)
+                ts(A("albe", 0, w), A("pa", 0, w), A("thr", t, t + 1), ALU.is_gt, 128.0, ALU.mult)
+                ts(A("pa", w, 2 * w), A("pa", w, 2 * w), A("thr", t, t + 1), ALU.is_gt, 128.0, ALU.mult)
+                tt(PR("x"), A("albe", 0, w), A("pa", w, 2 * w), ALU.mult)
                 tt(key, PR("x"), key, ALU.add)
                 tr(A("keyt"), key)
                 scan(A("scn"), A("seg"), A("keyt"), ALU.mult, ALU.max)
@@ -388,25 +400,27 @@ def build(g, T, topo, rank):
                     tt(PR(x), A("oh"), kk("pk", x), ALU.mult)
                 ts(PR("j"), A("oh"), R_, ALU.mult)
                 mm((A("pr0", 0, ns * WC), [(A("idb"), A("yw", 640, 664) if fin else A("jc", 0, ns * WC))] + [(W("wk", r), A("prod", r, ns * w, 16)) for r in range(16)]),
-                   (A("pr0", w, 2 * w), [(A("idb"), A("tri")), (A("bok"), PR("b"))]))
+                   *[(A("pr0", w + w * q, 2 * w + w * q), [(A("idb"), A("tri", w * q, w * q + w)), (A("bok"), PR("b"))]) for q in range(2)])
                 lo, nu = (40, 1) if fin else (0, 4)
                 cp(A("lst", lo, lo + nu * WC), A("pr0", 0, nu * WC))
-                act(A("zc"), A("pr0", (ns - 2) * WC, (ns - 1) * WC), ACT.Identity, bias=R16)
-                act(A("zx"), IND(A("zc"), A("cu", 0, WC)), ACT.Copy)
+                act(A("zc"), A("pr0", (ns - 2) * WC, (ns - 1) * WC), ACT.Identity, bias=float(TR))
+                act(A("zx"), IND(A("zc"), A("cu", 32, 48)), ACT.Copy)
                 cl = A("pr0", (ns - 1) * WC, ns * WC)
                 if fin:
                     for q in range(2 if t < TV - 1 else 1):
                         act(A("sm", WC * q, WC * q + WC), cl, ACT.Relu, bias=THETA / 2, scale=-0.5)
                 else:
                     act(A("yw", 656, 664), cl, ACT.Relu, bias=-128.0 * BIG, scale=16.0)
-                tt(A("ne"), A("zx"), A("pr0", w, 2 * w), ALU.not_equal)
+                tt(A("ne"), A("zx"), A("pr0", w, 3 * w), ALU.not_equal)
                 scan(A("nd"), A("rst"), A("ne"), ALU.max, ALU.min)
-                tt(A("zt"), A("nd", 15, w, 16), A("zc"), ALU.mult)
+                tt(A("zt"), A("nd", 31, 2 * w, 32), A("zx", 31, 2 * w, 32), ALU.mult)
                 act(A("xz"), IND(A("xb"), A("lst", lo, lo + WC)), ACT.Copy)
                 both("pr1", 0, w, [("db", ("xz",)), ("db", (yv,))])
                 act(A("hh"), A("pr1", 0, L), ACT.Identity, bias=191.75, scale=0.5)
-                both("pr0", 2 * w, WC, [("dk", ("zt",))])
-                ts(A("idx", 0, 32, 2), A("pr0", 2 * w, 2 * w + 2 * WC), R_, ALU.add)
+                mm(*[(A("pr0", 3 * w + 8 * q + 4 * h, 3 * w + 8 * q + 4 * h + 4), [(A("dk", 128 * h, 128 * h + 128), A("zt", 4 * q, 4 * q + 4))])
+                     for q in range(2) for h in range(2)])
+                for q in range(2):
+                    ts(A("idx", q, 16, 2), A("pr0", 3 * w + 8 * q, 3 * w + 8 * q + 8), (R_, R16)[q], ALU.max)
                 if fin:
                     k = old["n"]
                     tt(A("sm", 16, 16 + k), old, A("sm", 0, k), ALU.add)
@@ -414,8 +428,8 @@ def build(g, T, topo, rank):
                     if t < TV - 1:
                         cp(A("sa"), A("sm", 32, 48))
                         send(A("sa", 0, WC))
-                for c in range(2 * WC - 1, -1, -1):
-                    tt(IND(sw, A("idx", 2 * c, 2 * c + 1)), A("hh", 16 * c, 16 * c + 16), A("m192"), ALU.add)
+                for c in range(WC - 1, -1, -1):
+                    tt(IND(sw, A("idx", 2 * c, 2 * c + 2)), A("hh", 32 * c, 32 * c + 32), A("m192"), ALU.add)
                 dk = A("pk", 3 * w, 4 * w)
                 ts(A("rnd"), key, -49.0 / 128, ALU.add, 16200.0, ALU.max)
                 tt(A("nvc"), A("rnd"), key, ALU.is_lt)
@@ -438,8 +452,6 @@ def build(g, T, topo, rank):
                 mm((cnt, [(A("bok"), PR("x"))] + ([(A("id4k"), A("off0"))] if fin else [])))
                 if not fin:
                     act(A("off0"), cnt, ACT.Relu, bias=-512.0, scale=1.0 / 256)
-                    for h in range(2):
-                        act(A("yw", 2 * w, 3 * w, h=h), A("X", n0 + w * h, n0 + w * h + w, h=h), ACT.Copy)
                     mm((cnt, [(A("idb"), A(yv)), (A("nidb"), X0)]))
                     act(PP, cnt, ACT.Abs)
                     mm((cnt, [(A("idb"), PP), (A("nidb"), X0)]))

@@ -5,38 +5,42 @@ ALU = AluOpType
 ACT = ActivationFunctionType
 V, L, TV, LV, H = 1024, 256, 2, 2, 3
 W_, WC = 128, 8
-TR = 32
-CHUNKS = [32, 32, 32, 32]
-EMODE = [[[0, 0, 0, 1], [0, 1, 0, 1], [0, 1, 0, 1], [0, 1, 0, 1]], [[0, 1, 0, 1], [0, 0, 0, 1], [0, 1, 0, 1], [0, 0, 0, 0]]]
-SUBA, SUBV = 32, 32
-RED = [(0, 64), (64, 128)]
-ADDON = False
+TR = 16
+NX = V + 512
+STEPS = {0: [(0, 32, "r"), (32, 32, "r"), (64, 32, "r"), (96, 32, "r")],
+         1: [(0, 32, "r"), (96, 32, "e"), (32, 32, "r"), (64, 32, "r")],
+         2: [(0, 32, "r"), (96, 32, "e"), (64, 32, "e"), (32, 32, "r")]}
+EMODE = [[1, 1, 1, 1], [1, 1, 1, 1]]
+KS = [[0, 1, 1, 1], [1, 1, 1, 1]]
 LEAD = 9000.0
-TRIES, SEED = 128, 3050
+TRIES, SEED = 512, 3050
 BIG = 16384.0
-THETA = 8.5 * BIG
+HH = 2.0 ** 17
 
 B, F, I32, U, K = "bfloat16", "float32", "int32", "uint16", "float16"
 PER_STREAM = {
-    "X": (TR + 2048, B), "C": (1536, I32), "CO": (1024, F), "y": (128, B), "sa": (16, U), "ra": (8, U),
-    "ry": (128, B), "yn": (128, B), "ym": (128, B), "lst": (48, U), "k16": (384, U), "kf": (384, K),
+    "X": (2 * TR + NX, B), "C": (NX, I32), "CO": (512, F), "CI": (256, I32), "y": (128, B), "sa": (16, U), "ra": (8, U), "la": (24, U),
+    "ry": (128, B), "yn": (256, B), "lst": (24, U), "k16": (384, U), "kf": (384, K), "nv": (512, B),
     "xb": (2048, B), "xc": (2048, B), "dab": (2048, B), "dcb": (2048, B), "rab": (2048, B), "acb": (2048, B), "aac": (2048, B),
-    "pqr": (384, B), "albe": (256, K), "prod": (640, K), "keyt": (128, F), "scn": (128, F), "oht": (128, K), "oh": (128, K),
-    "zc": (8, F), "zx": (256, F), "ne": (256, B), "nd": (256, B), "zt": (8, K), "idx": (16, U), "xz": (128, B), "hh": (256, B),
-    "rnd": (128, I32), "nvc": (128, K), "w12": (256, K), "sm": (128, F), "off0": (128, B), "yw": (672, B), "thr": (4, F),
+    "pqr": (384, B), "thd": (256, K), "keys": (128, F), "scn": (128, F), "bs": (768, B), "ks": (256, K),
+    "rnd": (128, I32), "prod": (512, K), "lt": (256, K), "ad": (256, B), "nd": (256, B),
+    "idx": (16, U), "hh": (256, B), "sm": (128, F), "thr": (4, F),
 }
+PARTS = {n: ("bs", 128 * j) for j, n in enumerate(("tp", "col", "oht", "xz", "off0", "ty"))}
+PARTS.update({n: ("ks", 128 * j) for j, n in enumerate(("sel", "wv"))})
 SHARED = {
-    "l32": (56, I32), "la": (48, U), "ab": (32, F), "rc": (16, U),
-    "ones": (128, B), "idb": (128, B), "nidb": (128, B), "bo0": (128, B), "bob": (128, B), "idk": (128, K), "idp": (128, K), "idn": (128, K),
-    "id4k": (128, B), "bok": (128, K), "db": (256, B), "ndb": (256, B), "dk": (256, K), "dk128": (256, K), "dk4k": (256, K),
-    "wb": (144, B), "wn": (144, B), "wk": (144, K), "pi": (4, I32), "pc": (8, F), "tb": (128, B), "seg": (128, F), "rst": (256, B),
-    "tri": (256, B), "tri0": (256, F), "ci": (48, I32), "cu": (48, U), "jc": (48, B), "jf": (256, F), "nid": (512, F), "nl": (64, F), "m192": (32, B),
+    "l32": (56, I32), "lb": (16, U), "ab": (32, F), "rc": (16, U),
+    "ones": (128, B), "onk": (128, K), "idb": (128, B), "nidb": (128, B), "bo0": (128, B), "bob": (128, B), "idk": (128, K), "nidk": (256, K),
+    "id4k": (128, B), "id16k": (128, B), "idm": (128, B), "idh": (128, B), "bok": (128, K), "db": (256, B), "db4k": (256, B), "ndb4k": (256, B),
+    "dsum": (128, F), "wk": (144, K), "b8": (40, B), "bl16": (16, K), "tk": (256, B), "pi": (4, I32), "pc": (8, F), "seg": (128, F), "rst": (256, B),
+    "ee": (256, K), "i9": (8, K), "t1": (256, F), "t2": (256, F), "t3": (256, F), "t4": (16, F), "ci": (8, I32), "cu": (8, U),
+    "nid": (512, F), "nl": (64, F), "m192": (32, B),
 }
 SCRATCH = {n: ("sbuf", [128, c], d) for n, (c, d) in SHARED.items()}
 for s_ in range(2):
     SCRATCH.update({"%s_%d" % (n, s_): ("sbuf", [128, c], d) for n, (c, d) in PER_STREAM.items()})
-    SCRATCH.update({"%s_%d" % (n, s_): ("psum", [128, 512], F) for n in ("pa", "pk", "pr0", "pr1")})
-NDMA = 68
+    SCRATCH.update({"%s_%d" % (n, s_): ("psum", [128, 512], F) for n in ("pd", "pk", "pr0", "pr1")})
+NDMA = 100
 MSG = (("rc", "arc"), ("ra_0", "ara0"), ("ry_0", "ary0"), ("ra_1", "ara1"), ("ry_1", "ary1"))
 SEMAPHORES = ["dve", "act", "pe", "pool", "sent"] + [m_[1] for m_ in MSG] + ["d%d" % i for i in range(NDMA)]
 G_, SC_, PE_, TT_ = 1.6, 4.0, 0.52, 2.0
@@ -68,15 +72,18 @@ def build(g, T, topo, rank):
     ndma = [0]
     now = [None]
 
-    def A(name, a=None, b=None, s=None, h=None):
+    def A(name, a=None, b=None, s=None, h=None, p=None):
+        if name in PARTS:
+            name, a = PARTS[name]
+            b = a + 128
         if name not in SCRATCH:
             name = "%s_%d" % (name, now[0])
         n = SCRATCH[name][1][1]
         a0, b0, s0 = a or 0, n if b is None else b, s or 1
         cols = range(a0, b0, s0)
         bits = ((1 << (b0 - a0)) - 1) << a0 if s0 == 1 else sum(1 << c for c in cols)
-        bits = bits | bits << n if h is None else bits << (n * h)
-        p0, p1 = (0, 128) if h is None else (64 * h, 64 * h + 64)
+        p0, p1 = (0, p or 128) if h is None else (64 * h, 64 * h + 64)
+        bits = bits | bits << n if p1 - p0 > 64 else bits << (n * (p0 // 64))
         ap = T[name][p0:p1, a0:b0] if s0 == 1 else T[name][p0:p1, a0:b0:s0]
         return {"name": name, "ap": ap, "n": len(cols), "acc": [(name, bits)], "ind": False}
 
@@ -119,7 +126,8 @@ def build(g, T, topo, rank):
                     if st[3] is not None and st[3] != i:
                         dep(st[3])
                     st[3] = i
-        ops.append({"eng": eng, "fn": fn, "deps": deps, "busy": busy, "lat": lat, "sem": sem, "s": now[0]})
+        ops.append({"eng": eng, "fn": fn, "deps": deps, "busy": busy, "lat": lat, "sem": sem, "s": now[0],
+                    "out": writes[0]["name"] if writes else ""})
         return i
 
     def vcost(out, ins, two=False):
@@ -149,9 +157,6 @@ def build(g, T, topo, rank):
             fn = lambda: g.vector.tensor_scalar(out["ap"], a["ap"], sc(s1), sc(s2), o0, o1)
         return op("dve", fn, [a, s1, s2], [out], vcost(out, [a]))
 
-    def tr(out, a):
-        return op("dve", lambda: g.vector.transpose(out["ap"], a["ap"]), [a], [out], vcost(out, [a]))
-
     def scan(out, d0, d1, o0, o1):
         return op("dve", lambda: g.vector.tensor_tensor_scan(out["ap"], d0["ap"], d1["ap"], 0.0, o0, o1), [d0, d1], [out], vcost(out, [d0, d1]))
 
@@ -162,23 +167,22 @@ def build(g, T, topo, rank):
         if acc is None:
             fn = lambda: g.scalar.activation(out["ap"], a["ap"], f, sc(bias), scale)
         else:
-            fn = lambda: g.scalar.activation(out["ap"], a["ap"], f, accum_out=acc["ap"])
-        return op("act", fn, [a, bias], [out] + ([acc] if acc else []), 65 + max(64, out["n"] * (G_ if a["ind"] else 1)))
+            fn = lambda: g.scalar.activation(out["ap"], a["ap"], f, sc(bias), scale, accum_out=acc["ap"])
+        return op("act", fn, [a, bias], [out] + ([acc] if acc else []), 65 + max(64, out["n"] * (G_ if a["ind"] else 1)) + (140 if acc else 0))
 
-    def mm(*groups, start=True, stop=True):
+    def mm(*groups, start=True, stop=True, one=False):
         out = groups[0][0]
 
         def fn():
             r = out
-            for o, terms in groups:
+            for j, (o, terms) in enumerate(groups):
                 for q, (w, x) in enumerate(terms):
-                    r = g.tensor.matmul(o["ap"], w["ap"], x["ap"], start and q == 0, stop and q == len(terms) - 1)
+                    first = q == 0 and (j == 0 or not one)
+                    final = q == len(terms) - 1 and (j == len(groups) - 1 or not one)
+                    r = g.tensor.matmul(o["ap"], w["ap"], x["ap"], start and first, stop and final)
             return r
         return op("pe", fn, [a for o, terms in groups for t_ in terms for a in t_], [o for o, terms in groups],
-                  sum(12 + PE_ * max(64, x["n"]) for o, terms in groups for w, x in terms))
-
-    def both(name, a, n, terms):
-        return mm(*[(A(name, a + h * n, a + (h + 1) * n), [(A(w, 128 * h, 128 * h + 128), A(*x)) for w, x in terms]) for h in range(2)])
+                  sum(12 + PE_ * max(min(64, w["n"]), x["n"]) * (4 if wide(x) else 1) for o, terms in groups for w, x in terms))
 
     def iota(out, pat, base, cm):
         if SCRATCH[out["name"]][2] == I32:
@@ -215,15 +219,17 @@ def build(g, T, topo, rank):
         j = op("net", None, [], [A(land)], 0, 5000.0, (sem, na_))
         ops[j]["deps"][i] = "t"
 
+    SL = {"a": 0, "c": 1, "b": 2, "x": 3}
+    w = W_
     for s in range(2):
         now[0] = s
         rows = slice(64 * s, 64 * s + 64)
         for h in range(2):
             q = ("sp", "act")[h]
-            for j, x in ((1, T.sb), (2, T.ic), (0, T.ia)):
-                dma(q, A("l32", 16 * j + WC * s, 16 * j + WC * s + WC, h=h), x[rows, WC * h:WC * h + WC], 2048)
-            dma(q, A("X", TR, TR + V, h=h), T.x[rows, :], 262144 + 786432 * s)
-            dma(q, A("C", 0, V, h=h), T.ch[rows, :], 786432 * (s + 1))
+            for j, x in ((2, T.sb), (1, T.ic), (0, T.ia)):
+                dma(q, A("l32", 24 * s + WC * j, 24 * s + WC * j + WC, h=h), x[rows, WC * h:WC * h + WC], 2048)
+            dma(q, A("C", 0, V, h=h), T.ch[rows, :], 524288 + 786432 * s)
+            dma(q, A("X", TR, TR + V, h=h), T.x[rows, :], 786432 * (s + 1))
     for s in range(2):
         now[0] = s
         rows = slice(64 * s, 64 * s + 64)
@@ -231,12 +237,14 @@ def build(g, T, topo, rank):
             dma("sp", A("l32", 48 + 4 * s, 49 + 4 * s, h=h), T.th[rows, :], 786432 * 2)
             dma("sp", A("y", h=h), T.y[rows, W_ * h:W_ * h + W_], 786432 * 2)
         ms(A("X", 0, TR), 0.0)
+        ms(A("X", TR + V, 2 * TR + NX), 0.0)
     for q in ("sp", "act"):
         mine = [i for i, o in enumerate(ops) if o["eng"] == q]
         for i, j in zip(mine, mine[1:]):
             ops[j]["deps"][i] = "o"
     now[0] = None
     ms(A("ones"), 1.0)
+    cp(A("onk"), A("ones"))
     ms(A("m192"), -192.0)
     asel(A("idb"), A("ones"), [[-1, 128]], ALU.is_equal, 0.0, 0, 1)
     asel(A("bo0"), A("ones"), [[-16, 8], [0, 16]], ALU.is_ge, 0.0, 0, 1)
@@ -250,112 +258,126 @@ def build(g, T, topo, rank):
     ts(A("pi", 2, 3), A("pi", 0, 1), 64, ALU.bitwise_and)
     cp(A("pc", 0, 2), A("pi", 1, 3))
     ts(A("pc", 2, 3), A("pc", 0, 1), -1.0, ALU.mult, 15.0, ALU.add)
-    ts(A("pc", 3, 4), A("pc", 0, 1), 16.0, ALU.add)
+    ts(A("pc", 3, 4), A("pc", 0, 1), float(TR + NX), ALU.add)
     ts(A("pc", 4, 5), A("pc", 1, 2), 2.0, ALU.mult, A("pc", 0, 1), ALU.add)
-    ts(A("pc", 5, 6), A("pc", 0, 1), 16.0, ALU.mult)
-    R_, R15, R16, HR, RX16 = A("pc", 0, 1), A("pc", 2, 3), A("pc", 3, 4), A("pc", 4, 5), A("pc", 5, 6)
-    for name, w in (("nidb", -1.0), ("idk", 1.0), ("idp", 1.0 / 128), ("idn", -1.0 / 128), ("id4k", 4096.0)):
-        ts(A(name), A("idb"), w, ALU.mult)
-    for name, w in (("ndb", -1.0), ("dk", 1.0), ("dk128", -128.0), ("dk4k", 4096.0)):
-        ts(A(name), A("db"), w, ALU.mult)
-    cp(A("bok"), A("bob"))
-    for name, w in (("wb", 1.0), ("wn", -16.0), ("wk", 1.0)):
-        ms(A(name), 0.0)
-        ts(A(name, 15, 143, 16), A("bob", 0, 128, 16), w, ALU.mult)
+    ts(A("pc", 5, 6), A("pi", 0, 1), 16.0, ALU.is_ge, 4096.0, ALU.mult)
+    ts(A("pc", 6, 7), A("pi", 0, 1), 8.0, ALU.is_equal)
+    ts(A("pc", 7, 8), A("pc", 1, 2), 2.0, ALU.mult)
+    R_, R15, HI, HR, S16, S8, H128 = [A("pc", j, j + 1) for j in (0, 2, 3, 4, 5, 6, 7)]
+    for name, x in (("nidb", -1.0), ("idk", 1.0), ("id4k", 4096.0), ("id16k", BIG), ("idm", -9.0 / 64), ("idh", 0.5)):
+        act(A(name), A("idb"), ACT.Copy, scale=x)
+    for q in range(2):
+        act(A("nidk", 128 * q, 128 * q + 128), A("idb"), ACT.Copy, scale=-1.0)
+    ts(A("tk", 0, 128), A("idb"), R15, ALU.mult)
+    act(A("tk", 128, 256), A("idb"), ACT.Copy, scale=-1.0 / 64)
+    for name, x in (("db4k", 4096.0), ("ndb4k", -4096.0)):
+        act(A(name), A("db"), ACT.Copy, scale=x)
+    for h in range(2):
+        for q in range(2):
+            act(A("dsum", 64 * q, 64 * q + 64, h=h), A("idb", 64 * h, 64 * h + 64, h=h), ACT.Copy, scale=0.5)
+    act(A("bok"), A("bob"), ACT.Copy)
+    for j, x in enumerate((1.0, -16.0, 32.0, 32.0, -1.0)):
+        ts(A("b8", 8 * j, 8 * j + 8), A("bob", 0, 128, 16), x, ALU.mult)
+    for j in range(4):
+        cp(A("bl16", 4 * j, 4 * j + 4), A("bob", 64 * (j // 2), 64 * (j // 2) + 64, 16))
+    ms(A("bo0"), 0.0)
+    cp(A("wk", 0, 128), A("bo0"))
+    cp(A("wk", 128, 144), A("bo0", 0, 16))
+    cp(A("wk", 15, 143, 16), A("bob", 0, 128, 16))
 
-    def W(name, k):
-        return A(name, 15 - k, 143 - k)
-    ts(A("tb"), A("ones"), R15, ALU.mult)
+    def W(k):
+        return A("wk", 15 - k, 143 - k)
     ms(A("seg"), 1.0)
     ms(A("seg", 0, 128, 16), 0.0)
     ms(A("rst"), 0.0)
     ms(A("rst", 0, 256, 32), 1.0)
-    iota(A("tri0"), [[-16, 2], [0, 4], [1, 32]], 0, 0)
-    ts(A("jf"), A("tri0"), R_, ALU.is_ge, 4096.0, ALU.mult)
-    ts(A("tri"), A("jf"), float(TR), ALU.max)
-    iota(A("ci", 32, 48), [[1, 2], [2, 4], [0, 2]], 0, 0)
-    iota(A("ci", 0, 16), [[1, 16]], 0, 0)
-    iota(A("ci", 16, 32), [[16, 16]], 15, 0)
+    iota(A("t1"), [[-16, 2], [0, 4], [1, 32]], 16, -1)
+    iota(A("t2"), [[1, 2], [2, 4], [0, 32]], 0, -1)
+    ts(A("t1"), A("t1"), 0.0, ALU.is_ge, S16, ALU.mult)
+    ts(A("t2"), A("t2"), 0.0, ALU.is_equal, -1.0, ALU.mult)
+    tt(A("ee"), A("t1"), A("t2"), ALU.add)
+    iota(A("t3"), [[0, 16], [1, 16]], 16, -1)
+    iota(A("t4", 0, 8), [[1, 8]], 0, -1)
+    iota(A("t4", 8, 16), [[0, 4], [8192, 2]], TR - 4096, 0)
+    ts(A("t4", 0, 8), A("t4", 0, 8), 0.0, ALU.is_equal)
+    ts(A("t4", 8, 16), A("t4", 8, 16), S8, ALU.mult)
+    tt(A("i9"), A("t4", 0, 8), A("t4", 8, 16), ALU.add)
+    iota(A("ci"), [[16, 8]], 15, 0)
     cp(A("cu"), A("ci"))
-    ms(A("jc", WC, 48), 0.0)
-    ts(A("jc", 0, WC), A("ci", 0, WC), 256.0, ALU.mult, RX16, ALU.add)
-    iota(A("nid"), [[512, 2], [1, 256]], V + L, 0)
+    iota(A("nid", 256, 512), [[512, 2], [1, 128]], V + L, 0)
+    ts(A("nid", 0, 256), A("nid", 256, 512), H128, ALU.add)
     iota(A("nl", 32, 64), [[512, 2], [0, 2], [16, WC]], V, 0)
     ts(A("nl", 0, 32), A("nl", 32, 64), HR, ALU.add)
     for s in range(2):
         now[0] = s
-        for j in (1, 2, 0):
-            o = 16 * j + WC * s
-            cp(A("la", o, o + WC), A("l32", o, o + WC))
-            if j < 2:
-                cp(A("ab", 16 * s + WC * j, 16 * s + WC * j + WC), A("l32", o, o + WC))
-        cp(A("yw", 640, 656), A("jc", 0, 16))
+        o = 24 * s
+        cp(A("la"), A("l32", o, o + 24))
+        cp(A("lb", WC * s, WC * s + WC), A("l32", o + 16, o + 24))
+        cp(A("ab", 16 * s, 16 * s + WC), A("l32", o, o + WC))
+        cp(A("ab", 16 * s + WC, 16 * s + 16), A("l32", o + 16, o + 24))
+        ts(A("lt"), A("t3"), 0.0, ALU.is_equal, S8, ALU.add)
         cp(A("thr", 0, 1), A("l32", 48 + 4 * s, 49 + 4 * s))
+        ts(A("thd"), A("nidk"), A("thr", 0, 1), ALU.mult)
     now[0] = None
-    send(A("la", 16, 32))
+    send(A("lb"))
 
-    SL = {"a": 0, "c": 1, "b": 2}
-    w = W_
     for s in range(2):
         now[0] = s
         ring = [0]
-        PP, EE, X0, WY, OFF = [A("yw", w * q, w * q + w) for q in range(5)]
+        rows = slice(64 * s, 64 * s + 64)
         for t in range(TV):
             xw = A("X", TR, TR + V + 512 * t)
-            sw = A("X", 0, TR + V + 512 * t)
+            sw = A("X")
             yv = "y" if t == 0 else "ry"
-            n0 = TR + V + 512 * t
             old = A("ab", 16 * s, 16 * s + 16) if t == 0 else A("sm", 40, 48)
             for lev in range(LV):
                 fin = lev == LV - 1
-                n = n0 + lev * L
                 m = t * LV + lev
+                n = V + m * L
                 cw = A("C", 0, V + (0 if t == 0 else 256 * (lev + 1)))
-
-                def cur(x):
-                    if t == 0:
-                        o = {"a": 0, "b": 16, "c": 32}[x] + WC * s
-                        return A("la", o, o + WC)
-                    return {"a": A("ra"), "b": A("sa", WC, 2 * WC), "c": A("rc", WC * s, WC * s + WC)}[x]
 
                 def kk(name, x, a=0, b=w):
                     return A(name, SL[x] * w + a, SL[x] * w + b)
-                if lev > 0:
-                    cp(A("k16"), IND(cw, A("lst", WC, 4 * WC)))
-                    act(A("pqr"), IND(xw, A("lst", WC, 4 * WC)), ACT.Copy)
+                if m == 2:
+                    parts = [(A("sa", WC, 2 * WC), 2, 3), (A("rc", WC * s, WC * s + WC), 1, 2), (A("ra"), 0, 1)]
                 else:
-                    for x in "bca":
-                        cp(kk("k16", x), IND(cw, cur(x)))
-                    for x in "bca":
-                        act(kk("pqr", x), IND(xw, cur(x)), ACT.Copy)
-                cp(A("kf"), A("k16"))
-                q0 = 2 * w if fin else 0
-                mm((A("pk", q0, 3 * w), [(A("idk"), A("kf", q0, 3 * w))]),
-                   (A("pk", 3 * w, 4 * w), [(A("idp"), kk("kf", "a")), (A("idn"), kk("kf", "b"))]))
+                    parts = [(A("la" if m == 0 else "lst"), 0, 3)]
+                for lists, a, b in parts:
+                    if KS[s][m]:
+                        act(A("kf", a * w, b * w), IND(cw, lists), ACT.Copy)
+                        cp(A("k16", a * w, b * w), A("kf", a * w, b * w))
+                    else:
+                        cp(A("k16", a * w, b * w), IND(cw, lists))
+                        cp(A("kf", a * w, b * w), A("k16", a * w, b * w))
+                for lists, a, b in parts:
+                    act(A("pqr", a * w, b * w), IND(xw, lists), ACT.Copy)
                 mm((A("pr0", L, L + w), [(A("idb"), kk("pqr", "a")), (A("idb"), kk("pqr", "b")), (A("nidb"), kk("pqr", "c"))]))
-                own = ("pqr", 0, w) if fin else ("yw", 2 * w, 3 * w)
-                ts(A(*own), A("pr0", L, L + w), 0.0, ALU.max, 63.0, ALU.min)
-                if t < TV - 1:
-                    both("pr0", 0, w, [("db", own)])
-                    act(A("X", n, n + L), A("pr0", 0, L), ACT.Copy)
-                else:
-                    for h in range(2):
-                        dma("sp", T.xo[64 * s:64 * s + 64, n - TR + w * h:n - TR + w * h + w], A(*own, h=h), 16384)
-                s0 = 0
-                for cwid, em in zip(CHUNKS, EMODE[s][m]):
+                ts(A("nv", m * w, m * w + w), A("pr0", L, L + w), 0.0, ALU.max, 63.0, ALU.min)
+                for h in range(2):
+                    own = A("nv", m * w, m * w + w, h=h)
+                    if t < TV - 1:
+                        for h2 in range(2):
+                            dma("sp", A("X", TR + n + w * h, TR + n + w * h + w, h=h2), own, 16384)
+                    else:
+                        dma("sp", T.xo[rows, n + w * h:n + w * h + w], own, 16384)
+                dk, cn = A("pd", 2 * w, 3 * w), A("pd", 3 * w, 4 * w)
+                mm((dk, [(kk("kf", "a"), A("idk")), (kk("kf", "b"), A("nidk", 0, w))]))
+                mm((A("pd", 0, 2 * w), [(A("onk"), A("thd"))]), stop=False)
+                mm((A("pk", 0, 2 * w), [(A("ones"), A("tk"))]), stop=False)
+                steps = STEPS[EMODE[s][m]]
+                for s0, cwid, form in steps:
+                    em = form == "e"
                     a, b = 16 * s0, 16 * (s0 + cwid)
-                    for e0 in range(s0, s0 + cwid, SUBA):
-                        act(A("xb", 16 * e0, 16 * (e0 + SUBA)), IND(xw, kk("k16", "b", e0, e0 + SUBA)), ACT.Copy)
+                    act(A("xb", a, b), IND(xw, kk("k16", "b", s0, s0 + cwid)), ACT.Copy)
                     if em:
-                        for e0 in range(s0, s0 + cwid, SUBA):
-                            act(A("xc", 16 * e0, 16 * (e0 + SUBA)), IND(xw, kk("k16", "c", e0, e0 + SUBA)), ACT.Copy)
+                        act(A("xc", a, b), IND(xw, kk("k16", "c", s0, s0 + cwid)), ACT.Copy)
                     for x in ("a" if em else "ca"):
-                        for e0 in range(s0, s0 + cwid, SUBV):
-                            cols = (16 * e0, 16 * (e0 + SUBV))
-                            tt(A("d%sb" % x, *cols), IND(xw, kk("k16", x, e0, e0 + SUBV)), A("xb", *cols), ALU.subtract)
-                        if x == "c":
+                        tt(A("d%sb" % x, a, b), IND(xw, kk("k16", x, s0, s0 + cwid)), A("xb", a, b), ALU.subtract)
+                        if x == "c" and form == "n":
                             act(A("acb", a, b), A("dcb", a, b), ACT.Abs)
-                    ts(A("rab", a, b), A("dab", a, b), -2.0 ** -11, ALU.max, 32.0, ALU.mult)
+                        elif x == "c":
+                            ts(A("acb", a, b), A("dcb", a, b), 0.0, ALU.max, 2.0, ALU.mult)
+                    ts(A("rab", a, b), A("dab", a, b), -2.0 ** -11, ALU.max)
                     us = list(range(a, b, 512))
                     rbs = []
                     for u in us:
@@ -363,64 +385,57 @@ def build(g, T, topo, rank):
                         ring[0] += 1
                     if em:
                         for u, rb in zip(us, rbs):
-                            mm((rb, [(A("idb"), A("xc", u, u + 512)), (A("nidb"), A("xb", u, u + 512))]), stop=not ADDON)
+                            mm((rb, [(A("idb"), A("xc", u, u + 512)), (A("nidb"), A("xb", u, u + 512))]))
                             act(A("acb", u, u + 512), rb, ACT.Abs)
                     for u, rb in zip(us, rbs):
-                        if em and ADDON:
-                            mm((rb, [(A("nidb"), A("dab", u, u + 512))]), start=False)
-                        elif em:
+                        if em:
                             mm((rb, [(A("idb"), A("xb", u, u + 512)), (A("nidb"), A("xc", u, u + 512)), (A("idb"), A("dab", u, u + 512))]))
                         else:
                             mm((rb, [(A("nidb"), A("dcb", u, u + 512)), (A("idb"), A("dab", u, u + 512))]))
                         act(A("aac", u, u + 512), rb, ACT.Abs)
-                    s0 += cwid
 
-                def red(name, wn, a, b):
-                    return [(W(wn, k), A(name, 16 * a + k, 16 * b, 16)) for k in range(16)]
-                key = A("pa", 2 * w, 3 * w)
-                for a, b in RED:
-                    mm((A("pa", w + a, w + b), red("acb", "wb", a, b)))
-                    mm((A("pa", 2 * w + a, 2 * w + b), [(A("idb"), A("tb", a, b))] + red("dab", "wn", a, b)), stop=False)
-                    mm((A("pa", 2 * w + a, 2 * w + b), red("rab", "wb", a, b)), start=False)
-                    mm((A("pa", a, b), red("aac", "wb", a, b)))
-                slots = "jbx" if fin else "jacbx"
-                ns = len(slots)
-
-                def PR(x):
-                    return A("prod", slots.index(x) * w, (slots.index(x) + 1) * w)
-                ts(A("albe", 0, w), A("pa", 0, w), A("thr", t, t + 1), ALU.is_gt, 128.0, ALU.mult)
-                ts(A("pa", w, 2 * w), A("pa", w, 2 * w), A("thr", t, t + 1), ALU.is_gt, 128.0, ALU.mult)
-                tt(PR("x"), A("albe", 0, w), A("pa", w, 2 * w), ALU.mult)
-                tt(key, PR("x"), key, ALU.add)
-                tr(A("keyt"), key)
-                scan(A("scn"), A("seg"), A("keyt"), ALU.mult, ALU.max)
-                tt(A("oht"), IND(A("scn"), A("cu", 16, 16 + WC)), A("keyt"), ALU.is_equal)
-                tr(A("oh"), A("oht"))
-                for x in ("b" if fin else "bca"):
-                    tt(PR(x), A("oh"), kk("pk", x), ALU.mult)
-                ts(PR("j"), A("oh"), R_, ALU.mult)
-                mm((A("pr0", 0, ns * WC), [(A("idb"), A("yw", 640, 664) if fin else A("jc", 0, ns * WC))] + [(W("wk", r), A("prod", r, ns * w, 16)) for r in range(16)]),
-                   *[(A("pr0", w + w * q, 2 * w + w * q), [(A("idb"), A("tri", w * q, w * q + w)), (A("bok"), PR("b"))]) for q in range(2)])
-                lo, nu = (40, 1) if fin else (0, 4)
-                cp(A("lst", lo, lo + nu * WC), A("pr0", 0, nu * WC))
-                act(A("zc"), A("pr0", (ns - 2) * WC, (ns - 1) * WC), ACT.Identity, bias=float(TR))
-                act(A("zx"), IND(A("zc"), A("cu", 32, 48)), ACT.Copy)
-                cl = A("pr0", (ns - 1) * WC, ns * WC)
+                def red(name, bank_, c0, c1, j0, j1, stop=False, nl=w):
+                    mm(*[(A(bank_, c0 + k, c1, 16, p=nl), [(A(name, k, 16 * nl, 16), A("b8", j0, j1))]) for k in range(16)], start=False, stop=stop, one=True)
+                nr = sum(c for _, c, form in steps if form == "r")
+                if nr:
+                    red("dcb", "pd", w, 2 * w, 32, 40, nl=nr)
+                red("acb", "pd", w, 2 * w, 0, 8)
+                red("dab", "pk", 0, w, 8, 16)
+                red("rab", "pk", 0, 2 * w, 16, 32)
+                red("aac", "pd", 0, w, 0, 8, True)
+                ka, kc = A("pk", 0, w), A("pk", w, 2 * w)
+                act(A("tp"), A("pd", 0, w), ACT.Relu, bias=HH / 2, scale=-HH)
+                tt(A("col"), A("tp"), A("pd", w, 2 * w), ALU.is_lt)
+                mm((ka, [(A("id16k"), A("col"))]), (kc, [(A("idm"), A("col")), (A("idb"), A("tp"))]), start=False, one=True)
+                act(A("keys"), ka, ACT.Copy)
+                scan(A("scn"), A("seg"), A("keys"), ALU.mult, ALU.max)
+                tt(A("oht"), IND(A("scn"), A("cu")), A("keys"), ALU.is_equal)
+                p0 = 2 if fin else 0
+                mm(*[(A("pr0", j * w, j * w + w), [(A("oht"), A("idb"))]) for j in range(p0, 3)])
+                tt(A("prod", p0 * w, 3 * w), A("kf", p0 * w, 3 * w), A("pr0", p0 * w, 3 * w), ALU.mult)
+                mm((cn, [(A("col"), A("idb"))] + ([(A("idb"), A("off0"))] if fin else [])))
+                act(kk("prod", "x"), cn, ACT.Copy)
+                p1 = 4 if fin else 3
+                mm(*[(A("pr1", w + r, 3 * w, 16, p=8), [(A("prod", 2 * w + r, 3 * w, 16), A("bl16"))]) for r in range(16)])
+                act(A("lt", p=8), A("pr1", w, 3 * w, p=8), ACT.Copy)
+                mm((A("pr1", p0 * WC, p1 * WC), [(W(r), A("prod", p0 * w + r, p1 * w, 16)) for r in range(16)]))
+                cp(A("lst", p0 * WC, 3 * WC), A("pr1", p0 * WC, 3 * WC))
+                dd = A("pk", 2 * w, 4 * w)
+                mm((dd, [(A("lt", 64, 192, p=32), A("ee", p=32))]),
+                   *[(A("pk", (2 + q) * w, (3 + q) * w), [(A("bok"), kk("prod", "b"))]) for q in range(2)], one=True)
+                act(A("ad"), dd, ACT.Abs)
+                scan(A("nd"), A("rst"), A("ad"), ALU.max, ALU.min)
+                act(A("xz"), IND(xw, A("lst", 2 * WC, 3 * WC)), ACT.Copy)
+                mm(*[(A("pr0", h * w, h * w + w), [(A("db", 128 * h, 128 * h + 128), A(x)) for x in ("xz", yv)]) for h in range(2)])
+                act(A("hh"), A("pr0", 0, L), ACT.Identity, bias=191.75, scale=0.5)
                 if fin:
                     for q in range(2 if t < TV - 1 else 1):
-                        act(A("sm", WC * q, WC * q + WC), cl, ACT.Relu, bias=THETA / 2, scale=-0.5)
-                else:
-                    act(A("yw", 656, 664), cl, ACT.Relu, bias=-128.0 * BIG, scale=16.0)
-                tt(A("ne"), A("zx"), A("pr0", w, 3 * w), ALU.not_equal)
-                scan(A("nd"), A("rst"), A("ne"), ALU.max, ALU.min)
-                tt(A("zt"), A("nd", 31, 2 * w, 32), A("zx", 31, 2 * w, 32), ALU.mult)
-                act(A("xz"), IND(A("xb"), A("lst", lo, lo + WC)), ACT.Copy)
-                both("pr1", 0, w, [("db", ("xz",)), ("db", (yv,))])
-                act(A("hh"), A("pr1", 0, L), ACT.Identity, bias=191.75, scale=0.5)
-                mm(*[(A("pr0", 3 * w + 8 * q + 4 * h, 3 * w + 8 * q + 4 * h + 4), [(A("dk", 128 * h, 128 * h + 128), A("zt", 4 * q, 4 * q + 4))])
-                     for q in range(2) for h in range(2)])
-                for q in range(2):
-                    ts(A("idx", q, 16, 2), A("pr0", 3 * w + 8 * q, 3 * w + 8 * q + 8), (R_, R16)[q], ALU.max)
+                        act(A("sm", WC * q, WC * q + WC), A("pr1", 3 * WC, 4 * WC), ACT.Relu, bias=8.5 * 8192, scale=-8192.0)
+                for h in range(2):
+                    o = 400 + 8 * h
+                    mm((A("pr1", o, o + 8), [(A("lt", 128 * h, 128 * h + 128, p=32), A("i9", p=32))]),
+                       *[(A("pr1", o + q, o + 8, 2), [(A(("db4k", "ndb4k")[q], 128 * h, 128 * h + 128), A("nd", w * q + 31, w * q + w, 32))]) for q in range(2)], one=True)
+                ts(A("idx"), A("pr1", 400, 416), HI, ALU.min, R_, ALU.max)
                 if fin:
                     k = old["n"]
                     tt(A("sm", 16, 16 + k), old, A("sm", 0, k), ALU.add)
@@ -430,49 +445,42 @@ def build(g, T, topo, rank):
                         send(A("sa", 0, WC))
                 for c in range(WC - 1, -1, -1):
                     tt(IND(sw, A("idx", 2 * c, 2 * c + 2)), A("hh", 32 * c, 32 * c + 32), A("m192"), ALU.add)
-                dk = A("pk", 3 * w, 4 * w)
-                ts(A("rnd"), key, -49.0 / 128, ALU.add, 16200.0, ALU.max)
-                tt(A("nvc"), A("rnd"), key, ALU.is_lt)
-                tt(A("w12", 0, w), A("albe", 0, w), dk, ALU.mult)
-                tt(A("w12", w, 2 * w), A("nvc"), dk, ALU.mult)
-                terms = [("dk", ("kf", 2 * w, 3 * w)), ("dk", ("w12", 0, w)), ("dk128", ("w12", w, 2 * w))]
-                co, m0 = A("CO", m * L, (m + 1) * L), A("pk", 0, L)
-                both("pk", 0, w, terms + ([] if fin else [("dk4k", ("oh",))]))
+                mm((cn, [(A("bok"), kk("prod", "x"))]))
                 if not fin:
-                    tt(co, A("nid", t * L, t * L + L), m0, ALU.min)
-                    if t < TV - 1:
-                        cp(A("C", V + m * L, V + (m + 1) * L), co)
+                    act(A("off0"), cn, ACT.Relu, bias=-8.0)
                 else:
+                    yn = A("yn", t * w, t * w + w)
+                    act(cn, cn, ACT.Sign, A("thr", 2, 3) if t < TV - 1 else None, bias=-8.5)
+                    tt(A("ty"), A(yv), cn, ALU.mult)
+                    mm((cn, [(A("idh"), A("ty")), (A("idh"), A(yv)), (A("nidb"), A("nv", 2 * t * w, 2 * t * w + w))]))
+                    act(yn, cn, ACT.Abs)
                     if t < TV - 1:
-                        cp(A("C", V + m * L, V + (m + 1) * L), m0)
+                        send(yn)
+                ts(A("rnd"), kc, -29.0 / 128, ALU.add, 40000.0, ALU.min)
+                tt(A("sel"), A("rnd"), kc, ALU.is_gt)
+                tt(A("wv"), A("sel"), dk, ALU.mult)
+                if fin and t < TV - 1:
+                    mm((A("pd", 2 * w, 2 * w + 1), [(A("dsum"), A("thr", 2, 3))]))
+                    ts(A("thr", 1, 2), A("pd", 2 * w, 2 * w + 1), 128.0, ALU.add, A("thr", 0, 1), ALU.add)
+                    ts(A("thd"), A("nidk"), A("thr", 1, 2), ALU.mult)
+                co, m0 = A("CO", m * w, m * w + w), A("pr0", L, L + w)
+                mm((m0, [(A("wv"), A("idk")), (A("idk"), kk("kf", "b"))] + ([] if fin else [(A("oht"), A("id4k"))])))
+                if fin:
                     act(co, m0, ACT.Copy)
-                for h in range(2):
-                    dma("sp", T.co[64 * s:64 * s + 64, m * L + w * h:m * L + w * h + w], A("CO", m * L + w * h, m * L + w * h + w, h=h), 65536)
-                cnt = A("pa", 3 * w, 4 * w)
-                mm((cnt, [(A("bok"), PR("x"))] + ([(A("id4k"), A("off0"))] if fin else [])))
-                if not fin:
-                    act(A("off0"), cnt, ACT.Relu, bias=-512.0, scale=1.0 / 256)
-                    mm((cnt, [(A("idb"), A(yv)), (A("nidb"), X0)]))
-                    act(PP, cnt, ACT.Abs)
-                    mm((cnt, [(A("idb"), PP), (A("nidb"), X0)]))
-                    act(EE, cnt, ACT.Copy)
                 else:
-                    yn = "yn" if t == 0 else "ym"
-                    ts(OFF, cnt, THETA, ALU.is_ge)
-                    tt(WY, OFF, EE, ALU.mult)
-                    mm((cnt, [(A("idb"), WY), (A("idb"), X0)]))
-                    act(A(yn), cnt, ACT.Copy)
+                    tt(co, A("nid", t * w, t * w + w), m0, ALU.min)
+                if t < TV - 1:
+                    act(A("CI", m * w, m * w + w), co, ACT.Copy)
+                for h in range(2):
+                    dma("sp", T.co[rows, m * L + w * h:m * L + w * h + w], A("CO", m * w, m * w + w, h=h), 32768)
                     if t < TV - 1:
-                        send(A(yn))
-                        mm((cnt, [(A("db", 0, 128), OFF), (A("db", 128, 256), OFF)]))
-                        act(PP, cnt, ACT.Identity, A("thr", 2, 3))
-                        tt(A("thr", 1, 2), A("thr", 0, 1), A("thr", 2, 3), ALU.add)
-        rows = slice(64 * s, 64 * s + 64)
+                        for h2 in range(2):
+                            dma("sp", A("C", n + w * h, n + w * h + w, h=h2), A("CI", m * w, m * w + w, h=h), 32768)
         for h in range(2):
             q = ("sp", "act")[h]
             dma(q, T.xo[rows, 768 * h:768 * h + 768], A("X", TR + 768 * h, TR + 768 * h + 768, h=h), 196608)
             dma("sp", T.so[rows, WC * h:WC * h + WC], A("sm", 56, 64, h=h), 2048)
-            dma("sp", T.yo[rows, w * h:w * h + w], A("ym", h=h), 16384)
+            dma("sp", T.yo[rows, w * h:w * h + w], A("yn", w, 2 * w, h=h), 16384)
     return ops, ne_ * len(sends)
 
 

@@ -13,17 +13,18 @@ STEPS = {0: [(0, 32, "r"), (32, 32, "r"), (64, 32, "r"), (96, 32, "r")],
 EMODE = [[1, 1, 1, 1], [1, 1, 1, 1]]
 KS = [[0, 1, 1, 1], [1, 1, 1, 1]]
 LEAD = 9000.0
-TRIES, SEED = 512, 3050
+TRIES, SEED = 1500, 3050
+RED = 4
 BIG = 16384.0
 HH = 2.0 ** 17
 
 B, F, I32, U, K = "bfloat16", "float32", "int32", "uint16", "float16"
 PER_STREAM = {
     "X": (2 * TR + NX, B), "C": (NX, I32), "CO": (512, F), "CI": (256, I32), "y": (128, B), "sa": (16, U), "ra": (8, U), "la": (24, U),
-    "ry": (128, B), "yn": (256, B), "lst": (24, U), "k16": (384, U), "kf": (384, K), "nv": (512, B),
+    "ry": (128, B), "yn": (256, B), "lst": (24, U), "k16": (384, U), "kf": (768, K), "nv": (512, B),
     "xb": (2048, B), "xc": (2048, B), "dab": (2048, B), "dcb": (2048, B), "rab": (2048, B), "acb": (2048, B), "aac": (2048, B),
     "pqr": (384, B), "thd": (256, K), "keys": (128, F), "scn": (128, F), "bs": (768, B), "ks": (256, K),
-    "rnd": (128, I32), "prod": (512, K), "lt": (256, K), "ad": (256, B), "nd": (256, B),
+    "rnd": (128, I32), "prod": (512, K), "lt": (128, K), "ad": (256, B), "nd": (256, B),
     "idx": (16, U), "hh": (256, B), "sm": (128, F), "thr": (4, F),
 }
 PARTS = {n: ("bs", 128 * j) for j, n in enumerate(("tp", "col", "oht", "xz", "off0", "ty"))}
@@ -32,9 +33,9 @@ SHARED = {
     "l32": (56, I32), "lb": (16, U), "ab": (32, F), "rc": (16, U),
     "ones": (128, B), "onk": (128, K), "idb": (128, B), "nidb": (128, B), "bo0": (128, B), "bob": (128, B), "idk": (128, K), "nidk": (256, K),
     "id4k": (128, B), "id16k": (128, B), "idm": (128, B), "idh": (128, B), "bok": (128, K), "db": (256, B), "db4k": (256, B), "ndb4k": (256, B),
-    "dsum": (128, F), "wk": (144, K), "b8": (40, B), "bl16": (16, K), "tk": (256, B), "pi": (4, I32), "pc": (8, F), "seg": (128, F), "rst": (256, B),
-    "ee": (256, K), "i9": (8, K), "t1": (256, F), "t2": (256, F), "t3": (256, F), "t4": (16, F), "ci": (8, I32), "cu": (8, U),
-    "nid": (512, F), "nl": (64, F), "m192": (32, B),
+    "dsum": (128, F), "b8": (40, B), "tk": (256, B), "pi": (4, I32), "pc": (8, F), "seg": (128, B), "rst": (256, B),
+    "ee": (256, K), "i9": (16, K), "zero": (256, B), "t4": (16, F), "ci": (8, I32), "cu": (8, U),
+    "nid": (256, F), "nl": (64, F), "m192": (32, B),
 }
 SCRATCH = {n: ("sbuf", [128, c], d) for n, (c, d) in SHARED.items()}
 for s_ in range(2):
@@ -44,7 +45,9 @@ NDMA = 100
 MSG = (("rc", "arc"), ("ra_0", "ara0"), ("ry_0", "ary0"), ("ra_1", "ara1"), ("ry_1", "ary1"))
 SEMAPHORES = ["dve", "act", "pe", "pool", "sent"] + [m_[1] for m_ in MSG] + ["d%d" % i for i in range(NDMA)]
 G_, SC_, PE_, TT_ = 1.6, 4.0, 0.52, 2.0
-HOP, SAME = 110.0, 75.0
+HOP, SAME = 140.0, 90.0
+CASES = [(70.0, 40.0, {"dve": 0.85, "act": 0.9, "pe": 0.85}, 0.6), (240.0, 160.0, {"dve": 1.1, "act": 1.0, "pe": 1.15}, 1.3)]
+DMA0, DMAR = 1500.0, 200.0
 
 
 def way(T, topo, r):
@@ -82,7 +85,7 @@ def build(g, T, topo, rank):
         a0, b0, s0 = a or 0, n if b is None else b, s or 1
         cols = range(a0, b0, s0)
         bits = ((1 << (b0 - a0)) - 1) << a0 if s0 == 1 else sum(1 << c for c in cols)
-        p0, p1 = (0, p or 128) if h is None else (64 * h, 64 * h + 64)
+        p0, p1 = p if isinstance(p, tuple) else (0, p or 128) if h is None else (64 * h, 64 * h + 64)
         bits = bits | bits << n if p1 - p0 > 64 else bits << (n * (p0 // 64))
         ap = T[name][p0:p1, a0:b0] if s0 == 1 else T[name][p0:p1, a0:b0:s0]
         return {"name": name, "ap": ap, "n": len(cols), "acc": [(name, bits)], "ind": False}
@@ -200,7 +203,7 @@ def build(g, T, topo, rank):
         h = g.sync if q == "sp" else g.scalar
         rd = [in_] if isinstance(in_, dict) else []
         wr = [out] if isinstance(out, dict) else []
-        return op(q, lambda: h.dma_start(sc(out), sc(in_)), rd, wr, 70, 1800 + nbytes / 150.0, (s, 16))
+        return op(q, lambda: h.dma_start(sc(out), sc(in_)), rd, wr, 70, DMA0 + nbytes / DMAR, (s, 16))
 
     path = way(T, topo, rank)
     rid, pid = topo.addr(path[1], path[0])
@@ -219,14 +222,14 @@ def build(g, T, topo, rank):
         j = op("net", None, [], [A(land)], 0, 5000.0, (sem, na_))
         ops[j]["deps"][i] = "t"
 
-    SL = {"a": 0, "c": 1, "b": 2, "x": 3}
+    SL = {"x": -1, "b": 0, "a": 1, "c": 2}
     w = W_
     for s in range(2):
         now[0] = s
         rows = slice(64 * s, 64 * s + 64)
         for h in range(2):
             q = ("sp", "act")[h]
-            for j, x in ((2, T.sb), (1, T.ic), (0, T.ia)):
+            for j, x in ((0, T.sb), (2, T.ic), (1, T.ia)):
                 dma(q, A("l32", 24 * s + WC * j, 24 * s + WC * j + WC, h=h), x[rows, WC * h:WC * h + WC], 2048)
             dma(q, A("C", 0, V, h=h), T.ch[rows, :], 524288 + 786432 * s)
             dma(q, A("X", TR, TR + V, h=h), T.x[rows, :], 786432 * (s + 1))
@@ -246,13 +249,22 @@ def build(g, T, topo, rank):
     ms(A("ones"), 1.0)
     cp(A("onk"), A("ones"))
     ms(A("m192"), -192.0)
-    asel(A("idb"), A("ones"), [[-1, 128]], ALU.is_equal, 0.0, 0, 1)
+    ms(A("zero"), 0.0)
+
+    def spots(out, x, pat, base=0, cm=1, **kw):
+        asel(out, A("zero", 0, out["n"], **kw), pat, ALU.not_equal, x, base, cm)
+    for name, x in (("idb", 1.0), ("nidb", -1.0), ("idk", 1.0), ("id4k", 4096.0), ("id16k", BIG), ("idm", 49.0 / 128), ("idh", 0.5)):
+        spots(A(name), x, [[-1, 128]])
+    spots(A("tk", 128, 256), 32768.0, [[-1, 128]])
+    spots(A("nidk"), -1.0, [[0, 2], [-1, 128]])
     asel(A("bo0"), A("ones"), [[-16, 8], [0, 16]], ALU.is_ge, 0.0, 0, 1)
     asel(A("bob"), A("bo0"), [[16, 8], [0, 16]], ALU.is_ge, 0.0, 15, -1)
-    for h in range(2):
-        ms(A("db", 128 * h, 128 * h + 128, h=1 - h), 0.0)
-        for q in range(2):
-            cp(A("db", 128 * h + 64 * q, 128 * h + 64 * q + 64, h=h), A("idb", 64 * h, 64 * h + 64, h=h))
+    for name, x in (("db", 1.0), ("db4k", 4096.0), ("ndb4k", -4096.0)):
+        spots(A(name), x, [[-64, 2], [0, 2], [-1, 64]])
+    spots(A("dsum"), 0.5, [[0, 2], [-1, 64]])
+    asel(A("dsum"), A("dsum"), [[0, 2], [-1, 64]], ALU.not_equal, 0.5, -64, 1)
+    for h in (1, 0):
+        iota(A("nid", p=64 + 64 * h), [[512, 2], [1, 128]], V + L + w * h, 0)
     iota(A("pi", 0, 1), [[0, 1]], 0, 1)
     ts(A("pi", 1, 2), A("pi", 0, 1), 15, ALU.bitwise_and)
     ts(A("pi", 2, 3), A("pi", 0, 1), 64, ALU.bitwise_and)
@@ -260,62 +272,29 @@ def build(g, T, topo, rank):
     ts(A("pc", 2, 3), A("pc", 0, 1), -1.0, ALU.mult, 15.0, ALU.add)
     ts(A("pc", 3, 4), A("pc", 0, 1), float(TR + NX), ALU.add)
     ts(A("pc", 4, 5), A("pc", 1, 2), 2.0, ALU.mult, A("pc", 0, 1), ALU.add)
-    ts(A("pc", 5, 6), A("pi", 0, 1), 16.0, ALU.is_ge, 4096.0, ALU.mult)
-    ts(A("pc", 6, 7), A("pi", 0, 1), 8.0, ALU.is_equal)
-    ts(A("pc", 7, 8), A("pc", 1, 2), 2.0, ALU.mult)
-    R_, R15, HI, HR, S16, S8, H128 = [A("pc", j, j + 1) for j in (0, 2, 3, 4, 5, 6, 7)]
-    for name, x in (("nidb", -1.0), ("idk", 1.0), ("id4k", 4096.0), ("id16k", BIG), ("idm", -9.0 / 64), ("idh", 0.5)):
-        act(A(name), A("idb"), ACT.Copy, scale=x)
-    for q in range(2):
-        act(A("nidk", 128 * q, 128 * q + 128), A("idb"), ACT.Copy, scale=-1.0)
+    R_, R15, HI, HR = [A("pc", j, j + 1) for j in (0, 2, 3, 4)]
     ts(A("tk", 0, 128), A("idb"), R15, ALU.mult)
-    act(A("tk", 128, 256), A("idb"), ACT.Copy, scale=-1.0 / 64)
-    for name, x in (("db4k", 4096.0), ("ndb4k", -4096.0)):
-        act(A(name), A("db"), ACT.Copy, scale=x)
-    for h in range(2):
-        for q in range(2):
-            act(A("dsum", 64 * q, 64 * q + 64, h=h), A("idb", 64 * h, 64 * h + 64, h=h), ACT.Copy, scale=0.5)
     act(A("bok"), A("bob"), ACT.Copy)
-    for j, x in enumerate((1.0, -16.0, 32.0, 32.0, -1.0)):
-        ts(A("b8", 8 * j, 8 * j + 8), A("bob", 0, 128, 16), x, ALU.mult)
-    for j in range(4):
-        cp(A("bl16", 4 * j, 4 * j + 4), A("bob", 64 * (j // 2), 64 * (j // 2) + 64, 16))
-    ms(A("bo0"), 0.0)
-    cp(A("wk", 0, 128), A("bo0"))
-    cp(A("wk", 128, 144), A("bo0", 0, 16))
-    cp(A("wk", 15, 143, 16), A("bob", 0, 128, 16))
-
-    def W(k):
-        return A("wk", 15 - k, 143 - k)
-    ms(A("seg"), 1.0)
-    ms(A("seg", 0, 128, 16), 0.0)
-    ms(A("rst"), 0.0)
-    ms(A("rst", 0, 256, 32), 1.0)
-    iota(A("t1"), [[-16, 2], [0, 4], [1, 32]], 16, -1)
-    iota(A("t2"), [[1, 2], [2, 4], [0, 32]], 0, -1)
-    ts(A("t1"), A("t1"), 0.0, ALU.is_ge, S16, ALU.mult)
-    ts(A("t2"), A("t2"), 0.0, ALU.is_equal, -1.0, ALU.mult)
-    tt(A("ee"), A("t1"), A("t2"), ALU.add)
-    iota(A("t3"), [[0, 16], [1, 16]], 16, -1)
-    iota(A("t4", 0, 8), [[1, 8]], 0, -1)
-    iota(A("t4", 8, 16), [[0, 4], [8192, 2]], TR - 4096, 0)
-    ts(A("t4", 0, 8), A("t4", 0, 8), 0.0, ALU.is_equal)
-    ts(A("t4", 8, 16), A("t4", 8, 16), S8, ALU.mult)
-    tt(A("i9"), A("t4", 0, 8), A("t4", 8, 16), ALU.add)
+    for j, x in enumerate((1.0, -16.0, 32.0, -32.0, -1.0)):
+        act(A("b8", 8 * j, 8 * j + 8), A("bob", 0, 128, 16), ACT.Copy, scale=x)
+    asel(A("seg"), A("ones"), [[0, 8], [1, 16]], ALU.not_equal, 0.0, 0, 0)
+    spots(A("rst"), 1.0, [[0, 8], [1, 32]], cm=0)
+    asel(A("ee", p=64), A("zero", p=64), [[16, 2], [0, 4], [-1, 32]], ALU.is_gt, 4096.0, -32, 1)
+    spots(A("ee", p=32), -1.0, [[1, 2], [2, 4], [0, 32]], WC, -1, p=32)
+    iota(A("t4"), [[0, 8], [8192, 2]], TR - 4096, 0)
+    act(A("i9"), A("t4"), ACT.Copy, scale=1.0 / 32)
     iota(A("ci"), [[16, 8]], 15, 0)
     cp(A("cu"), A("ci"))
-    iota(A("nid", 256, 512), [[512, 2], [1, 128]], V + L, 0)
-    ts(A("nid", 0, 256), A("nid", 256, 512), H128, ALU.add)
     iota(A("nl", 32, 64), [[512, 2], [0, 2], [16, WC]], V, 0)
     ts(A("nl", 0, 32), A("nl", 32, 64), HR, ALU.add)
     for s in range(2):
         now[0] = s
         o = 24 * s
         cp(A("la"), A("l32", o, o + 24))
-        cp(A("lb", WC * s, WC * s + WC), A("l32", o + 16, o + 24))
-        cp(A("ab", 16 * s, 16 * s + WC), A("l32", o, o + WC))
-        cp(A("ab", 16 * s + WC, 16 * s + 16), A("l32", o + 16, o + 24))
-        ts(A("lt"), A("t3"), 0.0, ALU.is_equal, S8, ALU.add)
+        cp(A("lb", WC * s, WC * s + WC), A("l32", o, o + WC))
+        act(A("ab", 16 * s, 16 * s + WC), A("l32", o + WC, o + 16), ACT.Copy)
+        act(A("ab", 16 * s + WC, 16 * s + 16), A("l32", o, o + WC), ACT.Copy)
+        spots(A("lt", p=64), 1.0, [[0, 8], [1, 16]], 32, -1, p=64)
         cp(A("thr", 0, 1), A("l32", 48 + 4 * s, 49 + 4 * s))
         ts(A("thd"), A("nidk"), A("thr", 0, 1), ALU.mult)
     now[0] = None
@@ -336,23 +315,26 @@ def build(g, T, topo, rank):
                 n = V + m * L
                 cw = A("C", 0, V + (0 if t == 0 else 256 * (lev + 1)))
 
+                f0 = 3 * w * (m % 2)
+
                 def kk(name, x, a=0, b=w):
-                    return A(name, SL[x] * w + a, SL[x] * w + b)
+                    o = SL[x] * w + {"kf": f0, "prod": w}.get(name, 0)
+                    return A(name, o + a, o + b)
                 if m == 2:
-                    parts = [(A("sa", WC, 2 * WC), 2, 3), (A("rc", WC * s, WC * s + WC), 1, 2), (A("ra"), 0, 1)]
+                    parts = [(A("sa", WC, 2 * WC), 0, 1), (A("rc", WC * s, WC * s + WC), 2, 3), (A("ra"), 1, 2)]
                 else:
                     parts = [(A("la" if m == 0 else "lst"), 0, 3)]
                 for lists, a, b in parts:
                     if KS[s][m]:
-                        act(A("kf", a * w, b * w), IND(cw, lists), ACT.Copy)
-                        cp(A("k16", a * w, b * w), A("kf", a * w, b * w))
+                        act(A("kf", f0 + a * w, f0 + b * w), IND(cw, lists), ACT.Copy)
+                        cp(A("k16", a * w, b * w), A("kf", f0 + a * w, f0 + b * w))
                     else:
                         cp(A("k16", a * w, b * w), IND(cw, lists))
-                        cp(A("kf", a * w, b * w), A("k16", a * w, b * w))
+                        cp(A("kf", f0 + a * w, f0 + b * w), A("k16", a * w, b * w))
                 for lists, a, b in parts:
                     act(A("pqr", a * w, b * w), IND(xw, lists), ACT.Copy)
-                mm((A("pr0", L, L + w), [(A("idb"), kk("pqr", "a")), (A("idb"), kk("pqr", "b")), (A("nidb"), kk("pqr", "c"))]))
-                ts(A("nv", m * w, m * w + w), A("pr0", L, L + w), 0.0, ALU.max, 63.0, ALU.min)
+                mm((A("pk", 0, w), [(A("idb"), kk("pqr", "a")), (A("idb"), kk("pqr", "b")), (A("nidb"), kk("pqr", "c"))]))
+                ts(A("nv", m * w, m * w + w), A("pk", 0, w), 0.0, ALU.max, 63.0, ALU.min)
                 for h in range(2):
                     own = A("nv", m * w, m * w + w, h=h)
                     if t < TV - 1:
@@ -395,7 +377,9 @@ def build(g, T, topo, rank):
                         act(A("aac", u, u + 512), rb, ACT.Abs)
 
                 def red(name, bank_, c0, c1, j0, j1, stop=False, nl=w):
-                    mm(*[(A(bank_, c0 + k, c1, 16, p=nl), [(A(name, k, 16 * nl, 16), A("b8", j0, j1))]) for k in range(16)], start=False, stop=stop, one=True)
+                    for k0 in range(0, 16, RED):
+                        mm(*[(A(bank_, c0 + k, c1, 16, p=nl), [(A(name, k, 16 * nl, 16), A("b8", j0, j1))]) for k in range(k0, k0 + RED)],
+                           start=False, stop=stop and k0 + RED == 16, one=True)
                 nr = sum(c for _, c, form in steps if form == "r")
                 if nr:
                     red("dcb", "pd", w, 2 * w, 32, 40, nl=nr)
@@ -406,36 +390,38 @@ def build(g, T, topo, rank):
                 ka, kc = A("pk", 0, w), A("pk", w, 2 * w)
                 act(A("tp"), A("pd", 0, w), ACT.Relu, bias=HH / 2, scale=-HH)
                 tt(A("col"), A("tp"), A("pd", w, 2 * w), ALU.is_lt)
-                mm((ka, [(A("id16k"), A("col"))]), (kc, [(A("idm"), A("col")), (A("idb"), A("tp"))]), start=False, one=True)
+                mm((ka, [(A("id16k"), A("col"))]), (kc, [(A("idm"), A("col")), (A("nidb"), A("tp"))]), start=False, one=True)
                 act(A("keys"), ka, ACT.Copy)
                 scan(A("scn"), A("seg"), A("keys"), ALU.mult, ALU.max)
                 tt(A("oht"), IND(A("scn"), A("cu")), A("keys"), ALU.is_equal)
-                p0 = 2 if fin else 0
-                mm(*[(A("pr0", j * w, j * w + w), [(A("oht"), A("idb"))]) for j in range(p0, 3)])
-                tt(A("prod", p0 * w, 3 * w), A("kf", p0 * w, 3 * w), A("pr0", p0 * w, 3 * w), ALU.mult)
+                ns = 1 if fin else 3
+                mm(*[(A("pr0", j * w, j * w + w), [(A("oht"), A("idb"))]) for j in range(ns)])
+                tt(A("prod", w, w + ns * w), A("kf", f0, f0 + ns * w), A("pr0", 0, ns * w), ALU.mult)
                 mm((cn, [(A("col"), A("idb"))] + ([(A("idb"), A("off0"))] if fin else [])))
                 act(kk("prod", "x"), cn, ACT.Copy)
-                p1 = 4 if fin else 3
-                mm(*[(A("pr1", w + r, 3 * w, 16, p=8), [(A("prod", 2 * w + r, 3 * w, 16), A("bl16"))]) for r in range(16)])
-                act(A("lt", p=8), A("pr1", w, 3 * w, p=8), ACT.Copy)
-                mm((A("pr1", p0 * WC, p1 * WC), [(W(r), A("prod", p0 * w + r, p1 * w, 16)) for r in range(16)]))
-                cp(A("lst", p0 * WC, 3 * WC), A("pr1", p0 * WC, 3 * WC))
+                nr = WC * (ns + 1)
+                mm(*[(A("pr1", r, w, 16, p=nr), [(A("prod", r, w + ns * w, 16), A("bok", 0, w, 16))]) for r in range(16)])
+                act(A("lt", p=nr), A("pr1", 0, w, p=nr), ACT.Copy)
+                mm((A("pr1", w, w + nr), [(A("lt", p=32), A("idk", 0, nr, p=32))]))
+                cp(A("lst", 0, ns * WC), A("pr1", w + WC, w + nr))
                 dd = A("pk", 2 * w, 4 * w)
-                mm((dd, [(A("lt", 64, 192, p=32), A("ee", p=32))]),
+                mm((dd, [(A("lt", p=64), A("ee", p=64))]),
                    *[(A("pk", (2 + q) * w, (3 + q) * w), [(A("bok"), kk("prod", "b"))]) for q in range(2)], one=True)
                 act(A("ad"), dd, ACT.Abs)
                 scan(A("nd"), A("rst"), A("ad"), ALU.max, ALU.min)
-                act(A("xz"), IND(xw, A("lst", 2 * WC, 3 * WC)), ACT.Copy)
+                act(A("xz"), IND(xw, A("lst", 0, WC)), ACT.Copy)
                 mm(*[(A("pr0", h * w, h * w + w), [(A("db", 128 * h, 128 * h + 128), A(x)) for x in ("xz", yv)]) for h in range(2)])
                 act(A("hh"), A("pr0", 0, L), ACT.Identity, bias=191.75, scale=0.5)
                 if fin:
                     for q in range(2 if t < TV - 1 else 1):
-                        act(A("sm", WC * q, WC * q + WC), A("pr1", 3 * WC, 4 * WC), ACT.Relu, bias=8.5 * 8192, scale=-8192.0)
-                for h in range(2):
-                    o = 400 + 8 * h
-                    mm((A("pr1", o, o + 8), [(A("lt", 128 * h, 128 * h + 128, p=32), A("i9", p=32))]),
-                       *[(A("pr1", o + q, o + 8, 2), [(A(("db4k", "ndb4k")[q], 128 * h, 128 * h + 128), A("nd", w * q + 31, w * q + w, 32))]) for q in range(2)], one=True)
-                ts(A("idx"), A("pr1", 400, 416), HI, ALU.min, R_, ALU.max)
+                        act(A("sm", WC * q, WC * q + WC), A("pr1", w, w + WC), ACT.Relu, bias=8.5 * 8192, scale=-8192.0)
+                o = 400
+                mm((A("pr1", o, o + 16), [(A("onk", p=32), A("i9", p=32))]),
+                   *[(A("pr1", o + 8 * h, o + 8 * h + 8, h=h2), [(A("lt", 64 * h, 64 * h + 64, p=32), A("idk", WC, 2 * WC, p=32))]) for h in range(2) for h2 in range(2)],
+                   stop=False, one=True)
+                mm(*[(A("pr1", o + 8 * h + q, o + 8 * h + 8, 2), [(A(("db4k", "ndb4k")[q], 128 * h, 128 * h + 128), A("nd", w * q + 31, w * q + w, 32))])
+                     for h in range(2) for q in range(2)], start=False, one=True)
+                ts(A("idx"), A("pr1", o, o + 16), HI, ALU.min, R_, ALU.max)
                 if fin:
                     k = old["n"]
                     tt(A("sm", 16, 16 + k), old, A("sm", 0, k), ALU.add)
@@ -456,14 +442,14 @@ def build(g, T, topo, rank):
                     act(yn, cn, ACT.Abs)
                     if t < TV - 1:
                         send(yn)
-                ts(A("rnd"), kc, -29.0 / 128, ALU.add, 40000.0, ALU.min)
-                tt(A("sel"), A("rnd"), kc, ALU.is_gt)
+                act(A("rnd"), kc, ACT.Relu)
+                tt(A("sel"), A("rnd"), kc, ALU.is_le)
                 tt(A("wv"), A("sel"), dk, ALU.mult)
                 if fin and t < TV - 1:
                     mm((A("pd", 2 * w, 2 * w + 1), [(A("dsum"), A("thr", 2, 3))]))
                     ts(A("thr", 1, 2), A("pd", 2 * w, 2 * w + 1), 128.0, ALU.add, A("thr", 0, 1), ALU.add)
                     ts(A("thd"), A("nidk"), A("thr", 1, 2), ALU.mult)
-                co, m0 = A("CO", m * w, m * w + w), A("pr0", L, L + w)
+                co, m0 = A("CO", m * w, m * w + w), A("pk", 0, w)
                 mm((m0, [(A("wv"), A("idk")), (A("idk"), kk("kf", "b"))] + ([] if fin else [(A("oht"), A("id4k"))])))
                 if fin:
                     act(co, m0, ACT.Copy)
@@ -529,7 +515,7 @@ def plan(ops):
     for i in range(n - 1, -1, -1):
         base[i] = ops[i]["busy"] + max([base[u] + d for u, d in fw[i]] + [ops[i]["lat"]])
     rng = np.random.default_rng(SEED)
-    best = r = None
+    best = r = score = None
     for k in range(TRIES):
         look = float(rng.choice([40.0, 150.0, 300.0]))
         if k % 8 == 0 and k < TRIES // 2:
@@ -540,9 +526,25 @@ def plan(ops):
             z = rng.uniform(0, float(rng.choice([0.0, 100.0, 400.0])), n)
             prio = sweep(ops, fw, bw, [src[2][i] + float(z[i]) for i in range(n)], look, True)[2]
         r = sweep(ops, bw, fw, prio, look, False)
-        if best is None or max(r[2]) <= max(best[2]):
-            best = r
+        if best is None or max(r[2]) <= score[0] + 3000:
+            now = max(r[2]) + sum(replay(ops, r[0], *c) for c in CASES)
+            if best is None or now <= score[1]:
+                best, score = r, (max(r[2]), now)
     return best
+
+
+def replay(ops, order, hop, same, speed, lat):
+    free, end, fin = {}, [0.0] * len(ops), 0.0
+    for i in order:
+        o = ops[i]
+        t = free.get(o["eng"], 0.0)
+        for j, k in o["deps"].items():
+            d = end[j] + (0.0 if k == "o" else ops[j]["lat"] * lat + (0.0 if k == "t" else same if o["eng"] == ops[j]["eng"] else hop))
+            if d > t:
+                t = d
+        free[o["eng"]] = end[i] = t + o["busy"] * speed.get(o["eng"], 1.0)
+        fin = max(fin, end[i] + o["lat"] * lat)
+    return fin
 
 
 def emit(g, T, ops, order, nsent):

@@ -1,19 +1,44 @@
 import numpy as np
+from concourse.bass import DstId, RemoteDMATransfer
 from concourse.mybir import dt, AluOpType, AxisListType, ActivationFunctionType
 
 ALU = AluOpType
 ACT = ActivationFunctionType
 V, L, TV, LV, H = 1024, 256, 2, 2, 3
 W_, WC = 128, 8
-TR = 16
+BL = 64
+SECT = [(q, sum(16 * (u + 1) * W_ // BL for u in range(q + 1, BL // 16)), 16 * (q + 1)) for q in range(BL // 16 - 1, -1, -1)]
+ND = SECT[-1][1] + 16 * W_ // BL
+TR = BL // 2
 NX = V + 512
 STEPS = {0: [(0, 32, "r"), (32, 32, "r"), (64, 32, "r"), (96, 32, "r")],
          1: [(0, 32, "r"), (96, 32, "e"), (32, 32, "r"), (64, 32, "r")],
-         2: [(0, 32, "r"), (96, 32, "e"), (64, 32, "e"), (32, 32, "r")]}
-EMODE = [[1, 1, 1, 1], [1, 1, 1, 1]]
+         2: [(0, 32, "r"), (96, 32, "e"), (64, 32, "e"), (32, 32, "r")],
+         3: [(0, 32, "df"), (32, 32, "df"), (64, 32, "df"), (96, 32, "r")],
+         4: [(0, 32, "df"), (32, 32, "df"), (64, 32, "rf"), (96, 32, "r")],
+         5: [(0, 32, "d1"), (32, 32, "d1"), (64, 32, "r"), (96, 32, "r")],
+         6: [(0, 32, "rf"), (32, 32, "rf"), (96, 32, "e"), (64, 32, "e")],
+         7: [(0, 32, "df"), (32, 32, "df"), (64, 32, "r"), (96, 32, "r")]}
+STEPS[8] = [(0, 32, "r"), (32, 32, "r"), (64, 32, "n"), (96, 32, "e")]
+WORK = {e: [(x[0], int(x[1])) for x in "b0 c0 a0 b3 c3 a3 b1 c1 a1 b2 c2 a2".split()] for e in STEPS}
+STEPS[9] = [(0, 32, "rf"), (32, 32, "df"), (64, 32, "df"), (96, 32, "n")]
+WORK[9] = [(x[0], int(x[1])) for x in "b0 c0 b1 c1 b2 c2 a0 a1 a2 b3 c3 a3".split()]
+STEPS[10] = STEPS[8]
+WORK[10] = [(x[0], int(x[1])) for x in "b0 c0 a0 b3 a3 c3 b1 a1 c1 b2 a2 c2".split()]
+CHAIN = []
+FIRST, END = [16], []
+LAST = ""
+ADD0, ADD1, ADDR = 700.0, 1200.0, 1.2
+FOLD0, FOLDR = 2800.0, 1.5
+EMODE = [[10, 10, 10, 10], [10, 10, 10, 10]]
 KS = [[0, 1, 1, 1], [1, 1, 1, 1]]
-LEAD = 9000.0
-TRIES, SEED = 1500, 3050
+LEAD = 10000.0
+TRIES, SEED = 3500, 3050
+KEEP = 6
+NET = 4000.0
+STEP, CUM, PAIR = False, False, True
+LOOK = [40.0, 150.0, 300.0, 450.0]
+SUBA, SUBV = 32, 32
 RED = 4
 BIG = 16384.0
 HH = 2.0 ** 17
@@ -23,31 +48,33 @@ PER_STREAM = {
     "X": (2 * TR + NX, B), "C": (NX, I32), "CO": (512, F), "CI": (256, I32), "y": (128, B), "sa": (16, U), "ra": (8, U), "la": (24, U),
     "ry": (128, B), "yn": (256, B), "lst": (24, U), "k16": (384, U), "kf": (768, K), "nv": (512, B),
     "xb": (2048, B), "xc": (2048, B), "dab": (2048, B), "dcb": (2048, B), "rab": (2048, B), "acb": (2048, B), "aac": (2048, B),
-    "pqr": (384, B), "thd": (256, K), "keys": (128, F), "scn": (128, F), "bs": (768, B), "ks": (256, K),
-    "rnd": (128, I32), "prod": (512, K), "lt": (128, K), "ad": (256, B), "nd": (256, B),
+    "pqr": (384, B), "thd": (256, K), "keys": (128, F), "scn": (128, F), "bs": (896, B), "st": (130, B), "ks": (256, K),
+    "rnd": (128, I32), "prod": (512, K), "lt": (128, K), "ad": (ND, B), "nd": (ND, B),
     "idx": (16, U), "hh": (256, B), "sm": (128, F), "thr": (4, F),
 }
-PARTS = {n: ("bs", 128 * j) for j, n in enumerate(("tp", "col", "oht", "xz", "off0", "ty"))}
+PARTS = {n: ("bs", 128 * j) for j, n in enumerate(("tp", "col", "oht", "xz", "off0", "ty", "cum"))}
 PARTS.update({n: ("ks", 128 * j) for j, n in enumerate(("sel", "wv"))})
 SHARED = {
     "l32": (56, I32), "lb": (16, U), "ab": (32, F), "rc": (16, U),
     "ones": (128, B), "onk": (128, K), "idb": (128, B), "nidb": (128, B), "bo0": (128, B), "bob": (128, B), "idk": (128, K), "nidk": (256, K),
     "id4k": (128, B), "id16k": (128, B), "idm": (128, B), "idh": (128, B), "bok": (128, K), "db": (256, B), "db4k": (256, B), "ndb4k": (256, B),
-    "dsum": (128, F), "b8": (40, B), "tk": (256, B), "pi": (4, I32), "pc": (8, F), "seg": (128, B), "rst": (256, B),
-    "ee": (256, K), "i9": (16, K), "zero": (256, B), "t4": (16, F), "ci": (8, I32), "cu": (8, U),
-    "nid": (256, F), "nl": (64, F), "m192": (32, B),
+    "dsum": (128, F), "b8": (56, B), "tk": (256, B), "pi": (4, I32), "pc": (8, F), "seg": (128, B), "rst": (ND, B),
+    "ee": (ND, K), "tri": (ND, K), "r16": (128, K), "i9": (16, K), "i8": (16, K), "nid4k": (128, B), "e0": (128, B), "c4k": (128, B), "id16": (128, B), "zero": (256, B), "t4": (16, F), "ci": (8, I32), "cu": (8, U),
+    "nid": (256, F), "nl": (64, F), "m192": (BL, B),
 }
 SCRATCH = {n: ("sbuf", [128, c], d) for n, (c, d) in SHARED.items()}
 for s_ in range(2):
     SCRATCH.update({"%s_%d" % (n, s_): ("sbuf", [128, c], d) for n, (c, d) in PER_STREAM.items()})
     SCRATCH.update({"%s_%d" % (n, s_): ("psum", [128, 512], F) for n in ("pd", "pk", "pr0", "pr1")})
-NDMA = 100
+NDMA = 96
 MSG = (("rc", "arc"), ("ra_0", "ara0"), ("ry_0", "ary0"), ("ra_1", "ara1"), ("ry_1", "ary1"))
-SEMAPHORES = ["dve", "act", "pe", "pool", "sent"] + [m_[1] for m_ in MSG] + ["d%d" % i for i in range(NDMA)]
-G_, SC_, PE_, TT_ = 1.6, 4.0, 0.52, 2.0
-HOP, SAME = 140.0, 90.0
-CASES = [(70.0, 40.0, {"dve": 0.85, "act": 0.9, "pe": 0.85}, 0.6), (240.0, 160.0, {"dve": 1.1, "act": 1.0, "pe": 1.15}, 1.3)]
-DMA0, DMAR = 1500.0, 200.0
+SEMAPHORES = ["dve", "act", "pe", "pool", "sent"] + [m_[1] for m_ in MSG] + ["d%d" % i for i in range(NDMA)] + [
+    "%s%d_%d" % (n, s_, c) for n in ("ad", "fo") for s_ in range(2) for c in range(4)]
+G_, SC_, PE_, TT_ = 1.56, 3.8, 0.5, 2.0
+V0, V1, S0, P0 = 60.0, 60.0, 78.0, 18.0
+HOP, SAME = 150.0, 100.0
+CASES = [(90.0, 60.0, 1.15, 2.2, 12.0, 0.7), (100.0, 70.0, 2.0, 5.2, 18.0, 0.8), (260.0, 170.0, 1.56, 3.8, 28.0, 1.6), (200.0, 130.0, 1.25, 5.0, 12.0, 1.2)]
+DMA0, DMA1, DMAR = 800.0, 1500.0, 350.0
 
 
 def way(T, topo, r):
@@ -59,9 +86,15 @@ def way(T, topo, r):
     return [src, (near or can)[0], dst]
 
 
-def emask(topo, a, b):
-    e = topo.engines(a, b)[:8]
+def emask(topo, a, b, most=8):
+    e = topo.engines(a, b)[:most]
     return sum(1 << k for k in e), len(e)
+
+
+def mates_of(T, topo, r):
+    src = T.cores[r]
+    busy = list(T.cores) + way(T, topo, r)
+    return [c for c in topo.cores_of(src) if c not in busy and topo.die(c) == topo.die(src)][:2]
 
 
 def wide(a):
@@ -130,19 +163,20 @@ def build(g, T, topo, rank):
                         dep(st[3])
                     st[3] = i
         ops.append({"eng": eng, "fn": fn, "deps": deps, "busy": busy, "lat": lat, "sem": sem, "s": now[0],
-                    "out": writes[0]["name"] if writes else ""})
+                    "out": writes[0]["name"] if writes else "", "mm": len(reads) // 2 if eng == "pe" else 0,
+                    "ge": sum(a["n"] for a in reads if isinstance(a, dict) and a["ind"]), "se": sum(a["n"] for a in writes if a["ind"])})
         return i
 
     def vcost(out, ins, two=False):
         n = out["n"]
         if out["ind"]:
-            return 50 + n * SC_
+            return V0 + n * SC_
         if ins[0]["ind"]:
-            return 50 + n * G_
+            return V0 + n * G_
         if two:
             ps = any(SCRATCH[a["name"]][0] == "psum" for a in ins)
-            return 30 + max(64, n * (1 if ps else TT_))
-        return 30 + max(64, n * (1 if any(wide(a) for a in [out] + ins) else 0.5))
+            return V1 + max(64, n * (1 if ps else TT_))
+        return V1 + max(64, n * (1 if any(wide(a) for a in [out] + ins) else 0.5))
 
     def sc(x):
         return x["ap"] if isinstance(x, dict) else x
@@ -164,14 +198,14 @@ def build(g, T, topo, rank):
         return op("dve", lambda: g.vector.tensor_tensor_scan(out["ap"], d0["ap"], d1["ap"], 0.0, o0, o1), [d0, d1], [out], vcost(out, [d0, d1]))
 
     def ms(out, v):
-        return op("dve", lambda: g.vector.memset(out["ap"], v), [], [out], 30 + max(64, out["n"] * 0.5))
+        return op("dve", lambda: g.vector.memset(out["ap"], v), [], [out], V1 + max(64, out["n"] * 0.5))
 
     def act(out, a, f, acc=None, bias=0.0, scale=1.0):
         if acc is None:
             fn = lambda: g.scalar.activation(out["ap"], a["ap"], f, sc(bias), scale)
         else:
             fn = lambda: g.scalar.activation(out["ap"], a["ap"], f, sc(bias), scale, accum_out=acc["ap"])
-        return op("act", fn, [a, bias], [out] + ([acc] if acc else []), 65 + max(64, out["n"] * (G_ if a["ind"] else 1)) + (140 if acc else 0))
+        return op("act", fn, [a, bias], [out] + ([acc] if acc else []), S0 + max(64, out["n"] * (G_ if a["ind"] else 1)) + (140 if acc else 0))
 
     def mm(*groups, start=True, stop=True, one=False):
         out = groups[0][0]
@@ -185,7 +219,7 @@ def build(g, T, topo, rank):
                     r = g.tensor.matmul(o["ap"], w["ap"], x["ap"], start and first, stop and final)
             return r
         return op("pe", fn, [a for o, terms in groups for t_ in terms for a in t_], [o for o, terms in groups],
-                  sum(12 + PE_ * max(min(64, w["n"]), x["n"]) * (4 if wide(x) else 1) for o, terms in groups for w, x in terms))
+                  sum(P0 + PE_ * max(min(64, w["n"]), x["n"]) * (4 if wide(x) else 1) for o, terms in groups for w, x in terms))
 
     def iota(out, pat, base, cm):
         if SCRATCH[out["name"]][2] == I32:
@@ -203,7 +237,7 @@ def build(g, T, topo, rank):
         h = g.sync if q == "sp" else g.scalar
         rd = [in_] if isinstance(in_, dict) else []
         wr = [out] if isinstance(out, dict) else []
-        return op(q, lambda: h.dma_start(sc(out), sc(in_)), rd, wr, 70, DMA0 + nbytes / DMAR, (s, 16))
+        return op(q, lambda: h.dma_start(sc(out), sc(in_)), rd, wr, 70, (DMA1 if rd and wr else DMA0) + nbytes / DMAR, (s, 16))
 
     path = way(T, topo, rank)
     rid, pid = topo.addr(path[1], path[0])
@@ -219,8 +253,29 @@ def build(g, T, topo, rank):
         if sends:
             ops[i]["deps"].setdefault(sends[-1], "o")
         sends.append(i)
-        j = op("net", None, [], [A(land)], 0, 5000.0, (sem, na_))
+        j = op("net", None, [], [A(land)], 0, NET, (sem, na_))
         ops[j]["deps"][i] = "t"
+
+    uses, loads = {}, {}
+
+    def add(out, in_, s):
+        uses[s] = uses.get(s, 0) + 16
+        return op("pool", lambda: g.dma_start(out["ap"], in_["ap"], accum_op=ALU.add), [in_, out], [out], ADD0, ADD1 + out["n"] * ADDR, (s, uses[s]))
+
+    def fold(out, x, y, s):
+        mate = mates_of(T, topo, rank)[now[0]]
+        r2, p2 = topo.addr(mate, path[0])
+        m2, n2 = emask(topo, path[0], mate, 16)
+        fn = lambda: g.remote_dma_fused([RemoteDMATransfer(dst_ids=[DstId(rid=r2, pnc=p2)], dma_engine_mask=m2, remote_sem=T.sem[s], srcs=[x["ap"], y["ap"]],
+                                                           dsts=[out["ap"]], alu_op=2)], local_sem=T.sem.sent)
+        i = op("pool", fn, [x, y], [out], 400, 0.0, ("sent", None))
+        ops[i]["fold"] = (out["ap"], s, n2, x["ap"], y["ap"])
+        for a in (x, y):
+            last[a["name"]] = [e for e in last[a["name"]] if e[0] != i]
+        uses[s] = uses.get(s, 0) + emask(topo, mate, path[0], 16)[1]
+        uses["sent"] = uses.get("sent", 0) + n2
+        j = op("net", None, [x, y], [out], 0, FOLD0 + out["n"] * FOLDR, (s, uses[s]))
+        ops[j]["deps"] = {i: "t"}
 
     SL = {"x": -1, "b": 0, "a": 1, "c": 2}
     w = W_
@@ -228,11 +283,12 @@ def build(g, T, topo, rank):
         now[0] = s
         rows = slice(64 * s, 64 * s + 64)
         for h in range(2):
-            q = ("sp", "act")[h]
+            dma("sp", A("C", 0, V, h=h), T.ch[rows, :], 524288 + 786432 * s)
+        for h in range(2):
+            dma("sp", A("X", TR, TR + V, h=h), T.x[rows, :], 786432 * (s + 1))
+        for h in range(2):
             for j, x in ((0, T.sb), (2, T.ic), (1, T.ia)):
-                dma(q, A("l32", 24 * s + WC * j, 24 * s + WC * j + WC, h=h), x[rows, WC * h:WC * h + WC], 2048)
-            dma(q, A("C", 0, V, h=h), T.ch[rows, :], 524288 + 786432 * s)
-            dma(q, A("X", TR, TR + V, h=h), T.x[rows, :], 786432 * (s + 1))
+                dma("act", A("l32", 24 * s + WC * j, 24 * s + WC * j + WC, h=h), x[rows, WC * h:WC * h + WC], 2048 + 786432 * s)
     for s in range(2):
         now[0] = s
         rows = slice(64 * s, 64 * s + 64)
@@ -245,6 +301,7 @@ def build(g, T, topo, rank):
         mine = [i for i, o in enumerate(ops) if o["eng"] == q]
         for i, j in zip(mine, mine[1:]):
             ops[j]["deps"][i] = "o"
+        loads[q] = mine[-1]
     now[0] = None
     ms(A("ones"), 1.0)
     cp(A("onk"), A("ones"))
@@ -272,16 +329,30 @@ def build(g, T, topo, rank):
     ts(A("pc", 2, 3), A("pc", 0, 1), -1.0, ALU.mult, 15.0, ALU.add)
     ts(A("pc", 3, 4), A("pc", 0, 1), float(TR + NX), ALU.add)
     ts(A("pc", 4, 5), A("pc", 1, 2), 2.0, ALU.mult, A("pc", 0, 1), ALU.add)
+    if BL == 64:
+        ts(A("pc", 5, 6), A("pc", 0, 1), float(TR + NX + 16), ALU.add)
+        ts(A("pc", 6, 7), A("pc", 0, 1), 16.0, ALU.add)
     R_, R15, HI, HR = [A("pc", j, j + 1) for j in (0, 2, 3, 4)]
     ts(A("tk", 0, 128), A("idb"), R15, ALU.mult)
     act(A("bok"), A("bob"), ACT.Copy)
     for j, x in enumerate((1.0, -16.0, 32.0, -32.0, -1.0)):
         act(A("b8", 8 * j, 8 * j + 8), A("bob", 0, 128, 16), ACT.Copy, scale=x)
     asel(A("seg"), A("ones"), [[0, 8], [1, 16]], ALU.not_equal, 0.0, 0, 0)
-    spots(A("rst"), 1.0, [[0, 8], [1, 32]], cm=0)
-    asel(A("ee", p=64), A("zero", p=64), [[16, 2], [0, 4], [-1, 32]], ALU.is_gt, 4096.0, -32, 1)
-    spots(A("ee", p=32), -1.0, [[1, 2], [2, 4], [0, 32]], WC, -1, p=32)
-    iota(A("t4"), [[0, 8], [8192, 2]], TR - 4096, 0)
+    nb = w // BL
+    spots(A("r16", p=32), 1.0, [[0, 8], [1, 16]], 0, -1, p=32)
+    for q, a, c in SECT:
+        spots(A("rst", a, a + nb * c), 1.0, [[0, nb], [1, c]], cm=0)
+        asel(A("tri", a, a + nb * c, p=32), A("zero", 0, nb * c, p=32), [[0, nb], [-1, c]], ALU.is_gt, 4096.0, 16 * q, 1)
+        spots(A("ee", a, a + nb * c, p=32), -1.0, [[BL // 16, nb], [0, c]], WC + q, -1, p=32)
+    if STEP:
+        spots(A("nid4k"), -4096.0, [[-1, 128]])
+        spots(A("e0", p=32), 1.0 / 32, [[0, 8], [1, 16]], cm=0, p=32)
+        iota(A("c4k"), [[0, 128]], 4096, 0)
+    if CUM:
+        spots(A("id16"), 16.0, [[-1, 128]])
+    asel(A("i8", p=64), A("zero", 0, 16, p=64), [[0, 16]], ALU.is_ge, 8.5 * 4096, 31, -1)
+    asel(A("i8", p=64), A("i8", p=64), [[0, 2], [-1, 8]], ALU.not_equal, -4096.0, 0, 1)
+    iota(A("t4"), [[0, L // BL], [8192, 2], [0, BL // 32]], TR - 4096, 0)
     act(A("i9"), A("t4"), ACT.Copy, scale=1.0 / 32)
     iota(A("ci"), [[16, 8]], 15, 0)
     cp(A("cu"), A("ci"))
@@ -295,6 +366,9 @@ def build(g, T, topo, rank):
         act(A("ab", 16 * s, 16 * s + WC), A("l32", o + WC, o + 16), ACT.Copy)
         act(A("ab", 16 * s + WC, 16 * s + 16), A("l32", o, o + WC), ACT.Copy)
         spots(A("lt", p=64), 1.0, [[0, 8], [1, 16]], 32, -1, p=64)
+        if STEP:
+            ms(A("st", 0, 2), 1.0)
+        ms(A("prod", 0, w), 0.0)
         cp(A("thr", 0, 1), A("l32", 48 + 4 * s, 49 + 4 * s))
         ts(A("thd"), A("nidk"), A("thr", 0, 1), ALU.mult)
     now[0] = None
@@ -347,94 +421,158 @@ def build(g, T, topo, rank):
                 mm((A("pd", 0, 2 * w), [(A("onk"), A("thd"))]), stop=False)
                 mm((A("pk", 0, 2 * w), [(A("ones"), A("tk"))]), stop=False)
                 steps = STEPS[EMODE[s][m]]
-                for s0, cwid, form in steps:
-                    em = form == "e"
-                    a, b = 16 * s0, 16 * (s0 + cwid)
-                    act(A("xb", a, b), IND(xw, kk("k16", "b", s0, s0 + cwid)), ACT.Copy)
-                    if em:
-                        act(A("xc", a, b), IND(xw, kk("k16", "c", s0, s0 + cwid)), ACT.Copy)
-                    for x in ("a" if em else "ca"):
-                        tt(A("d%sb" % x, a, b), IND(xw, kk("k16", x, s0, s0 + cwid)), A("xb", a, b), ALU.subtract)
-                        if x == "c" and form == "n":
-                            act(A("acb", a, b), A("dcb", a, b), ACT.Abs)
-                        elif x == "c":
-                            ts(A("acb", a, b), A("dcb", a, b), 0.0, ALU.max, 2.0, ALU.mult)
-                    ts(A("rab", a, b), A("dab", a, b), -2.0 ** -11, ALU.max)
-                    us = list(range(a, b, 512))
-                    rbs = []
-                    for u in us:
-                        rbs.append(A("pr%d" % (ring[0] % 2)))
-                        ring[0] += 1
-                    if em:
-                        for u, rb in zip(us, rbs):
-                            mm((rb, [(A("idb"), A("xc", u, u + 512)), (A("nidb"), A("xb", u, u + 512))]))
-                            act(A("acb", u, u + 512), rb, ACT.Abs)
-                    for u, rb in zip(us, rbs):
-                        if em:
-                            mm((rb, [(A("idb"), A("xb", u, u + 512)), (A("nidb"), A("xc", u, u + 512)), (A("idb"), A("dab", u, u + 512))]))
-                        else:
-                            mm((rb, [(A("nidb"), A("dcb", u, u + 512)), (A("idb"), A("dab", u, u + 512))]))
-                        act(A("aac", u, u + 512), rb, ACT.Abs)
+                i0 = len(ops)
 
-                def red(name, bank_, c0, c1, j0, j1, stop=False, nl=w):
+                def diff(out, a, b, terms):
+                    for u in range(a, b, 512):
+                        v = min(b, u + 512)
+                        rb = A("pr%d" % (ring[0] % 2), 0, v - u)
+                        ring[0] += 1
+                        mm((rb, [(A(x), A(y, u, v)) for x, y in terms]))
+                        act(A(out, u, v), rb, ACT.Abs)
+                work = WORK[EMODE[s][m]]
+
+                def pair(x, j, forms=None):
+                    s0, cw_ = steps[j][:2]
+                    o = [q for q, st in enumerate(steps) if st[0] == s0 ^ 32 and st[1] == cw_ == 32]
+                    if PAIR and o and (forms is None or (steps[j][2] in forms and steps[o[0]][2] in forms)):
+                        return (1024 * (s0 // 64), 1024 * (s0 // 64 + 1)) if work.index((x, j)) > work.index((x, o[0])) else None
+                    return 16 * s0, 16 * (s0 + cw_)
+                for x, j in work:
+                    s0, cwid, form = steps[j]
+                    a, b = 16 * s0, 16 * (s0 + cwid)
+                    neg = form in ("df", "d1")
+                    xb, xc, dab, dcb, rab, acb, aac = [A(q, a, b) for q in ("xb", "xc", "dab", "dcb", "rab", "acb", "aac")]
+                    lst = IND(xw, kk("k16", x, s0, s0 + cwid))
+                    cuts = [0] + (FIRST if (x, j) in work[:2] else END if (x, j) == work[-1] else []) + [cwid]
+
+                    def gsub(out):
+                        for c0, c1 in zip(cuts, cuts[1:]):
+                            u = (a + 16 * c0, a + 16 * c1)
+                            tt(A(out, *u), IND(xw, kk("k16", x, s0 + c0, s0 + c1)), A("xb", *u), ALU.add if neg else ALU.subtract)
+                    if x == "b":
+                        for c0, c1 in zip(cuts, cuts[1:]):
+                            act(A("xb", a + 16 * c0, a + 16 * c1), IND(xw, kk("k16", x, s0 + c0, s0 + c1)), ACT.Copy, scale=-1.0 if neg else 1.0)
+                    elif x == "c" and form == "e":
+                        act(xc, lst, ACT.Copy)
+                        diff("acb", a, b, [("idb", "xc"), ("nidb", "xb")])
+                    elif x == "c":
+                        if neg:
+                            for c0, c1 in zip(cuts, cuts[1:]):
+                                act(A("dcb", a + 16 * c0, a + 16 * c1), IND(xw, kk("k16", x, s0 + c0, s0 + c1)), ACT.Copy)
+                            add(dcb, xb, "ad%d_%d" % (s, j))
+                        else:
+                            gsub("dcb")
+                        if form == "n":
+                            act(acb, dcb, ACT.Abs)
+                        elif pair(x, j, ("r", "rf")):
+                            ts(A("acb", *pair(x, j, ("r", "rf"))), A("dcb", *pair(x, j, ("r", "rf"))), 0.0, ALU.max, 2.0, ALU.mult)
+                    else:
+                        gsub("dab")
+                        if pair(x, j):
+                            ts(A("rab", *pair(x, j)), A("dab", *pair(x, j)), -2.0 ** -11, ALU.max)
+                    if x != "b" and work.index((x, j)) == max(work.index(("a", j)), work.index(("c", j))):
+                        for c0, c1 in zip(cuts, cuts[1:]) if (x, j) == work[-1] else [(0, cwid)]:
+                            if form in ("df", "rf"):
+                                fold(aac, dab, dcb, "fo%d_%d" % (s, j))
+                            elif form == "e":
+                                diff("aac", a + 16 * c0, a + 16 * c1, [("idb", "xb"), ("nidb", "xc"), ("idb", "dab")])
+                            else:
+                                diff("aac", a + 16 * c0, a + 16 * c1, [("nidb", "dcb"), ("idb", "dab")])
+                for e in CHAIN:
+                    mine = [i for i in range(i0, len(ops)) if ops[i]["eng"] == e]
+                    for i, j in zip(mine, mine[1:]):
+                        ops[j]["deps"].setdefault(i, "o")
+
+                def red(name, bank_, c0, c1, j0, j1, stop=False, l0=0, l1=w):
+                    if name in LAST.split() and (l0, l1) == (0, w):
+                        red(name, bank_, c0, c1, j0, j1, False, 0, 96)
+                        l0 = 96
                     for k0 in range(0, 16, RED):
-                        mm(*[(A(bank_, c0 + k, c1, 16, p=nl), [(A(name, k, 16 * nl, 16), A("b8", j0, j1))]) for k in range(k0, k0 + RED)],
+                        mm(*[(A(bank_, c0 + k, c1, 16, p=(l0, l1)), [(A(name, 16 * l0 + k, 16 * l1, 16), A("b8", j0, j1))]) for k in range(k0, k0 + RED)],
                            start=False, stop=stop and k0 + RED == 16, one=True)
-                nr = sum(c for _, c, form in steps if form == "r")
-                if nr:
-                    red("dcb", "pd", w, 2 * w, 32, 40, nl=nr)
+                nf = sum(c for _, c, form in steps if form in ("df", "rf"))
+                nr = nf + sum(c for _, c, form in steps if form in ("r", "d1"))
+                if nf:
+                    red("dab", "pd", 0, w, 32, 40, l1=nf)
+                    red("dcb", "pd", 0, 2 * w, 32, 48, l1=nf)
+                if nr > nf:
+                    red("dcb", "pd", w, 2 * w, 32, 40, l0=nf, l1=nr)
                 red("acb", "pd", w, 2 * w, 0, 8)
                 red("dab", "pk", 0, w, 8, 16)
                 red("rab", "pk", 0, 2 * w, 16, 32)
-                red("aac", "pd", 0, w, 0, 8, True)
+                if nf < w:
+                    red("aac", "pd", 0, w, 0, 8, True, l0=nf)
+                if nf:
+                    red("aac", "pd", 0, w, 48, 56, True, l1=nf)
                 ka, kc = A("pk", 0, w), A("pk", w, 2 * w)
                 act(A("tp"), A("pd", 0, w), ACT.Relu, bias=HH / 2, scale=-HH)
                 tt(A("col"), A("tp"), A("pd", w, 2 * w), ALU.is_lt)
                 mm((ka, [(A("id16k"), A("col"))]), (kc, [(A("idm"), A("col")), (A("nidb"), A("tp"))]), start=False, one=True)
-                act(A("keys"), ka, ACT.Copy)
-                scan(A("scn"), A("seg"), A("keys"), ALU.mult, ALU.max)
-                tt(A("oht"), IND(A("scn"), A("cu")), A("keys"), ALU.is_equal)
                 ns = 1 if fin else 3
-                mm(*[(A("pr0", j * w, j * w + w), [(A("oht"), A("idb"))]) for j in range(ns)])
-                tt(A("prod", w, w + ns * w), A("kf", f0, f0 + ns * w), A("pr0", 0, ns * w), ALU.mult)
-                mm((cn, [(A("col"), A("idb"))] + ([(A("idb"), A("off0"))] if fin else [])))
-                act(kk("prod", "x"), cn, ACT.Copy)
+                if STEP:
+                    scan(A("scn"), A("seg"), ka, ALU.mult, ALU.max)
+                    tt(A("st", 2, w + 2), IND(A("scn"), A("cu")), A("scn"), ALU.is_equal)
+
+                    def hot(pos, neg, one):
+                        return [(A("st", 2, w + 2), A(pos)), (A("st", 1, w + 1), A(neg)), (A("e0", p=32), A(one, p=32))]
+                    mm((A("pr0", 0, w), hot("idb", "nidb", "ones")))
+                    for j in range(ns):
+                        tt(A("prod", w + j * w, 2 * w + j * w), A("kf", f0 + j * w, f0 + j * w + w), A("pr0", 0, w), ALU.mult)
+                else:
+                    act(A("keys"), ka, ACT.Copy)
+                    scan(A("scn"), A("seg"), A("keys"), ALU.mult, ALU.max)
+                    tt(A("oht"), IND(A("scn"), A("cu")), A("keys"), ALU.is_equal)
+                    mm(*[(A("pr0", j * w, j * w + w), [(A("oht"), A("idb"))]) for j in range(ns)])
+                    tt(A("prod", w, w + ns * w), A("kf", f0, f0 + ns * w), A("pr0", 0, ns * w), ALU.mult)
+                if fin:
+                    mm((cn, [(A("col"), A("idb")), (A("off0"), A("id16")) if CUM else (A("idb"), A("off0"))]))
+                    act(kk("prod", "x"), cn, ACT.Copy)
+                elif CUM:
+                    scan(A("cum"), A("seg"), A("col"), ALU.mult, ALU.add)
+                    ts(A("off0"), A("cum"), -8.0, ALU.add, 0.0, ALU.max)
+
                 nr = WC * (ns + 1)
                 mm(*[(A("pr1", r, w, 16, p=nr), [(A("prod", r, w + ns * w, 16), A("bok", 0, w, 16))]) for r in range(16)])
                 act(A("lt", p=nr), A("pr1", 0, w, p=nr), ACT.Copy)
-                mm((A("pr1", w, w + nr), [(A("lt", p=32), A("idk", 0, nr, p=32))]))
-                cp(A("lst", 0, ns * WC), A("pr1", w + WC, w + nr))
-                dd = A("pk", 2 * w, 4 * w)
-                mm((dd, [(A("lt", p=64), A("ee", p=64))]),
-                   *[(A("pk", (2 + q) * w, (3 + q) * w), [(A("bok"), kk("prod", "b"))]) for q in range(2)], one=True)
+                mm((A("pk", 2 * w, 2 * w + nr), [(A("lt", p=32), A("idk", 0, nr, p=32))]),
+                   *([(A("pk", 2 * w + 32, 2 * w + 32 + old["n"]), [(A("lt", p=64), A("i8", 0, old["n"], p=64))])] if fin else []))
+                cp(A("lst", 0, ns * WC), A("pk", 2 * w + WC, 2 * w + nr))
+                dd = A("pr0", 0, ND)
+                mm((dd, [(A("r16", p=32), A("tri", p=32))]),
+                   *[(A("pr0", a + c * j, a + c * j + c), [(A("bok"), kk("prod", "b", BL * j, BL * j + c))]) for q, a, c in SECT[1:] for j in range(w // BL)],
+                   (A("pr0", 0, w), [(A("bok"), kk("prod", "b"))]), stop=False, one=True)
+                mm((dd, [(A("lt", p=32), A("ee", p=32))]), start=False)
                 act(A("ad"), dd, ACT.Abs)
                 scan(A("nd"), A("rst"), A("ad"), ALU.max, ALU.min)
                 act(A("xz"), IND(xw, A("lst", 0, WC)), ACT.Copy)
-                mm(*[(A("pr0", h * w, h * w + w), [(A("db", 128 * h, 128 * h + 128), A(x)) for x in ("xz", yv)]) for h in range(2)])
-                act(A("hh"), A("pr0", 0, L), ACT.Identity, bias=191.75, scale=0.5)
-                if fin:
-                    for q in range(2 if t < TV - 1 else 1):
-                        act(A("sm", WC * q, WC * q + WC), A("pr1", w, w + WC), ACT.Relu, bias=8.5 * 8192, scale=-8192.0)
-                o = 400
-                mm((A("pr1", o, o + 16), [(A("onk", p=32), A("i9", p=32))]),
-                   *[(A("pr1", o + 8 * h, o + 8 * h + 8, h=h2), [(A("lt", 64 * h, 64 * h + 64, p=32), A("idk", WC, 2 * WC, p=32))]) for h in range(2) for h2 in range(2)],
-                   stop=False, one=True)
-                mm(*[(A("pr1", o + 8 * h + q, o + 8 * h + 8, 2), [(A(("db4k", "ndb4k")[q], 128 * h, 128 * h + 128), A("nd", w * q + 31, w * q + w, 32))])
-                     for h in range(2) for q in range(2)], start=False, one=True)
-                ts(A("idx"), A("pr1", o, o + 16), HI, ALU.min, R_, ALU.max)
+                mm(*[(A("pr1", h * w, h * w + w), [(A("db", 128 * h, 128 * h + 128), A(x)) for x in ("xz", yv)]) for h in range(2)])
+                act(A("hh"), A("pr1", 0, L), ACT.Identity, bias=191.75, scale=0.5)
                 if fin:
                     k = old["n"]
-                    tt(A("sm", 16, 16 + k), old, A("sm", 0, k), ALU.add)
-                    tt(A("sm", 32 + 24 * t, 32 + 24 * t + k), A("sm", 16, 16 + k), A("nl", 16 * t, 16 * t + k), ALU.min)
+                    tt(A("sm", 0, k), A("nl", 16 * t, 16 * t + k), A("pk", 2 * w + 32, 2 * w + 32 + k), ALU.min)
+                    tt(A("sm", 32 + 24 * t, 32 + 24 * t + k), A("sm", 0, k), old, ALU.max)
                     if t < TV - 1:
                         cp(A("sa"), A("sm", 32, 48))
                         send(A("sa", 0, WC))
-                for c in range(WC - 1, -1, -1):
-                    tt(IND(sw, A("idx", 2 * c, 2 * c + 2)), A("hh", 32 * c, 32 * c + 32), A("m192"), ALU.add)
-                mm((cn, [(A("bok"), kk("prod", "x"))]))
-                if not fin:
+                o, nq = 3 * w, BL // 16
+                mm((A("pk", o, o + 16), [(A("onk", p=32), A("i9", p=32))]),
+                   *[(A("pk", o + 8 * h, o + 8 * h + 8, h=h2), [(A("lt", 64 * h, 64 * h + 64, p=32), A("idk", WC, 2 * WC, p=32))]) for h in range(2) for h2 in range(2)],
+                   stop=False, one=True)
+                mm(*[(A("pk", o + 8 * h + q, o + 8 * h + 8, nq), [(A(("db4k", "ndb4k")[2 * q // nq], 128 * h, 128 * h + 128), A("nd", a + c - 1, a + c * w // BL, c))])
+                     for h in range(2) for q, a, c in SECT], start=False, one=True)
+                for q in range(nq // 2):
+                    ts(A("idx", q, 16, nq // 2), A("pk", o + q, o + 16, nq // 2), A("pc", 3 + 2 * q, 4 + 2 * q), ALU.min, A("pc", 6 * q, 6 * q + 1), ALU.max)
+                for c in range(L // BL - 1, -1, -1):
+                    tt(IND(sw, A("idx", nq * c, nq * c + nq)), A("hh", BL * c, BL * c + BL), A("m192"), ALU.add)
+                if not fin and not CUM:
+                    mm((cn, [(A("col"), A("idb"))]))
+                    act(kk("prod", "x"), cn, ACT.Copy)
+                if fin or not CUM:
+                    mm((cn, [(A("bok"), kk("prod", "x"))]))
+                if not fin and not CUM:
                     act(A("off0"), cn, ACT.Relu, bias=-8.0)
-                else:
+                if fin:
                     yn = A("yn", t * w, t * w + w)
                     act(cn, cn, ACT.Sign, A("thr", 2, 3) if t < TV - 1 else None, bias=-8.5)
                     tt(A("ty"), A(yv), cn, ALU.mult)
@@ -450,7 +588,7 @@ def build(g, T, topo, rank):
                     ts(A("thr", 1, 2), A("pd", 2 * w, 2 * w + 1), 128.0, ALU.add, A("thr", 0, 1), ALU.add)
                     ts(A("thd"), A("nidk"), A("thr", 1, 2), ALU.mult)
                 co, m0 = A("CO", m * w, m * w + w), A("pk", 0, w)
-                mm((m0, [(A("wv"), A("idk")), (A("idk"), kk("kf", "b"))] + ([] if fin else [(A("oht"), A("id4k"))])))
+                mm((m0, [(A("wv"), A("idk")), (A("idk"), kk("kf", "b"))] + ([] if fin else hot("id4k", "nid4k", "c4k") if STEP else [(A("oht"), A("id4k"))])))
                 if fin:
                     act(co, m0, ACT.Copy)
                 else:
@@ -467,7 +605,10 @@ def build(g, T, topo, rank):
             dma(q, T.xo[rows, 768 * h:768 * h + 768], A("X", TR + 768 * h, TR + 768 * h + 768, h=h), 196608)
             dma("sp", T.so[rows, WC * h:WC * h + WC], A("sm", 56, 64, h=h), 2048)
             dma("sp", T.yo[rows, w * h:w * h + w], A("yn", w, 2 * w, h=h), 16384)
-    return ops, ne_ * len(sends)
+    for o in ops[loads["act"] + 1:]:
+        if o["eng"] == "act":
+            o["deps"].setdefault(loads["act"], "o")
+    return ops, ne_ * len(sends) + uses.get("sent", 0)
 
 
 def sweep(ops, before, after, prio, look, back):
@@ -515,35 +656,46 @@ def plan(ops):
     for i in range(n - 1, -1, -1):
         base[i] = ops[i]["busy"] + max([base[u] + d for u, d in fw[i]] + [ops[i]["lat"]])
     rng = np.random.default_rng(SEED)
-    best = r = score = None
+    late = np.array([1.0 if o["s"] == 1 else 0.0 for o in ops])
+    cases = [case(ops, *c) for c in CASES]
+    kept = []
     for k in range(TRIES):
-        look = float(rng.choice([40.0, 150.0, 300.0]))
-        if k % 8 == 0 and k < TRIES // 2:
-            lead = LEAD * float(rng.uniform(0.5, 2.0))
-            prio = [p + (lead if ops[i]["s"] != 1 else 0.0) for i, p in enumerate(base)]
+        look = float(rng.choice(LOOK))
+        if k < 4 * KEEP:
+            r = sweep(ops, bw, fw, (np.array(base) * rng.uniform(1.0, 1.4) - late * LEAD * rng.uniform(0.4, 1.6)).tolist(), look, False)
+            for _ in range(3):
+                r = sweep(ops, bw, fw, sweep(ops, fw, bw, r[2], look, True)[2], look, False)
         else:
-            src = r if k < TRIES // 2 else best
-            z = rng.uniform(0, float(rng.choice([0.0, 100.0, 400.0])), n)
-            prio = sweep(ops, fw, bw, [src[2][i] + float(z[i]) for i in range(n)], look, True)[2]
-        r = sweep(ops, bw, fw, prio, look, False)
-        if best is None or max(r[2]) <= score[0] + 3000:
-            now = max(r[2]) + sum(replay(ops, r[0], *c) for c in CASES)
-            if best is None or now <= score[1]:
-                best, score = r, (max(r[2]), now)
-    return best
+            e = np.array(kept[int(rng.integers(len(kept)))][1][2])
+            lo = rng.uniform(0, e.max())
+            z = rng.uniform(0, float(rng.choice([100.0, 400.0, 1200.0])), n)
+            if rng.random() < 0.3:
+                z = z + late * rng.uniform(-1500, 1500)
+            z = z * ((e > lo) & (e < lo + rng.uniform(3000, 30000)))
+            r = sweep(ops, bw, fw, sweep(ops, fw, bw, (e + z).tolist(), look, True)[2], look, False)
+        if len(kept) < KEEP or max(r[2]) <= max(kept[0][1][2]) + 2000:
+            kept.append((max(r[2]) + sum(replay(r[0], *c) for c in cases), r))
+            kept.sort(key=lambda x: x[0])
+            del kept[KEEP:]
+    return kept[0][1]
 
 
-def replay(ops, order, hop, same, speed, lat):
-    free, end, fin = {}, [0.0] * len(ops), 0.0
+def case(ops, hop, same, gather, scatter, fixed, lat):
+    busy = [o["busy"] + o["ge"] * (gather - G_) + o["se"] * (scatter - SC_) + o["mm"] * (fixed - P0) for o in ops]
+    pre = [[(j, 0.0 if k == "o" else ops[j]["lat"] * lat + (0.0 if k == "t" else same if o["eng"] == ops[j]["eng"] else hop)) for j, k in o["deps"].items()] for o in ops]
+    return [o["eng"] for o in ops], busy, pre, [o["lat"] * lat for o in ops]
+
+
+def replay(order, eng, busy, pre, tail):
+    free, end, fin = dict.fromkeys(eng, 0.0), [0.0] * len(eng), 0.0
     for i in order:
-        o = ops[i]
-        t = free.get(o["eng"], 0.0)
-        for j, k in o["deps"].items():
-            d = end[j] + (0.0 if k == "o" else ops[j]["lat"] * lat + (0.0 if k == "t" else same if o["eng"] == ops[j]["eng"] else hop))
-            if d > t:
-                t = d
-        free[o["eng"]] = end[i] = t + o["busy"] * speed.get(o["eng"], 1.0)
-        fin = max(fin, end[i] + o["lat"] * lat)
+        t = free[eng[i]]
+        for j, d in pre[i]:
+            if end[j] + d > t:
+                t = end[j] + d
+        free[eng[i]] = end[i] = t = t + busy[i]
+        if t + tail[i] > fin:
+            fin = t + tail[i]
     return fin
 
 
@@ -584,9 +736,8 @@ def emit(g, T, ops, order, nsent):
         if count[e]:
             g.wait_ge(T.sem[e], count[e])
     g.wait_ge(T.sem.sent, nsent)
-    for i, o in enumerate(ops):
-        if o["sem"] is not None and o["sem"][1] is not None:
-            g.wait_ge(T.sem[o["sem"][0]], o["sem"][1])
+    for s, v in {o["sem"][0]: o["sem"][1] for o in ops if o["sem"] is not None and o["sem"][1] is not None}.items():
+        g.wait_ge(T.sem[s], v)
 
 
 ORDER = []
@@ -605,6 +756,22 @@ def rank_program(g, core, T, topo):
                     g.wait_ge(T.sem[sem], nin)
                     g.remote_dma(T[land][:], T[land][:], T.sem[sem], T.sem.sent, pid, rid, mk)
                 g.wait_ge(T.sem.sent, nout * len(MSG))
+            if core in mates_of(T, topo, r):
+                ops = build(g, T, topo, r)[0]
+                if not ORDER:
+                    ORDER.append(plan(ops))
+                rid, pid = topo.addr(path[0], core)
+                mk, nout = emask(topo, core, path[0], 16)
+                got = {"sent": 0}
+                for i in ORDER[0][0]:
+                    if "fold" in ops[i] and ops[i]["s"] == mates_of(T, topo, r).index(core):
+                        ap, sem, nin = ops[i]["fold"][:3]
+                        got[sem] = got.get(sem, 0) + nin
+                        got["sent"] += nout
+                        g.wait_ge(T.sem[sem], got[sem])
+                        g.remote_dma(ap, ap, T.sem[sem], T.sem.sent, pid, rid, mk)
+                if got["sent"]:
+                    g.wait_ge(T.sem.sent, got["sent"])
         return
     ops, nsent = build(g, T, topo, rank)
     if not ORDER:

import numpy as np
from concourse.bass import DstId, RemoteDMATransfer
from concourse.mybir import dt, AluOpType, AxisListType, ActivationFunctionType

ALU = AluOpType
ACT = ActivationFunctionType
V, L, TV, LV, H = 1024, 256, 2, 2, 3
W_, WC = 128, 8
BL = 64
SECT = [(q, sum(16 * (u + 1) * W_ // BL for u in range(q + 1, BL // 16)), 16 * (q + 1)) for q in range(BL // 16 - 1, -1, -1)]
ND = SECT[-1][1] + 16 * W_ // BL
TR = BL // 2
NX = V + 512
STEPS = {0: [(0, 32, "r"), (32, 32, "r"), (64, 32, "r"), (96, 32, "r")],
         1: [(0, 32, "r"), (96, 32, "e"), (32, 32, "r"), (64, 32, "r")],
         2: [(0, 32, "r"), (96, 32, "e"), (64, 32, "e"), (32, 32, "r")],
         3: [(0, 32, "df"), (32, 32, "df"), (64, 32, "df"), (96, 32, "r")],
         4: [(0, 32, "df"), (32, 32, "df"), (64, 32, "rf"), (96, 32, "r")],
         5: [(0, 32, "d1"), (32, 32, "d1"), (64, 32, "r"), (96, 32, "r")],
         6: [(0, 32, "rf"), (32, 32, "rf"), (96, 32, "e"), (64, 32, "e")],
         7: [(0, 32, "df"), (32, 32, "df"), (64, 32, "r"), (96, 32, "r")]}
STEPS[8] = [(0, 32, "r"), (32, 32, "r"), (64, 32, "n"), (96, 32, "e")]
WORK = {e: [(x[0], int(x[1])) for x in "b0 c0 a0 b3 c3 a3 b1 c1 a1 b2 c2 a2".split()] for e in STEPS}
STEPS[9] = [(0, 32, "rf"), (32, 32, "df"), (64, 32, "df"), (96, 32, "n")]
WORK[9] = [(x[0], int(x[1])) for x in "b0 c0 b1 c1 b2 c2 a0 a1 a2 b3 c3 a3".split()]
STEPS[10] = STEPS[8]
WORK[10] = [(x[0], int(x[1])) for x in "b0 c0 a0 b3 a3 c3 b1 a1 c1 b2 a2 c2".split()]
CHAIN = []
FIRST, END = [16], []
LAST = ""
ADD0, ADD1, ADDR = 700.0, 1200.0, 1.2
FOLD0, FOLDR = 2800.0, 1.5
EMODE = [[10, 10, 10, 10], [10, 10, 10, 10]]
KS = [[0, 1, 1, 1], [1, 1, 1, 1]]
LEAD = 10000.0
TRIES, SEED = 3500, 3050
KEEP = 6
NET = 4000.0
STEP, CUM, PAIR = False, False, True
LOOK = [40.0, 150.0, 300.0, 450.0]
SUBA, SUBV = 32, 32
RED = 4
BIG = 16384.0
HH = 2.0 ** 17

B, F, I32, U, K = "bfloat16", "float32", "int32", "uint16", "float16"
PER_STREAM = {
    "X": (2 * TR + NX, B), "C": (NX, I32), "CO": (512, F), "CI": (256, I32), "y": (128, B), "sa": (16, U), "ra": (8, U), "la": (24, U),
    "ry": (128, B), "yn": (256, B), "lst": (24, U), "k16": (384, U), "kf": (768, K), "nv": (512, B),
    "xb": (2048, B), "xc": (2048, B), "dab": (2048, B), "dcb": (2048, B), "rab": (2048, B), "acb": (2048, B), "aac": (2048, B),
    "pqr": (384, B), "thd": (256, K), "keys": (128, F), "scn": (128, F), "bs": (896, B), "st": (130, B), "ks": (256, K),
    "rnd": (128, I32), "prod": (512, K), "lt": (128, K), "ad": (ND, B), "nd": (ND, B),
    "idx": (16, U), "hh": (256, B), "sm": (128, F), "thr": (4, F),
}
PARTS = {n: ("bs", 128 * j) for j, n in enumerate(("tp", "col", "oht", "xz", "off0", "ty", "cum"))}
PARTS.update({n: ("ks", 128 * j) for j, n in enumerate(("sel", "wv"))})
SHARED = {
    "l32": (56, I32), "lb": (16, U), "ab": (32, F), "rc": (16, U),
    "ones": (128, B), "onk": (128, K), "idb": (128, B), "nidb": (128, B), "bo0": (128, B), "bob": (128, B), "idk": (128, K), "nidk": (256, K),
    "id4k": (128, B), "id16k": (128, B), "idm": (128, B), "idh": (128, B), "bok": (128, K), "db": (256, B), "db4k": (256, B), "ndb4k": (256, B),
    "dsum": (128, F), "b8": (56, B), "tk": (256, B), "pi": (4, I32), "pc": (8, F), "seg": (128, B), "rst": (ND, B),
    "ee": (ND, K), "tri": (ND, K), "r16": (128, K), "i9": (16, K), "i8": (16, K), "nid4k": (128, B), "e0": (128, B), "c4k": (128, B), "id16": (128, B), "zero": (256, B), "t4": (16, F), "ci": (8, I32), "cu": (8, U),
    "nid": (256, F), "nl": (64, F), "m192": (BL, B),
}
SCRATCH = {n: ("sbuf", [128, c], d) for n, (c, d) in SHARED.items()}
for s_ in range(2):
    SCRATCH.update({"%s_%d" % (n, s_): ("sbuf", [128, c], d) for n, (c, d) in PER_STREAM.items()})
    SCRATCH.update({"%s_%d" % (n, s_): ("psum", [128, 512], F) for n in ("pd", "pk", "pr0", "pr1")})
NDMA = 96
MSG = (("rc", "arc"), ("ra_0", "ara0"), ("ry_0", "ary0"), ("ra_1", "ara1"), ("ry_1", "ary1"))
SEMAPHORES = ["dve", "act", "pe", "pool", "sent"] + [m_[1] for m_ in MSG] + ["d%d" % i for i in range(NDMA)] + [
    "%s%d_%d" % (n, s_, c) for n in ("ad", "fo") for s_ in range(2) for c in range(4)]
G_, SC_, PE_, TT_ = 1.56, 3.8, 0.5, 2.0
V0, V1, S0, P0 = 60.0, 60.0, 78.0, 18.0
HOP, SAME = 150.0, 100.0
CASES = [(90.0, 60.0, 1.15, 2.2, 12.0, 0.7), (100.0, 70.0, 2.0, 5.2, 18.0, 0.8), (260.0, 170.0, 1.56, 3.8, 28.0, 1.6), (200.0, 130.0, 1.25, 5.0, 12.0, 1.2)]
DMA0, DMA1, DMAR = 800.0, 1500.0, 350.0


def way(T, topo, r):
    src, dst = T.cores[r], T.cores[(r + H) % len(T.cores)]
    if topo.may_write(src, dst):
        return [src, dst]
    can = [c for c in topo.cores_of(src) if c not in T.cores and topo.may_write(src, c) and topo.may_write(c, dst)]
    near = [c for c in can if topo.die(c) == topo.die(src)]
    return [src, (near or can)[0], dst]


def emask(topo, a, b, most=8):
    e = topo.engines(a, b)[:most]
    return sum(1 << k for k in e), len(e)


def mates_of(T, topo, r):
    src = T.cores[r]
    busy = list(T.cores) + way(T, topo, r)
    return [c for c in topo.cores_of(src) if c not in busy and topo.die(c) == topo.die(src)][:2]


def wide(a):
    return SCRATCH[a["name"]][2] in (F, I32)


def build(g, T, topo, rank):
    ops = []
    last = {}
    bank = {}
    ndma = [0]
    now = [None]

    def A(name, a=None, b=None, s=None, h=None, p=None):
        if name in PARTS:
            name, a = PARTS[name]
            b = a + 128
        if name not in SCRATCH:
            name = "%s_%d" % (name, now[0])
        n = SCRATCH[name][1][1]
        a0, b0, s0 = a or 0, n if b is None else b, s or 1
        cols = range(a0, b0, s0)
        bits = ((1 << (b0 - a0)) - 1) << a0 if s0 == 1 else sum(1 << c for c in cols)
        p0, p1 = p if isinstance(p, tuple) else (0, p or 128) if h is None else (64 * h, 64 * h + 64)
        bits = bits | bits << n if p1 - p0 > 64 else bits << (n * (p0 // 64))
        ap = T[name][p0:p1, a0:b0] if s0 == 1 else T[name][p0:p1, a0:b0:s0]
        return {"name": name, "ap": ap, "n": len(cols), "acc": [(name, bits)], "ind": False}

    def IND(win, off):
        return {"name": win["name"], "ap": win["ap"].indirect(off["ap"]), "n": 16 * off["n"], "acc": win["acc"], "off": off["acc"], "ind": True}

    def op(eng, fn, reads, writes, busy, lat=0.0, sem=None):
        i = len(ops)
        deps = {}

        def dep(j):
            same = eng == "pe" and ops[j]["eng"] == "pe"
            if deps.get(j) != "w":
                deps[j] = "o" if same else "w"
        acc = []
        for a in reads:
            if isinstance(a, dict):
                acc += [(x, False) for x in a["acc"] + a.get("off", [])]
        for a in writes:
            acc += [(x, True) for x in a["acc"]] + [(x, False) for x in a.get("off", [])]
        for (name, bits), w in acc:
            keep = []
            for (j, bj, wj) in last.get(name, []):
                if j != i and bj & bits and (w or wj):
                    dep(j)
                if w and not (bj & ~bits) and j != i:
                    continue
                keep.append((j, bj, wj))
            keep.append((i, bits, w))
            last[name] = keep
            if SCRATCH[name][0] == "psum":
                st = bank.setdefault(name, [eng, [], [], None])
                if st[0] != eng:
                    st[0], st[1], st[2] = eng, [], st[1]
                for j in st[2]:
                    dep(j)
                if i not in st[1]:
                    st[1].append(i)
                if eng == "pe":
                    if st[3] is not None and st[3] != i:
                        dep(st[3])
                    st[3] = i
        ops.append({"eng": eng, "fn": fn, "deps": deps, "busy": busy, "lat": lat, "sem": sem, "s": now[0],
                    "out": writes[0]["name"] if writes else "", "mm": len(reads) // 2 if eng == "pe" else 0,
                    "ge": sum(a["n"] for a in reads if isinstance(a, dict) and a["ind"]), "se": sum(a["n"] for a in writes if a["ind"])})
        return i

    def vcost(out, ins, two=False):
        n = out["n"]
        if out["ind"]:
            return V0 + n * SC_
        if ins[0]["ind"]:
            return V0 + n * G_
        if two:
            ps = any(SCRATCH[a["name"]][0] == "psum" for a in ins)
            return V1 + max(64, n * (1 if ps else TT_))
        return V1 + max(64, n * (1 if any(wide(a) for a in [out] + ins) else 0.5))

    def sc(x):
        return x["ap"] if isinstance(x, dict) else x

    def cp(out, in_):
        return op("dve", lambda: g.vector.tensor_copy(out["ap"], in_["ap"]), [in_], [out], vcost(out, [in_]))

    def tt(out, a, b, o):
        return op("dve", lambda: g.vector.tensor_tensor(out["ap"], a["ap"], b["ap"], o), [a, b], [out], vcost(out, [a, b], True))

    def ts(out, a, s1, o0, s2=None, o1=None):
        if o1 is None:
            fn = lambda: g.vector.tensor_scalar(out["ap"], a["ap"], sc(s1), None, o0)
        else:
            fn = lambda: g.vector.tensor_scalar(out["ap"], a["ap"], sc(s1), sc(s2), o0, o1)
        return op("dve", fn, [a, s1, s2], [out], vcost(out, [a]))

    def scan(out, d0, d1, o0, o1):
        return op("dve", lambda: g.vector.tensor_tensor_scan(out["ap"], d0["ap"], d1["ap"], 0.0, o0, o1), [d0, d1], [out], vcost(out, [d0, d1]))

    def ms(out, v):
        return op("dve", lambda: g.vector.memset(out["ap"], v), [], [out], V1 + max(64, out["n"] * 0.5))

    def act(out, a, f, acc=None, bias=0.0, scale=1.0):
        if acc is None:
            fn = lambda: g.scalar.activation(out["ap"], a["ap"], f, sc(bias), scale)
        else:
            fn = lambda: g.scalar.activation(out["ap"], a["ap"], f, sc(bias), scale, accum_out=acc["ap"])
        return op("act", fn, [a, bias], [out] + ([acc] if acc else []), S0 + max(64, out["n"] * (G_ if a["ind"] else 1)) + (140 if acc else 0))

    def mm(*groups, start=True, stop=True, one=False):
        out = groups[0][0]

        def fn():
            r = out
            for j, (o, terms) in enumerate(groups):
                for q, (w, x) in enumerate(terms):
                    first = q == 0 and (j == 0 or not one)
                    final = q == len(terms) - 1 and (j == len(groups) - 1 or not one)
                    r = g.tensor.matmul(o["ap"], w["ap"], x["ap"], start and first, stop and final)
            return r
        return op("pe", fn, [a for o, terms in groups for t_ in terms for a in t_], [o for o, terms in groups],
                  sum(P0 + PE_ * max(min(64, w["n"]), x["n"]) * (4 if wide(x) else 1) for o, terms in groups for w, x in terms))

    def iota(out, pat, base, cm):
        if SCRATCH[out["name"]][2] == I32:
            fn = lambda: g.iota(out["ap"], pat, base, cm)
        else:
            fn = lambda: g.iota(out["ap"], pat, base, cm, allow_small_or_imprecise_dtypes=True)
        return op("pool", fn, [], [out], 130 + 2 * out["n"])

    def asel(out, a, pat, cmp_, fill, base, cm):
        return op("pool", lambda: g.affine_select(out["ap"], a["ap"], pat, cmp_, fill, base, cm), [a], [out], 170 + 2 * out["n"])

    def dma(q, out, in_, nbytes):
        s = "d%d" % ndma[0]
        ndma[0] += 1
        h = g.sync if q == "sp" else g.scalar
        rd = [in_] if isinstance(in_, dict) else []
        wr = [out] if isinstance(out, dict) else []
        return op(q, lambda: h.dma_start(sc(out), sc(in_)), rd, wr, 70, (DMA1 if rd and wr else DMA0) + nbytes / DMAR, (s, 16))

    path = way(T, topo, rank)
    rid, pid = topo.addr(path[1], path[0])
    mk, ne_ = emask(topo, path[0], path[1])
    back = way(T, topo, (rank - H) % len(T.cores))
    na_ = emask(topo, back[-2], back[-1])[1]
    sends = []

    def send(src):
        land, sem = MSG[len(sends)]
        fn = lambda: g.remote_dma(T[land][:], src["ap"], T.sem[sem], T.sem.sent, pid, rid, mk)
        i = op("pool", fn, [src], [], 500, 0.0, ("sent", None))
        if sends:
            ops[i]["deps"].setdefault(sends[-1], "o")
        sends.append(i)
        j = op("net", None, [], [A(land)], 0, NET, (sem, na_))
        ops[j]["deps"][i] = "t"

    uses, loads = {}, {}

    def add(out, in_, s):
        uses[s] = uses.get(s, 0) + 16
        return op("pool", lambda: g.dma_start(out["ap"], in_["ap"], accum_op=ALU.add), [in_, out], [out], ADD0, ADD1 + out["n"] * ADDR, (s, uses[s]))

    def fold(out, x, y, s):
        mate = mates_of(T, topo, rank)[now[0]]
        r2, p2 = topo.addr(mate, path[0])
        m2, n2 = emask(topo, path[0], mate, 16)
        fn = lambda: g.remote_dma_fused([RemoteDMATransfer(dst_ids=[DstId(rid=r2, pnc=p2)], dma_engine_mask=m2, remote_sem=T.sem[s], srcs=[x["ap"], y["ap"]],
                                                           dsts=[out["ap"]], alu_op=2)], local_sem=T.sem.sent)
        i = op("pool", fn, [x, y], [out], 400, 0.0, ("sent", None))
        ops[i]["fold"] = (out["ap"], s, n2, x["ap"], y["ap"])
        for a in (x, y):
            last[a["name"]] = [e for e in last[a["name"]] if e[0] != i]
        uses[s] = uses.get(s, 0) + emask(topo, mate, path[0], 16)[1]
        uses["sent"] = uses.get("sent", 0) + n2
        j = op("net", None, [x, y], [out], 0, FOLD0 + out["n"] * FOLDR, (s, uses[s]))
        ops[j]["deps"] = {i: "t"}

    SL = {"x": -1, "b": 0, "a": 1, "c": 2}
    w = W_
    for s in range(2):
        now[0] = s
        rows = slice(64 * s, 64 * s + 64)
        for h in range(2):
            dma("sp", A("C", 0, V, h=h), T.ch[rows, :], 524288 + 786432 * s)
        for h in range(2):
            dma("sp", A("X", TR, TR + V, h=h), T.x[rows, :], 786432 * (s + 1))
        for h in range(2):
            for j, x in ((0, T.sb), (2, T.ic), (1, T.ia)):
                dma("act", A("l32", 24 * s + WC * j, 24 * s + WC * j + WC, h=h), x[rows, WC * h:WC * h + WC], 2048 + 786432 * s)
    for s in range(2):
        now[0] = s
        rows = slice(64 * s, 64 * s + 64)
        for h in range(2):
            dma("sp", A("l32", 48 + 4 * s, 49 + 4 * s, h=h), T.th[rows, :], 786432 * 2)
            dma("sp", A("y", h=h), T.y[rows, W_ * h:W_ * h + W_], 786432 * 2)
        ms(A("X", 0, TR), 0.0)
        ms(A("X", TR + V, 2 * TR + NX), 0.0)
    for q in ("sp", "act"):
        mine = [i for i, o in enumerate(ops) if o["eng"] == q]
        for i, j in zip(mine, mine[1:]):
            ops[j]["deps"][i] = "o"
        loads[q] = mine[-1]
    now[0] = None
    ms(A("ones"), 1.0)
    cp(A("onk"), A("ones"))
    ms(A("m192"), -192.0)
    ms(A("zero"), 0.0)

    def spots(out, x, pat, base=0, cm=1, **kw):
        asel(out, A("zero", 0, out["n"], **kw), pat, ALU.not_equal, x, base, cm)
    for name, x in (("idb", 1.0), ("nidb", -1.0), ("idk", 1.0), ("id4k", 4096.0), ("id16k", BIG), ("idm", 49.0 / 128), ("idh", 0.5)):
        spots(A(name), x, [[-1, 128]])
    spots(A("tk", 128, 256), 32768.0, [[-1, 128]])
    spots(A("nidk"), -1.0, [[0, 2], [-1, 128]])
    asel(A("bo0"), A("ones"), [[-16, 8], [0, 16]], ALU.is_ge, 0.0, 0, 1)
    asel(A("bob"), A("bo0"), [[16, 8], [0, 16]], ALU.is_ge, 0.0, 15, -1)
    for name, x in (("db", 1.0), ("db4k", 4096.0), ("ndb4k", -4096.0)):
        spots(A(name), x, [[-64, 2], [0, 2], [-1, 64]])
    spots(A("dsum"), 0.5, [[0, 2], [-1, 64]])
    asel(A("dsum"), A("dsum"), [[0, 2], [-1, 64]], ALU.not_equal, 0.5, -64, 1)
    for h in (1, 0):
        iota(A("nid", p=64 + 64 * h), [[512, 2], [1, 128]], V + L + w * h, 0)
    iota(A("pi", 0, 1), [[0, 1]], 0, 1)
    ts(A("pi", 1, 2), A("pi", 0, 1), 15, ALU.bitwise_and)
    ts(A("pi", 2, 3), A("pi", 0, 1), 64, ALU.bitwise_and)
    cp(A("pc", 0, 2), A("pi", 1, 3))
    ts(A("pc", 2, 3), A("pc", 0, 1), -1.0, ALU.mult, 15.0, ALU.add)
    ts(A("pc", 3, 4), A("pc", 0, 1), float(TR + NX), ALU.add)
    ts(A("pc", 4, 5), A("pc", 1, 2), 2.0, ALU.mult, A("pc", 0, 1), ALU.add)
    if BL == 64:
        ts(A("pc", 5, 6), A("pc", 0, 1), float(TR + NX + 16), ALU.add)
        ts(A("pc", 6, 7), A("pc", 0, 1), 16.0, ALU.add)
    R_, R15, HI, HR = [A("pc", j, j + 1) for j in (0, 2, 3, 4)]
    ts(A("tk", 0, 128), A("idb"), R15, ALU.mult)
    act(A("bok"), A("bob"), ACT.Copy)
    for j, x in enumerate((1.0, -16.0, 32.0, -32.0, -1.0)):
        act(A("b8", 8 * j, 8 * j + 8), A("bob", 0, 128, 16), ACT.Copy, scale=x)
    asel(A("seg"), A("ones"), [[0, 8], [1, 16]], ALU.not_equal, 0.0, 0, 0)
    nb = w // BL
    spots(A("r16", p=32), 1.0, [[0, 8], [1, 16]], 0, -1, p=32)
    for q, a, c in SECT:
        spots(A("rst", a, a + nb * c), 1.0, [[0, nb], [1, c]], cm=0)
        asel(A("tri", a, a + nb * c, p=32), A("zero", 0, nb * c, p=32), [[0, nb], [-1, c]], ALU.is_gt, 4096.0, 16 * q, 1)
        spots(A("ee", a, a + nb * c, p=32), -1.0, [[BL // 16, nb], [0, c]], WC + q, -1, p=32)
    if STEP:
        spots(A("nid4k"), -4096.0, [[-1, 128]])
        spots(A("e0", p=32), 1.0 / 32, [[0, 8], [1, 16]], cm=0, p=32)
        iota(A("c4k"), [[0, 128]], 4096, 0)
    if CUM:
        spots(A("id16"), 16.0, [[-1, 128]])
    asel(A("i8", p=64), A("zero", 0, 16, p=64), [[0, 16]], ALU.is_ge, 8.5 * 4096, 31, -1)
    asel(A("i8", p=64), A("i8", p=64), [[0, 2], [-1, 8]], ALU.not_equal, -4096.0, 0, 1)
    iota(A("t4"), [[0, L // BL], [8192, 2], [0, BL // 32]], TR - 4096, 0)
    act(A("i9"), A("t4"), ACT.Copy, scale=1.0 / 32)
    iota(A("ci"), [[16, 8]], 15, 0)
    cp(A("cu"), A("ci"))
    iota(A("nl", 32, 64), [[512, 2], [0, 2], [16, WC]], V, 0)
    ts(A("nl", 0, 32), A("nl", 32, 64), HR, ALU.add)
    for s in range(2):
        now[0] = s
        o = 24 * s
        cp(A("la"), A("l32", o, o + 24))
        cp(A("lb", WC * s, WC * s + WC), A("l32", o, o + WC))
        act(A("ab", 16 * s, 16 * s + WC), A("l32", o + WC, o + 16), ACT.Copy)
        act(A("ab", 16 * s + WC, 16 * s + 16), A("l32", o, o + WC), ACT.Copy)
        spots(A("lt", p=64), 1.0, [[0, 8], [1, 16]], 32, -1, p=64)
        if STEP:
            ms(A("st", 0, 2), 1.0)
        ms(A("prod", 0, w), 0.0)
        cp(A("thr", 0, 1), A("l32", 48 + 4 * s, 49 + 4 * s))
        ts(A("thd"), A("nidk"), A("thr", 0, 1), ALU.mult)
    now[0] = None
    send(A("lb"))

    for s in range(2):
        now[0] = s
        ring = [0]
        rows = slice(64 * s, 64 * s + 64)
        for t in range(TV):
            xw = A("X", TR, TR + V + 512 * t)
            sw = A("X")
            yv = "y" if t == 0 else "ry"
            old = A("ab", 16 * s, 16 * s + 16) if t == 0 else A("sm", 40, 48)
            for lev in range(LV):
                fin = lev == LV - 1
                m = t * LV + lev
                n = V + m * L
                cw = A("C", 0, V + (0 if t == 0 else 256 * (lev + 1)))

                f0 = 3 * w * (m % 2)

                def kk(name, x, a=0, b=w):
                    o = SL[x] * w + {"kf": f0, "prod": w}.get(name, 0)
                    return A(name, o + a, o + b)
                if m == 2:
                    parts = [(A("sa", WC, 2 * WC), 0, 1), (A("rc", WC * s, WC * s + WC), 2, 3), (A("ra"), 1, 2)]
                else:
                    parts = [(A("la" if m == 0 else "lst"), 0, 3)]
                for lists, a, b in parts:
                    if KS[s][m]:
                        act(A("kf", f0 + a * w, f0 + b * w), IND(cw, lists), ACT.Copy)
                        cp(A("k16", a * w, b * w), A("kf", f0 + a * w, f0 + b * w))
                    else:
                        cp(A("k16", a * w, b * w), IND(cw, lists))
                        cp(A("kf", f0 + a * w, f0 + b * w), A("k16", a * w, b * w))
                for lists, a, b in parts:
                    act(A("pqr", a * w, b * w), IND(xw, lists), ACT.Copy)
                mm((A("pk", 0, w), [(A("idb"), kk("pqr", "a")), (A("idb"), kk("pqr", "b")), (A("nidb"), kk("pqr", "c"))]))
                ts(A("nv", m * w, m * w + w), A("pk", 0, w), 0.0, ALU.max, 63.0, ALU.min)
                for h in range(2):
                    own = A("nv", m * w, m * w + w, h=h)
                    if t < TV - 1:
                        for h2 in range(2):
                            dma("sp", A("X", TR + n + w * h, TR + n + w * h + w, h=h2), own, 16384)
                    else:
                        dma("sp", T.xo[rows, n + w * h:n + w * h + w], own, 16384)
                dk, cn = A("pd", 2 * w, 3 * w), A("pd", 3 * w, 4 * w)
                mm((dk, [(kk("kf", "a"), A("idk")), (kk("kf", "b"), A("nidk", 0, w))]))
                mm((A("pd", 0, 2 * w), [(A("onk"), A("thd"))]), stop=False)
                mm((A("pk", 0, 2 * w), [(A("ones"), A("tk"))]), stop=False)
                steps = STEPS[EMODE[s][m]]
                i0 = len(ops)

                def diff(out, a, b, terms):
                    for u in range(a, b, 512):
                        v = min(b, u + 512)
                        rb = A("pr%d" % (ring[0] % 2), 0, v - u)
                        ring[0] += 1
                        mm((rb, [(A(x), A(y, u, v)) for x, y in terms]))
                        act(A(out, u, v), rb, ACT.Abs)
                work = WORK[EMODE[s][m]]

                def pair(x, j, forms=None):
                    s0, cw_ = steps[j][:2]
                    o = [q for q, st in enumerate(steps) if st[0] == s0 ^ 32 and st[1] == cw_ == 32]
                    if PAIR and o and (forms is None or (steps[j][2] in forms and steps[o[0]][2] in forms)):
                        return (1024 * (s0 // 64), 1024 * (s0 // 64 + 1)) if work.index((x, j)) > work.index((x, o[0])) else None
                    return 16 * s0, 16 * (s0 + cw_)
                for x, j in work:
                    s0, cwid, form = steps[j]
                    a, b = 16 * s0, 16 * (s0 + cwid)
                    neg = form in ("df", "d1")
                    xb, xc, dab, dcb, rab, acb, aac = [A(q, a, b) for q in ("xb", "xc", "dab", "dcb", "rab", "acb", "aac")]
                    lst = IND(xw, kk("k16", x, s0, s0 + cwid))
                    cuts = [0] + (FIRST if (x, j) in work[:2] else END if (x, j) == work[-1] else []) + [cwid]

                    def gsub(out):
                        for c0, c1 in zip(cuts, cuts[1:]):
                            u = (a + 16 * c0, a + 16 * c1)
                            tt(A(out, *u), IND(xw, kk("k16", x, s0 + c0, s0 + c1)), A("xb", *u), ALU.add if neg else ALU.subtract)
                    if x == "b":
                        for c0, c1 in zip(cuts, cuts[1:]):
                            act(A("xb", a + 16 * c0, a + 16 * c1), IND(xw, kk("k16", x, s0 + c0, s0 + c1)), ACT.Copy, scale=-1.0 if neg else 1.0)
                    elif x == "c" and form == "e":
                        act(xc, lst, ACT.Copy)
                        diff("acb", a, b, [("idb", "xc"), ("nidb", "xb")])
                    elif x == "c":
                        if neg:
                            for c0, c1 in zip(cuts, cuts[1:]):
                                act(A("dcb", a + 16 * c0, a + 16 * c1), IND(xw, kk("k16", x, s0 + c0, s0 + c1)), ACT.Copy)
                            add(dcb, xb, "ad%d_%d" % (s, j))
                        else:
                            gsub("dcb")
                        if form == "n":
                            act(acb, dcb, ACT.Abs)
                        elif pair(x, j, ("r", "rf")):
                            ts(A("acb", *pair(x, j, ("r", "rf"))), A("dcb", *pair(x, j, ("r", "rf"))), 0.0, ALU.max, 2.0, ALU.mult)
                    else:
                        gsub("dab")
                        if pair(x, j):
                            ts(A("rab", *pair(x, j)), A("dab", *pair(x, j)), -2.0 ** -11, ALU.max)
                    if x != "b" and work.index((x, j)) == max(work.index(("a", j)), work.index(("c", j))):
                        for c0, c1 in zip(cuts, cuts[1:]) if (x, j) == work[-1] else [(0, cwid)]:
                            if form in ("df", "rf"):
                                fold(aac, dab, dcb, "fo%d_%d" % (s, j))
                            elif form == "e":
                                diff("aac", a + 16 * c0, a + 16 * c1, [("idb", "xb"), ("nidb", "xc"), ("idb", "dab")])
                            else:
                                diff("aac", a + 16 * c0, a + 16 * c1, [("nidb", "dcb"), ("idb", "dab")])
                for e in CHAIN:
                    mine = [i for i in range(i0, len(ops)) if ops[i]["eng"] == e]
                    for i, j in zip(mine, mine[1:]):
                        ops[j]["deps"].setdefault(i, "o")

                def red(name, bank_, c0, c1, j0, j1, stop=False, l0=0, l1=w):
                    if name in LAST.split() and (l0, l1) == (0, w):
                        red(name, bank_, c0, c1, j0, j1, False, 0, 96)
                        l0 = 96
                    for k0 in range(0, 16, RED):
                        mm(*[(A(bank_, c0 + k, c1, 16, p=(l0, l1)), [(A(name, 16 * l0 + k, 16 * l1, 16), A("b8", j0, j1))]) for k in range(k0, k0 + RED)],
                           start=False, stop=stop and k0 + RED == 16, one=True)
                nf = sum(c for _, c, form in steps if form in ("df", "rf"))
                nr = nf + sum(c for _, c, form in steps if form in ("r", "d1"))
                if nf:
                    red("dab", "pd", 0, w, 32, 40, l1=nf)
                    red("dcb", "pd", 0, 2 * w, 32, 48, l1=nf)
                if nr > nf:
                    red("dcb", "pd", w, 2 * w, 32, 40, l0=nf, l1=nr)
                red("acb", "pd", w, 2 * w, 0, 8)
                red("dab", "pk", 0, w, 8, 16)
                red("rab", "pk", 0, 2 * w, 16, 32)
                if nf < w:
                    red("aac", "pd", 0, w, 0, 8, True, l0=nf)
                if nf:
                    red("aac", "pd", 0, w, 48, 56, True, l1=nf)
                ka, kc = A("pk", 0, w), A("pk", w, 2 * w)
                act(A("tp"), A("pd", 0, w), ACT.Relu, bias=HH / 2, scale=-HH)
                tt(A("col"), A("tp"), A("pd", w, 2 * w), ALU.is_lt)
                mm((ka, [(A("id16k"), A("col"))]), (kc, [(A("idm"), A("col")), (A("nidb"), A("tp"))]), start=False, one=True)
                ns = 1 if fin else 3
                if STEP:
                    scan(A("scn"), A("seg"), ka, ALU.mult, ALU.max)
                    tt(A("st", 2, w + 2), IND(A("scn"), A("cu")), A("scn"), ALU.is_equal)

                    def hot(pos, neg, one):
                        return [(A("st", 2, w + 2), A(pos)), (A("st", 1, w + 1), A(neg)), (A("e0", p=32), A(one, p=32))]
                    mm((A("pr0", 0, w), hot("idb", "nidb", "ones")))
                    for j in range(ns):
                        tt(A("prod", w + j * w, 2 * w + j * w), A("kf", f0 + j * w, f0 + j * w + w), A("pr0", 0, w), ALU.mult)
                else:
                    act(A("keys"), ka, ACT.Copy)
                    scan(A("scn"), A("seg"), A("keys"), ALU.mult, ALU.max)
                    tt(A("oht"), IND(A("scn"), A("cu")), A("keys"), ALU.is_equal)
                    mm(*[(A("pr0", j * w, j * w + w), [(A("oht"), A("idb"))]) for j in range(ns)])
                    tt(A("prod", w, w + ns * w), A("kf", f0, f0 + ns * w), A("pr0", 0, ns * w), ALU.mult)
                if fin:
                    mm((cn, [(A("col"), A("idb")), (A("off0"), A("id16")) if CUM else (A("idb"), A("off0"))]))
                    act(kk("prod", "x"), cn, ACT.Copy)
                elif CUM:
                    scan(A("cum"), A("seg"), A("col"), ALU.mult, ALU.add)
                    ts(A("off0"), A("cum"), -8.0, ALU.add, 0.0, ALU.max)

                nr = WC * (ns + 1)
                mm(*[(A("pr1", r, w, 16, p=nr), [(A("prod", r, w + ns * w, 16), A("bok", 0, w, 16))]) for r in range(16)])
                act(A("lt", p=nr), A("pr1", 0, w, p=nr), ACT.Copy)
                mm((A("pk", 2 * w, 2 * w + nr), [(A("lt", p=32), A("idk", 0, nr, p=32))]),
                   *([(A("pk", 2 * w + 32, 2 * w + 32 + old["n"]), [(A("lt", p=64), A("i8", 0, old["n"], p=64))])] if fin else []))
                cp(A("lst", 0, ns * WC), A("pk", 2 * w + WC, 2 * w + nr))
                dd = A("pr0", 0, ND)
                mm((dd, [(A("r16", p=32), A("tri", p=32))]),
                   *[(A("pr0", a + c * j, a + c * j + c), [(A("bok"), kk("prod", "b", BL * j, BL * j + c))]) for q, a, c in SECT[1:] for j in range(w // BL)],
                   (A("pr0", 0, w), [(A("bok"), kk("prod", "b"))]), stop=False, one=True)
                mm((dd, [(A("lt", p=32), A("ee", p=32))]), start=False)
                act(A("ad"), dd, ACT.Abs)
                scan(A("nd"), A("rst"), A("ad"), ALU.max, ALU.min)
                act(A("xz"), IND(xw, A("lst", 0, WC)), ACT.Copy)
                mm(*[(A("pr1", h * w, h * w + w), [(A("db", 128 * h, 128 * h + 128), A(x)) for x in ("xz", yv)]) for h in range(2)])
                act(A("hh"), A("pr1", 0, L), ACT.Identity, bias=191.75, scale=0.5)
                if fin:
                    k = old["n"]
                    tt(A("sm", 0, k), A("nl", 16 * t, 16 * t + k), A("pk", 2 * w + 32, 2 * w + 32 + k), ALU.min)
                    tt(A("sm", 32 + 24 * t, 32 + 24 * t + k), A("sm", 0, k), old, ALU.max)
                    if t < TV - 1:
                        cp(A("sa"), A("sm", 32, 48))
                        send(A("sa", 0, WC))
                o, nq = 3 * w, BL // 16
                mm((A("pk", o, o + 16), [(A("onk", p=32), A("i9", p=32))]),
                   *[(A("pk", o + 8 * h, o + 8 * h + 8, h=h2), [(A("lt", 64 * h, 64 * h + 64, p=32), A("idk", WC, 2 * WC, p=32))]) for h in range(2) for h2 in range(2)],
                   stop=False, one=True)
                mm(*[(A("pk", o + 8 * h + q, o + 8 * h + 8, nq), [(A(("db4k", "ndb4k")[2 * q // nq], 128 * h, 128 * h + 128), A("nd", a + c - 1, a + c * w // BL, c))])
                     for h in range(2) for q, a, c in SECT], start=False, one=True)
                for q in range(nq // 2):
                    ts(A("idx", q, 16, nq // 2), A("pk", o + q, o + 16, nq // 2), A("pc", 3 + 2 * q, 4 + 2 * q), ALU.min, A("pc", 6 * q, 6 * q + 1), ALU.max)
                for c in range(L // BL - 1, -1, -1):
                    tt(IND(sw, A("idx", nq * c, nq * c + nq)), A("hh", BL * c, BL * c + BL), A("m192"), ALU.add)
                if not fin and not CUM:
                    mm((cn, [(A("col"), A("idb"))]))
                    act(kk("prod", "x"), cn, ACT.Copy)
                if fin or not CUM:
                    mm((cn, [(A("bok"), kk("prod", "x"))]))
                if not fin and not CUM:
                    act(A("off0"), cn, ACT.Relu, bias=-8.0)
                if fin:
                    yn = A("yn", t * w, t * w + w)
                    act(cn, cn, ACT.Sign, A("thr", 2, 3) if t < TV - 1 else None, bias=-8.5)
                    tt(A("ty"), A(yv), cn, ALU.mult)
                    mm((cn, [(A("idh"), A("ty")), (A("idh"), A(yv)), (A("nidb"), A("nv", 2 * t * w, 2 * t * w + w))]))
                    act(yn, cn, ACT.Abs)
                    if t < TV - 1:
                        send(yn)
                act(A("rnd"), kc, ACT.Relu)
                tt(A("sel"), A("rnd"), kc, ALU.is_le)
                tt(A("wv"), A("sel"), dk, ALU.mult)
                if fin and t < TV - 1:
                    mm((A("pd", 2 * w, 2 * w + 1), [(A("dsum"), A("thr", 2, 3))]))
                    ts(A("thr", 1, 2), A("pd", 2 * w, 2 * w + 1), 128.0, ALU.add, A("thr", 0, 1), ALU.add)
                    ts(A("thd"), A("nidk"), A("thr", 1, 2), ALU.mult)
                co, m0 = A("CO", m * w, m * w + w), A("pk", 0, w)
                mm((m0, [(A("wv"), A("idk")), (A("idk"), kk("kf", "b"))] + ([] if fin else hot("id4k", "nid4k", "c4k") if STEP else [(A("oht"), A("id4k"))])))
                if fin:
                    act(co, m0, ACT.Copy)
                else:
                    tt(co, A("nid", t * w, t * w + w), m0, ALU.min)
                if t < TV - 1:
                    act(A("CI", m * w, m * w + w), co, ACT.Copy)
                for h in range(2):
                    dma("sp", T.co[rows, m * L + w * h:m * L + w * h + w], A("CO", m * w, m * w + w, h=h), 32768)
                    if t < TV - 1:
                        for h2 in range(2):
                            dma("sp", A("C", n + w * h, n + w * h + w, h=h2), A("CI", m * w, m * w + w, h=h), 32768)
        for h in range(2):
            q = ("sp", "act")[h]
            dma(q, T.xo[rows, 768 * h:768 * h + 768], A("X", TR + 768 * h, TR + 768 * h + 768, h=h), 196608)
            dma("sp", T.so[rows, WC * h:WC * h + WC], A("sm", 56, 64, h=h), 2048)
            dma("sp", T.yo[rows, w * h:w * h + w], A("yn", w, 2 * w, h=h), 16384)
    for o in ops[loads["act"] + 1:]:
        if o["eng"] == "act":
            o["deps"].setdefault(loads["act"], "o")
    return ops, ne_ * len(sends) + uses.get("sent", 0)


def sweep(ops, before, after, prio, look, back):
    n = len(ops)
    left = [len(b) for b in before]
    ready = [ops[i]["lat"] if back else 0.0 for i in range(n)]
    pool = {o["eng"]: [] for o in ops}
    for i, o in enumerate(ops):
        if not left[i]:
            pool[o["eng"]].append(i)
    free = {e: 0.0 for e in pool}
    order, end, start = [], [0.0] * n, [0.0] * n
    for _ in range(n):
        best = None
        for e, lst in pool.items():
            if lst:
                t0 = max(free[e], min([ready[i] for i in lst]))
                if best is None or t0 < best[0]:
                    best = (t0, e)
        t0, e = best
        i = -max([(prio[i], -i) for i in pool[e] if ready[i] <= t0 + look])[1]
        pool[e].remove(i)
        start[i] = max(free[e], ready[i])
        free[e] = start[i] + ops[i]["busy"]
        end[i] = free[e] + (0.0 if back else ops[i]["lat"])
        order.append(i)
        for u, d in after[i]:
            if ready[u] < free[e] + d:
                ready[u] = free[e] + d
            left[u] -= 1
            if not left[u]:
                pool[ops[u]["eng"]].append(u)
    return order, start, end


def plan(ops):
    n = len(ops)
    fw, bw = [[] for _ in ops], [[] for _ in ops]
    for i, o in enumerate(ops):
        for j, k in o["deps"].items():
            d = 0.0 if k == "o" else ops[j]["lat"] + (0.0 if k == "t" else SAME if o["eng"] == ops[j]["eng"] else HOP)
            fw[j].append((i, d))
            bw[i].append((j, d))
    base = [0.0] * n
    for i in range(n - 1, -1, -1):
        base[i] = ops[i]["busy"] + max([base[u] + d for u, d in fw[i]] + [ops[i]["lat"]])
    rng = np.random.default_rng(SEED)
    late = np.array([1.0 if o["s"] == 1 else 0.0 for o in ops])
    cases = [case(ops, *c) for c in CASES]
    kept = []
    for k in range(TRIES):
        look = float(rng.choice(LOOK))
        if k < 4 * KEEP:
            r = sweep(ops, bw, fw, (np.array(base) * rng.uniform(1.0, 1.4) - late * LEAD * rng.uniform(0.4, 1.6)).tolist(), look, False)
            for _ in range(3):
                r = sweep(ops, bw, fw, sweep(ops, fw, bw, r[2], look, True)[2], look, False)
        else:
            e = np.array(kept[int(rng.integers(len(kept)))][1][2])
            lo = rng.uniform(0, e.max())
            z = rng.uniform(0, float(rng.choice([100.0, 400.0, 1200.0])), n)
            if rng.random() < 0.3:
                z = z + late * rng.uniform(-1500, 1500)
            z = z * ((e > lo) & (e < lo + rng.uniform(3000, 30000)))
            r = sweep(ops, bw, fw, sweep(ops, fw, bw, (e + z).tolist(), look, True)[2], look, False)
        if len(kept) < KEEP or max(r[2]) <= max(kept[0][1][2]) + 2000:
            kept.append((max(r[2]) + sum(replay(r[0], *c) for c in cases), r))
            kept.sort(key=lambda x: x[0])
            del kept[KEEP:]
    return kept[0][1]


def case(ops, hop, same, gather, scatter, fixed, lat):
    busy = [o["busy"] + o["ge"] * (gather - G_) + o["se"] * (scatter - SC_) + o["mm"] * (fixed - P0) for o in ops]
    pre = [[(j, 0.0 if k == "o" else ops[j]["lat"] * lat + (0.0 if k == "t" else same if o["eng"] == ops[j]["eng"] else hop)) for j, k in o["deps"].items()] for o in ops]
    return [o["eng"] for o in ops], busy, pre, [o["lat"] * lat for o in ops]


def replay(order, eng, busy, pre, tail):
    free, end, fin = dict.fromkeys(eng, 0.0), [0.0] * len(eng), 0.0
    for i in order:
        t = free[eng[i]]
        for j, d in pre[i]:
            if end[j] + d > t:
                t = end[j] + d
        free[eng[i]] = end[i] = t = t + busy[i]
        if t + tail[i] > fin:
            fin = t + tail[i]
    return fin


def emit(g, T, ops, order, nsent):
    Q = {"dve": g.vector, "act": g.scalar, "pe": g.tensor, "pool": g, "sp": g.sync}
    need = set(j for o in ops for j, k in o["deps"].items() if k == "w")
    count = {e: 0 for e in Q}
    known = {e: {} for e in Q}
    mark, clock = {}, {}
    for i in order:
        o = ops[i]
        e = o["eng"]
        if e == "net":
            mark[i], clock[i] = o["sem"], {o["sem"][0]: o["sem"][1]}
            continue
        kn = known[e]
        want = sorted((j for j, k in o["deps"].items() if k == "w"), key=lambda j: -mark[j][1])
        for j in want:
            s, v = mark[j]
            if kn.get(s, 0) < v:
                Q[e].wait_ge(T.sem[s], v)
                for s2, v2 in clock[j].items():
                    if kn.get(s2, 0) < v2:
                        kn[s2] = v2
        ins = o["fn"]()
        if o["sem"] is None:
            if i in need:
                count[e] += 1
                ins.then_inc(T.sem[e], 1)
                mark[i] = (e, count[e])
        elif o["sem"][1] is not None:
            ins.then_inc(T.sem[o["sem"][0]], 16)
            mark[i] = o["sem"]
        if i in mark:
            clock[i] = dict(kn)
            clock[i][mark[i][0]] = mark[i][1]
    for e in ("dve", "act", "pe", "pool"):
        if count[e]:
            g.wait_ge(T.sem[e], count[e])
    g.wait_ge(T.sem.sent, nsent)
    for s, v in {o["sem"][0]: o["sem"][1] for o in ops if o["sem"] is not None and o["sem"][1] is not None}.items():
        g.wait_ge(T.sem[s], v)


ORDER = []


def rank_program(g, core, T, topo):
    rank = T.rank_of(core)
    if rank is None:
        for r in range(len(T.cores)):
            path = way(T, topo, r)
            if len(path) == 3 and path[1] == core:
                rid, pid = topo.addr(path[2], core)
                nin = emask(topo, path[0], core)[1]
                mk, nout = emask(topo, core, path[2])
                for land, sem in MSG:
                    g.wait_ge(T.sem[sem], nin)
                    g.remote_dma(T[land][:], T[land][:], T.sem[sem], T.sem.sent, pid, rid, mk)
                g.wait_ge(T.sem.sent, nout * len(MSG))
            if core in mates_of(T, topo, r):
                ops = build(g, T, topo, r)[0]
                if not ORDER:
                    ORDER.append(plan(ops))
                rid, pid = topo.addr(path[0], core)
                mk, nout = emask(topo, core, path[0], 16)
                got = {"sent": 0}
                for i in ORDER[0][0]:
                    if "fold" in ops[i] and ops[i]["s"] == mates_of(T, topo, r).index(core):
                        ap, sem, nin = ops[i]["fold"][:3]
                        got[sem] = got.get(sem, 0) + nin
                        got["sent"] += nout
                        g.wait_ge(T.sem[sem], got[sem])
                        g.remote_dma(ap, ap, T.sem[sem], T.sem.sent, pid, rid, mk)
                if got["sent"]:
                    g.wait_ge(T.sem.sent, got["sent"])
        return
    ops, nsent = build(g, T, topo, rank)
    if not ORDER:
        ORDER.append(plan(ops))
    emit(g, T, ops, ORDER[0][0], nsent)
